import numpy as np
import ml_dtypes


def mxq(x, axis, fmt="e4m3"):
    dtype, down = {"e4m3": (ml_dtypes.float8_e4m3fn, 7), "e5m2": (ml_dtypes.float8_e5m2, 14)}[fmt]
    v = np.moveaxis(np.asarray(x, np.float32).astype(ml_dtypes.bfloat16).astype(np.float64), axis, -1)
    blocks = v.reshape(v.shape[:-1] + (-1, 32))
    amax = np.abs(blocks).max(-1, keepdims=True)
    byte = np.maximum(np.where(amax > 0, np.frexp(amax)[1] - 1 + 127, 0) - down, 1)
    scale = np.exp2(byte - 127.0)
    codes = (blocks / scale).astype(np.float32).astype(dtype).astype(np.float64)
    return np.moveaxis((codes * scale).reshape(v.shape), -1, axis)


WIDE = False


def mx_kscale(k):
    if not WIDE:
        return np.ones(k)
    levels = np.array([10, -10, 5, -5, 0])
    if k % 512:
        return np.exp2(np.random.permutation(np.resize(levels, k // 32))).repeat(32)
    a = np.empty((k // 512, 16))
    for p in range(k // 512):
        a[p, :8] = np.random.permutation(np.resize(levels, 8))
        for g in range(8):
            far = levels[np.abs(levels - a[p, g]) >= 10]
            a[p, g + 8] = far[np.random.randint(len(far))]
    return np.exp2(a.ravel()).repeat(32)


def f64(x):
    return np.asarray(x).astype(np.float64)


def striped(idx):
    return np.tile(idx.reshape(-1, 16).T, (8, 1)).astype(np.uint16)


def unstriped(offs):
    return offs[:16].T.reshape(-1).astype(np.int64)


E2M1 = np.array([0.0, 0.5, 1.0, 1.5, 2.0, 3.0, 4.0, 6.0, -0.0, -0.5, -1.0, -1.5, -2.0, -3.0, -4.0, -6.0])


def pack_weight(w, fmt):
    k, n = w.shape
    w = f64(np.asarray(w, np.float32).astype(ml_dtypes.bfloat16)).reshape(k // 32, 32, n)
    amax = np.abs(w).max(1)
    if fmt == "e4m3":
        byte = np.frexp(amax)[1] - 1 + 127 - 7
    else:
        mant, ex = np.frexp(amax / 6.0)
        byte = np.where(mant > 0.5, ex, ex - 1) + 127
    byte = np.clip(np.where(amax > 0, byte, 1), 1, 254)
    scaled = (w * np.exp2(127.0 - byte)[:, None, :]).reshape(k, n).astype(np.float32)
    by_word = np.ascontiguousarray(scaled.reshape(k // 512, 128, 4, n).transpose(0, 1, 3, 2))
    if fmt == "e4m3":
        words = by_word.astype(ml_dtypes.float8_e4m3fn).view(np.uint8)
    else:
        c = by_word.astype(ml_dtypes.float4_e2m1fn).view(np.uint8) & 0xF
        words = (c[..., 0::2] | (c[..., 1::2] << 4)).reshape(k // 512, 128, 2 * n)
    return np.ascontiguousarray(words), np.ascontiguousarray(byte.astype(np.uint8).reshape(k // 512, 16, n))


def unpack_weight(words, scales, fmt):
    g, _, n = scales.shape
    words = np.ascontiguousarray(words).reshape(g, 128, n, -1)
    if fmt == "e4m3":
        vals = words.view(ml_dtypes.float8_e4m3fn).astype(np.float64)
    else:
        nib = np.empty((g, 128, n, 4), np.uint8)
        nib[..., 0::2] = words & 0xF
        nib[..., 1::2] = words >> 4
        vals = E2M1[nib]
    vals = vals * np.repeat(np.exp2(scales.astype(np.float64) - 127.0), 8, axis=1)[..., None]
    return vals.transpose(0, 1, 3, 2).reshape(g * 512, n)


def gelu(v):
    return 0.5 * v * (1.0 + np.tanh(np.sqrt(2.0 / np.pi) * (v + 0.044715 * v**3)))


K, T, E, C, H, N = 1024, 1024, 2, 256, 512, 512


def by_expert(wq, xq):
    return np.concatenate([wq[e].T @ xq[:, e * C:(e + 1) * C] for e in range(E)], axis=1)


def setup_inputs():
    n = np.random.standard_normal
    s = mx_kscale(K)
    u = mx_kscale(H)
    slot_token = np.concatenate([np.random.permutation(T)[:C] for e in range(E)])
    x = pack_weight(n((K, T)) * s[:, None], "e4m3")
    w = [pack_weight(m, "e2m1") for m in n((E, K, N)) / np.sqrt(K) / s[None, :, None]]
    wb = [pack_weight(m, "e4m3") for m in n((E, H, N)) / np.sqrt(H) / u[None, :, None]]
    return {
        "x_words": x[0],
        "x_scales": x[1],
        "w_words": np.stack([m[0] for m in w]),
        "w_scales": np.stack([m[1] for m in w]),
        "wa": (n((E, K, H)) / np.sqrt(K) / s[None, :, None] * u).astype(np.float32),
        "wb_words": np.stack([m[0] for m in wb]),
        "wb_scales": np.stack([m[1] for m in wb]),
        "offs": striped(slot_token),
    }


def reference(x_words, x_scales, w_words, w_scales, wa, wb_words, wb_scales, offs):
    w = np.stack([unpack_weight(w_words[e], w_scales[e], "e2m1") for e in range(E)])
    waq = mxq(f64(wa), 1, "e4m3")
    wb = np.stack([unpack_weight(wb_words[e], wb_scales[e], "e4m3") for e in range(E)])
    idx = unstriped(offs)
    xq = unpack_weight(x_words, x_scales, "e4m3")[:, idx]
    h = gelu(by_expert(waq, xq))
    y = by_expert(w, xq) + by_expert(wb, mxq(h, 0, "e4m3"))
    out = y
    return out

@@ -1,0 +1,277 @@
+from contextlib import ExitStack
+
+import concourse.mybir as mybir
+
+K, T, E, C, H, N = 1024, 1024, 2, 256, 512, 512
+FLOPS = 2 * E * C * (K * N + K * H + H * N)
+
+F32 = mybir.dt.float32
+BF16 = mybir.dt.bfloat16
+I32 = mybir.dt.int32
+U32 = mybir.dt.uint32
+U16 = mybir.dt.uint16
+U8 = mybir.dt.uint8
+FP8X4 = mybir.dt.float8_e4m3fn_x4
+FP4X4 = mybir.dt.float4_e2m1fn_x4
+GELU = mybir.ActivationFunctionType.Gelu_apprx_tanh
+
+P = 128
+PACK = 4
+PASSES = K // (P * PACK)
+HALF = 128
+HALVES = C // HALF
+TILES = 4
+CHUNKS = 2
+M_CHUNK = P // CHUNKS
+
+
+def tile_moe_elr_s_gelu_kernel(tc, x_words, x_scales, w_words, w_scales, wa, wb_words, wb_scales, offs, out):
+    nc = tc.nc
+    with ExitStack() as ctx:
+        keep = ctx.enter_context(tc.tile_pool(name="keep", bufs=1))
+        psum = ctx.enter_context(tc.psum_pool(name="psum", bufs=1))
+
+        def sb(name, shape, dtype):
+            return keep.tile(shape, dtype, name=name, align_bytes=64)
+
+        offsets = keep.tile([P, E * C // 16], U16, name="offsets")
+        nc.sync.dma_start(offsets[:], offs)
+
+        warm = sb("warm", [P, 8], F32)
+        warm_out = sb("warm_out", [P, 8], F32)
+        xs = sb("xs", [P, PASSES, T], U8)
+        ws = sb("ws", [P, E * PASSES, N], U8)
+        wbs = sb("wbs", [P, N], U8)
+        nc.vector.memset(warm[:], 0.0)
+        nc.scalar.activation(warm_out[:], warm[:], GELU)
+        nc.vector.memset(xs[:].bitcast(I32), 0)
+        nc.vector.memset(ws[:].bitcast(I32), 0)
+        nc.vector.memset(wbs[:].bitcast(I32), 0)
+
+        xw = [sb(f"xw{s}", [P, T], I32) for s in range(PASSES)]
+        width = PACK * M_CHUNK
+        raw, whole = {}, {}
+        for e in range(E):
+            for s in range(PASSES):
+                if e == s:
+                    for c in range(CHUNKS):
+                        raw[e, s, c] = sb(f"raw{e}{s}{c}", [P, PACK, width], F32)[:]
+                else:
+                    whole[e, s] = sb(f"raw{e}{s}", [P, PACK, H], F32)
+                    for c in range(CHUNKS):
+                        raw[e, s, c] = whole[e, s][:, :, c * width : (c + 1) * width]
+        ww = [sb(f"ww{e}", [P, PASSES, 2 * N], U8) for e in range(E)]
+        wbw = [sb(f"wbw{e}", [P, N], I32) for e in range(E)]
+
+        def load_x(s):
+            nc.sync.dma_start(xw[s][:], x_words[s].rearrange("p t d -> p (t d)").bitcast(I32))
+
+        def load_xs(r):
+            rows = x_scales.rearrange("s (q r) t -> r q s t", r=4)
+            nc.sync.dma_start(xs[r:P:32].bitcast(I32), rows[r].bitcast(I32))
+
+        def load_wa(e, s, c):
+            rows = wa[e, 512 * s : 512 * (s + 1), :].rearrange("(p j) i -> p j i", j=PACK)
+            if c is None:
+                nc.sync.dma_start(whole[e, s][:], rows)
+            else:
+                nc.sync.dma_start(raw[e, s, c], rows[:, :, c * width : (c + 1) * width])
+
+        def load_ws(r):
+            rows = w_scales.rearrange("e s (q r) n -> r q (e s) n", r=4)
+            nc.sync.dma_start(ws[r:P:32].bitcast(I32), rows[r].bitcast(I32))
+
+        def load_wbs(q):
+            nc.sync.dma_start(
+                wbs[32 * q + 4 : 32 * q + 4 + 4 * E].bitcast(I32), wb_scales[:, 0, 4 * q : 4 * q + 4, :].bitcast(I32)
+            )
+
+        def load_w(e):
+            nc.sync.dma_start(ww[e][:].bitcast(I32), w_words[e].rearrange("s p b -> p s b").bitcast(I32))
+
+        def load_wb(e):
+            nc.sync.dma_start(wbw[e][:], wb_words[e, 0].rearrange("p n d -> p (n d)").bitcast(I32))
+
+        load_x(0)
+        load_wa(0, 0, 0)
+        for r in range(4):
+            load_xs(r)
+        load_wa(0, 0, 1)
+        load_x(1)
+        load_wa(0, 1, None)
+        for r in range(4):
+            load_ws(r)
+        load_w(0)
+        load_wa(1, 0, None)
+        for r in range(4):
+            load_wbs(r)
+        load_wb(0)
+        load_wa(1, 1, 0)
+        load_w(1)
+        load_wa(1, 1, 1)
+        load_wb(1)
+
+        xg = [sb(f"xg{s}", [P, E * C], U32) for s in range(PASSES)]
+        xgs = [sb(f"xgs{s}", [P, E * C], U8) for s in range(PASSES)]
+        grouped, wa_codes, wa_scale = {}, {}, {}
+        for e in range(E):
+            for s in range(PASSES):
+                grouped[e, s] = sb(f"grouped{e}{s}", [P, TILES, P, PACK], BF16)
+                wa_codes[e, s] = sb(f"wa_codes{e}{s}", [P, TILES, P], U32)
+                wa_scale[e, s] = sb(f"wa_scale{e}{s}", [P, TILES, P], U8)
+        h_bank, y_bank, h_bf, h_codes, h_scale = {}, {}, {}, {}, {}
+        for e in range(E):
+            for u in range(HALVES):
+                h_bank[e, u] = psum.tile([P, TILES, HALF], F32, name=f"h_bank{e}{u}")
+                y_bank[e, u] = psum.tile([P, TILES, HALF], F32, name=f"y_bank{e}{u}")
+                h_bf[e, u] = sb(f"h_bf{e}{u}", [P, HALF, PACK], BF16)
+                h_codes[e, u] = sb(f"h_codes{e}{u}", [P, HALF], U32)
+                h_scale[e, u] = sb(f"h_scale{e}{u}", [P, HALF], U8)
+        y_sb = [sb(f"y_sb{e}", [P, TILES, C], F32) for e in range(E)]
+
+        def gather_words(e, s):
+            picks = offsets[:, e * C // 16 : (e + 1) * C // 16]
+            nc.vector.tensor_copy(xg[s][:, e * C : (e + 1) * C], xw[s][:].bitcast(U32).indirect(picks))
+
+        def gather_scales(e, s):
+            picks = offsets[:, e * C // 16 : (e + 1) * C // 16]
+            nc.vector.tensor_copy(xgs[s][:, e * C : (e + 1) * C], xs[:, s, :].indirect(picks))
+
+        def cast(engine, e, s, c, m0=0, m1=M_CHUNK):
+            src = raw[e, s, c].rearrange("p j (m t) -> p m j t", t=TILES)[:, m0:m1]
+            dst = grouped[e, s][:].rearrange("p t m j -> p m j t")[:, c * M_CHUNK + m0 : c * M_CHUNK + m1]
+            if engine == "scalar":
+                nc.scalar.copy(dst, src)
+            else:
+                nc.vector.tensor_copy(dst, src)
+
+        def quantize_pass(e, s):
+            nc.vector.quantize_mx(
+                out=wa_codes[e, s][:].rearrange("p t m -> p (t m)").bitcast(FP8X4),
+                scales=wa_scale[e, s][:].rearrange("p t m -> p (t m)"),
+                in_=grouped[e, s][:].rearrange("p t m j -> p (t m j)"),
+            )
+
+        def quantize_chunk(e, s, c, t):
+            ms = slice(c * M_CHUNK, (c + 1) * M_CHUNK)
+            nc.vector.quantize_mx(
+                out=wa_codes[e, s][:, t, ms].bitcast(FP8X4),
+                scales=wa_scale[e, s][:, t, ms],
+                in_=grouped[e, s][:, t, ms, :].rearrange("p m j -> p (m j)"),
+            )
+
+        def slots(e, u):
+            return slice(e * C + u * HALF, e * C + (u + 1) * HALF)
+
+        def h_pass(e, s, u):
+            for t in range(TILES):
+                nc.tensor.matmul_mx(
+                    out=h_bank[e, u][:, t, :],
+                    lhsT=wa_codes[e, s][:, t, :].bitcast(FP8X4),
+                    lhsT_scale=wa_scale[e, s][:, t, :],
+                    rhs=xg[s][:, slots(e, u)].bitcast(FP8X4),
+                    rhs_scale=xgs[s][:, slots(e, u)],
+                    start=(s == 0 and t == 0),
+                    stop=(s == PASSES - 1 and t == TILES - 1),
+                )
+
+        def w_passes(e, u):
+            for s in range(PASSES):
+                for q in range(TILES):
+                    nc.tensor.matmul_mx(
+                        out=y_bank[e, u][:, q, :],
+                        lhsT=ww[e][:, s, 2 * P * q : 2 * P * (q + 1)].bitcast(FP4X4),
+                        lhsT_scale=ws[:, e * PASSES + s, P * q : P * (q + 1)],
+                        rhs=xg[s][:, slots(e, u)].bitcast(FP8X4),
+                        rhs_scale=xgs[s][:, slots(e, u)],
+                        start=(s == 0 and q == 0),
+                        stop=False,
+                    )
+
+        def gelu(e, u):
+            nc.scalar.activation(h_bf[e, u][:], h_bank[e, u][:].rearrange("p t n -> p n t"), GELU)
+
+        def quantize_h(e, u):
+            nc.vector.quantize_mx(
+                out=h_codes[e, u][:].bitcast(FP8X4),
+                scales=h_scale[e, u][:],
+                in_=h_bf[e, u][:].rearrange("p n t -> p (n t)"),
+            )
+
+        def wb_pass(e, u):
+            for q in range(TILES):
+                nc.tensor.matmul_mx(
+                    out=y_bank[e, u][:, q, :],
+                    lhsT=wbw[e][:, P * q : P * (q + 1)].bitcast(FP8X4),
+                    lhsT_scale=wbs[4 * (e + 1) : P, P * q : P * (q + 1)],
+                    rhs=h_codes[e, u][:].bitcast(FP8X4),
+                    rhs_scale=h_scale[e, u][:],
+                    start=False,
+                    stop=(q == TILES - 1),
+                )
+
+        def evacuate(engine, e, u):
+            dst = y_sb[e][:, :, u * HALF : (u + 1) * HALF]
+            if engine == "scalar":
+                nc.scalar.copy(dst, y_bank[e, u][:])
+            else:
+                nc.vector.tensor_copy(dst, y_bank[e, u][:])
+
+        out_rows = out.rearrange("(q p) j -> p q j", p=P)
+
+        def store(e, u0, u1):
+            nc.sync.dma_start(
+                out_rows[:, :, e * C + u0 * HALF : e * C + u1 * HALF], y_sb[e][:, :, u0 * HALF : u1 * HALF]
+            )
+
+        gather_words(0, 0)
+        cast("scalar", 0, 0, 0)
+        gather_words(1, 0)
+        cast("scalar", 0, 0, 1)
+        gather_scales(0, 0)
+        gather_words(0, 1)
+        quantize_pass(0, 0)
+        gather_scales(0, 1)
+        for u in range(HALVES):
+            h_pass(0, 0, u)
+        cast("scalar", 0, 1, 0)
+        cast("scalar", 0, 1, 1)
+        gather_words(1, 1)
+        gather_scales(1, 0)
+        quantize_pass(0, 1)
+        gather_scales(1, 1)
+        for u in range(HALVES):
+            h_pass(0, 1, u)
+        for u in range(HALVES):
+            gelu(0, u)
+            w_passes(0, u)
+        cast("vector", 1, 0, 0)
+        for u in range(HALVES):
+            quantize_h(0, u)
+            wb_pass(0, u)
+        cast("scalar", 1, 0, 1)
+        evacuate("vector", 0, 0)
+        quantize_pass(1, 0)
+        for u in range(HALVES):
+            h_pass(1, 0, u)
+        cast("scalar", 1, 1, 0)
+        evacuate("vector", 0, 1)
+        store(0, 0, HALVES)
+        for t in range(TILES):
+            quantize_chunk(1, 1, 0, t)
+        for u in range(HALVES):
+            w_passes(1, u)
+        cast("vector", 1, 1, 1, 0, 40)
+        cast("scalar", 1, 1, 1, 40, M_CHUNK)
+        for t in range(TILES):
+            quantize_chunk(1, 1, 1, t)
+        for u in range(HALVES):
+            h_pass(1, 1, u)
+        for u in range(HALVES):
+            gelu(1, u)
+            quantize_h(1, u)
+            wb_pass(1, u)
+        evacuate("vector", 1, 0)
+        store(1, 0, 1)
+        evacuate("scalar", 1, 1)
+        store(1, 1, 2)

@@ -49,17 +49,11 @@ def tile_moe_elr_s_gelu_kernel(tc, x_words, x_scales, w_words, w_scales, wa, wb_
         nc.vector.memset(wbs[:].bitcast(I32), 0)
 
         xw = [sb(f"xw{s}", [P, T], I32) for s in range(PASSES)]
-        width = PACK * M_CHUNK
-        raw, whole = {}, {}
+        raw = {}
         for e in range(E):
             for s in range(PASSES):
-                if e == s:
-                    for c in range(CHUNKS):
-                        raw[e, s, c] = sb(f"raw{e}{s}{c}", [P, PACK, width], F32)[:]
-                else:
-                    whole[e, s] = sb(f"raw{e}{s}", [P, PACK, H], F32)
-                    for c in range(CHUNKS):
-                        raw[e, s, c] = whole[e, s][:, :, c * width : (c + 1) * width]
+                for c in range(CHUNKS):
+                    raw[e, s, c] = sb(f"raw{e}{s}{c}", [P, PACK, PACK * M_CHUNK], F32)
         ww = [sb(f"ww{e}", [P, PASSES, 2 * N], U8) for e in range(E)]
         wbw = [sb(f"wbw{e}", [P, N], I32) for e in range(E)]
 
@@ -72,10 +66,8 @@ def tile_moe_elr_s_gelu_kernel(tc, x_words, x_scales, w_words, w_scales, wa, wb_
 
         def load_wa(e, s, c):
             rows = wa[e, 512 * s : 512 * (s + 1), :].rearrange("(p j) i -> p j i", j=PACK)
-            if c is None:
-                nc.sync.dma_start(whole[e, s][:], rows)
-            else:
-                nc.sync.dma_start(raw[e, s, c], rows[:, :, c * width : (c + 1) * width])
+            width = PACK * M_CHUNK
+            nc.sync.dma_start(raw[e, s, c][:], rows[:, :, c * width : (c + 1) * width])
 
         def load_ws(r):
             rows = w_scales.rearrange("e s (q r) n -> r q (e s) n", r=4)
@@ -94,21 +86,29 @@ def tile_moe_elr_s_gelu_kernel(tc, x_words, x_scales, w_words, w_scales, wa, wb_
 
         load_x(0)
         load_wa(0, 0, 0)
-        for r in range(4):
-            load_xs(r)
-        load_wa(0, 0, 1)
+        load_xs(0)
+        load_xs(1)
+        load_xs(2)
+        load_xs(3)
         load_x(1)
-        load_wa(0, 1, None)
-        for r in range(4):
-            load_ws(r)
-        load_w(0)
-        load_wa(1, 0, None)
-        for r in range(4):
-            load_wbs(r)
-        load_wb(0)
+        load_wa(0, 0, 1)
+        load_wa(1, 0, 0)
+        load_wa(0, 1, 0)
+        load_wbs(0)
+        load_wbs(1)
+        load_wbs(2)
+        load_wbs(3)
+        load_wa(0, 1, 1)
+        load_wa(1, 0, 1)
         load_wa(1, 1, 0)
-        load_w(1)
+        load_ws(0)
+        load_ws(1)
+        load_ws(2)
+        load_ws(3)
+        load_w(0)
         load_wa(1, 1, 1)
+        load_wb(0)
+        load_w(1)
         load_wb(1)
 
         xg = [sb(f"xg{s}", [P, E * C], U32) for s in range(PASSES)]
@@ -122,23 +122,23 @@ def tile_moe_elr_s_gelu_kernel(tc, x_words, x_scales, w_words, w_scales, wa, wb_
         h_bank, y_bank, h_bf, h_codes, h_scale = {}, {}, {}, {}, {}
         for e in range(E):
             for u in range(HALVES):
-                h_bank[e, u] = psum.tile([P, TILES, HALF], F32, name=f"h_bank{e}{u}")
-                y_bank[e, u] = psum.tile([P, TILES, HALF], F32, name=f"y_bank{e}{u}")
+                h_bank[e, u] = psum.tile([P, TILES, HALF], F32, name=f"h_bank{e}{u}", tag=f"h{e}{u}")
                 h_bf[e, u] = sb(f"h_bf{e}{u}", [P, HALF, PACK], BF16)
                 h_codes[e, u] = sb(f"h_codes{e}{u}", [P, HALF], U32)
                 h_scale[e, u] = sb(f"h_scale{e}{u}", [P, HALF], U8)
         y_sb = [sb(f"y_sb{e}", [P, TILES, C], F32) for e in range(E)]
 
-        def gather_words(e, s):
-            picks = offsets[:, e * C // 16 : (e + 1) * C // 16]
-            nc.vector.tensor_copy(xg[s][:, e * C : (e + 1) * C], xw[s][:].bitcast(U32).indirect(picks))
+        def gather_words(s):
+            nc.vector.tensor_copy(xg[s][:], xw[s][:].bitcast(U32).indirect(offsets[:]))
 
-        def gather_scales(e, s):
-            picks = offsets[:, e * C // 16 : (e + 1) * C // 16]
-            nc.vector.tensor_copy(xgs[s][:, e * C : (e + 1) * C], xs[:, s, :].indirect(picks))
+        def gather_scales(s):
+            nc.vector.tensor_copy(xgs[s][:], xs[:, s, :].indirect(offsets[:]))
+
+        def groups(e, u):
+            return ((0, 2), (2, 4)) if (e, u) == (1, 1) else ((0, 4),)
 
         def cast(engine, e, s, c, m0=0, m1=M_CHUNK):
-            src = raw[e, s, c].rearrange("p j (m t) -> p m j t", t=TILES)[:, m0:m1]
+            src = raw[e, s, c][:].rearrange("p j (m t) -> p m j t", t=TILES)[:, m0:m1]
             dst = grouped[e, s][:].rearrange("p t m j -> p m j t")[:, c * M_CHUNK + m0 : c * M_CHUNK + m1]
             if engine == "scalar":
                 nc.scalar.copy(dst, src)
@@ -175,16 +175,19 @@ def tile_moe_elr_s_gelu_kernel(tc, x_words, x_scales, w_words, w_scales, wa, wb_
                     stop=(s == PASSES - 1 and t == TILES - 1),
                 )
 
-        def w_passes(e, u):
-            for s in range(PASSES):
-                for q in range(TILES):
+        def w_pass(e, u, s):
+            for q0, q1 in groups(e, u):
+                if s == 0:
+                    tag = "h00" if q0 else f"y{e}{u}"
+                    y_bank[e, u, q0] = psum.tile([P, q1 - q0, HALF], F32, name=f"y_bank{e}{u}{q0}", tag=tag)
+                for q in range(q0, q1):
                     nc.tensor.matmul_mx(
-                        out=y_bank[e, u][:, q, :],
+                        out=y_bank[e, u, q0][:, q - q0, :],
                         lhsT=ww[e][:, s, 2 * P * q : 2 * P * (q + 1)].bitcast(FP4X4),
                         lhsT_scale=ws[:, e * PASSES + s, P * q : P * (q + 1)],
                         rhs=xg[s][:, slots(e, u)].bitcast(FP8X4),
                         rhs_scale=xgs[s][:, slots(e, u)],
-                        start=(s == 0 and q == 0),
+                        start=(s == 0 and q == q0),
                         stop=False,
                     )
 
@@ -199,79 +202,93 @@ def tile_moe_elr_s_gelu_kernel(tc, x_words, x_scales, w_words, w_scales, wa, wb_
             )
 
         def wb_pass(e, u):
-            for q in range(TILES):
-                nc.tensor.matmul_mx(
-                    out=y_bank[e, u][:, q, :],
-                    lhsT=wbw[e][:, P * q : P * (q + 1)].bitcast(FP8X4),
-                    lhsT_scale=wbs[4 * (e + 1) : P, P * q : P * (q + 1)],
-                    rhs=h_codes[e, u][:].bitcast(FP8X4),
-                    rhs_scale=h_scale[e, u][:],
-                    start=False,
-                    stop=(q == TILES - 1),
-                )
+            for q0, q1 in groups(e, u):
+                for q in range(q0, q1):
+                    nc.tensor.matmul_mx(
+                        out=y_bank[e, u, q0][:, q - q0, :],
+                        lhsT=wbw[e][:, P * q : P * (q + 1)].bitcast(FP8X4),
+                        lhsT_scale=wbs[4 * (e + 1) : P, P * q : P * (q + 1)],
+                        rhs=h_codes[e, u][:].bitcast(FP8X4),
+                        rhs_scale=h_scale[e, u][:],
+                        start=False,
+                        stop=(q == q1 - 1),
+                    )
 
-        def evacuate(engine, e, u):
-            dst = y_sb[e][:, :, u * HALF : (u + 1) * HALF]
+        def evacuate(engine, e, u, q0, q1):
+            dst = y_sb[e][:, q0:q1, u * HALF : (u + 1) * HALF]
             if engine == "scalar":
-                nc.scalar.copy(dst, y_bank[e, u][:])
+                nc.scalar.copy(dst, y_bank[e, u, q0][:])
             else:
-                nc.vector.tensor_copy(dst, y_bank[e, u][:])
+                nc.vector.tensor_copy(dst, y_bank[e, u, q0][:])
 
         out_rows = out.rearrange("(q p) j -> p q j", p=P)
 
-        def store(e, u0, u1):
+        def store(e, u0, u1, q0, q1):
             nc.sync.dma_start(
-                out_rows[:, :, e * C + u0 * HALF : e * C + u1 * HALF], y_sb[e][:, :, u0 * HALF : u1 * HALF]
+                out_rows[:, q0:q1, e * C + u0 * HALF : e * C + u1 * HALF], y_sb[e][:, q0:q1, u0 * HALF : u1 * HALF]
             )
 
-        gather_words(0, 0)
-        cast("scalar", 0, 0, 0)
-        gather_words(1, 0)
-        cast("scalar", 0, 0, 1)
-        gather_scales(0, 0)
-        gather_words(0, 1)
+        gather_words(0)
+        gather_scales(0)
+        gather_words(1)
+        gather_scales(1)
+        cast("vector", 0, 0, 0, 0, 16)
+        cast("scalar", 0, 0, 0, 16, 64)
+        cast("vector", 0, 0, 1, 0, 16)
+        cast("scalar", 0, 0, 1, 16, 64)
         quantize_pass(0, 0)
-        gather_scales(0, 1)
-        for u in range(HALVES):
-            h_pass(0, 0, u)
-        cast("scalar", 0, 1, 0)
-        cast("scalar", 0, 1, 1)
-        gather_words(1, 1)
-        gather_scales(1, 0)
-        quantize_pass(0, 1)
-        gather_scales(1, 1)
-        for u in range(HALVES):
-            h_pass(0, 1, u)
-        for u in range(HALVES):
-            gelu(0, u)
-            w_passes(0, u)
-        cast("vector", 1, 0, 0)
-        for u in range(HALVES):
-            quantize_h(0, u)
-            wb_pass(0, u)
-        cast("scalar", 1, 0, 1)
-        evacuate("vector", 0, 0)
+        h_pass(0, 0, 0)
+        h_pass(0, 0, 1)
+        cast("vector", 1, 0, 0, 0, 32)
+        cast("scalar", 1, 0, 0, 32, 64)
+        cast("vector", 1, 0, 1, 0, 32)
+        cast("scalar", 1, 0, 1, 32, 64)
         quantize_pass(1, 0)
-        for u in range(HALVES):
-            h_pass(1, 0, u)
-        cast("scalar", 1, 1, 0)
-        evacuate("vector", 0, 1)
-        store(0, 0, HALVES)
+        h_pass(1, 0, 0)
+        h_pass(1, 0, 1)
+        cast("vector", 0, 1, 0, 0, 32)
+        cast("scalar", 0, 1, 0, 32, 64)
+        cast("vector", 0, 1, 1, 0, 32)
+        cast("scalar", 0, 1, 1, 32, 64)
+        quantize_pass(0, 1)
+        h_pass(0, 1, 0)
+        h_pass(0, 1, 1)
+        cast("vector", 1, 1, 0, 0, 40)
+        cast("scalar", 1, 1, 0, 40, 64)
         for t in range(TILES):
             quantize_chunk(1, 1, 0, t)
-        for u in range(HALVES):
-            w_passes(1, u)
         cast("vector", 1, 1, 1, 0, 40)
-        cast("scalar", 1, 1, 1, 40, M_CHUNK)
+        cast("scalar", 1, 1, 1, 40, 64)
         for t in range(TILES):
             quantize_chunk(1, 1, 1, t)
-        for u in range(HALVES):
-            h_pass(1, 1, u)
-        for u in range(HALVES):
-            gelu(1, u)
-            quantize_h(1, u)
-            wb_pass(1, u)
-        evacuate("vector", 1, 0)
-        store(1, 0, 1)
-        evacuate("scalar", 1, 1)
-        store(1, 1, 2)
+        h_pass(1, 1, 0)
+        h_pass(1, 1, 1)
+        gelu(0, 0)
+        gelu(0, 1)
+        quantize_h(0, 0)
+        quantize_h(0, 1)
+        w_pass(0, 0, 0)
+        w_pass(0, 0, 1)
+        w_pass(0, 1, 0)
+        w_pass(0, 1, 1)
+        gelu(1, 0)
+        quantize_h(1, 0)
+        gelu(1, 1)
+        quantize_h(1, 1)
+        wb_pass(0, 0)
+        wb_pass(0, 1)
+        w_pass(1, 0, 0)
+        w_pass(1, 0, 1)
+        w_pass(1, 1, 0)
+        w_pass(1, 1, 1)
+        wb_pass(1, 0)
+        wb_pass(1, 1)
+        evacuate("scalar", 0, 0, 0, 4)
+        evacuate("vector", 0, 1, 0, 4)
+        store(0, 0, 2, 0, 4)
+        evacuate("vector", 1, 0, 0, 4)
+        store(1, 0, 1, 0, 4)
+        evacuate("vector", 1, 1, 0, 2)
+        store(1, 1, 2, 0, 2)
+        evacuate("scalar", 1, 1, 2, 4)
+        store(1, 1, 2, 2, 4)

@@ -21,8 +21,6 @@ PASSES = K // (P * PACK)
 HALF = 128
 HALVES = C // HALF
 TILES = 4
-CHUNKS = 2
-M_CHUNK = P // CHUNKS
 
 
 def tile_moe_elr_s_gelu_kernel(tc, x_words, x_scales, w_words, w_scales, wa, wb_words, wb_scales, offs, out):
@@ -44,16 +42,15 @@ def tile_moe_elr_s_gelu_kernel(tc, x_words, x_scales, w_words, w_scales, wa, wb_
         wbs = sb("wbs", [P, N], U8)
         nc.vector.memset(warm[:], 0.0)
         nc.scalar.activation(warm_out[:], warm[:], GELU)
-        nc.vector.memset(xs[:].bitcast(I32), 0)
         nc.vector.memset(ws[:].bitcast(I32), 0)
+        nc.vector.memset(xs[:].bitcast(I32), 0)
         nc.vector.memset(wbs[:].bitcast(I32), 0)
 
         xw = [sb(f"xw{s}", [P, T], I32) for s in range(PASSES)]
         raw = {}
         for e in range(E):
             for s in range(PASSES):
-                for c in range(CHUNKS):
-                    raw[e, s, c] = sb(f"raw{e}{s}{c}", [P, PACK, PACK * M_CHUNK], F32)
+                raw[e, s] = sb(f"raw{e}{s}", [P, PACK, H], F32)
         ww = [sb(f"ww{e}", [P, PASSES, 2 * N], U8) for e in range(E)]
         wbw = [sb(f"wbw{e}", [P, N], I32) for e in range(E)]
 
@@ -64,14 +61,13 @@ def tile_moe_elr_s_gelu_kernel(tc, x_words, x_scales, w_words, w_scales, wa, wb_
             rows = x_scales.rearrange("s (q r) t -> r q s t", r=4)
             nc.sync.dma_start(xs[r:P:32].bitcast(I32), rows[r].bitcast(I32))
 
-        def load_wa(e, s, c):
+        def load_wa(e, s):
             rows = wa[e, 512 * s : 512 * (s + 1), :].rearrange("(p j) i -> p j i", j=PACK)
-            width = PACK * M_CHUNK
-            nc.sync.dma_start(raw[e, s, c][:], rows[:, :, c * width : (c + 1) * width])
+            nc.sync.dma_start(raw[e, s][:], rows)
 
         def load_ws(r):
             rows = w_scales.rearrange("e s (q r) n -> r q (e s) n", r=4)
-            nc.sync.dma_start(ws[r:P:32].bitcast(I32), rows[r].bitcast(I32))
+            nc.gpsimd.dma_start(ws[r:P:32].bitcast(I32), rows[r].bitcast(I32))
 
         def load_wbs(q):
             nc.sync.dma_start(
@@ -84,32 +80,28 @@ def tile_moe_elr_s_gelu_kernel(tc, x_words, x_scales, w_words, w_scales, wa, wb_
         def load_wb(e):
             nc.sync.dma_start(wbw[e][:], wb_words[e, 0].rearrange("p n d -> p (n d)").bitcast(I32))
 
-        load_x(0)
-        load_wa(0, 0, 0)
-        load_xs(0)
-        load_xs(1)
-        load_xs(2)
-        load_xs(3)
-        load_x(1)
-        load_wa(0, 0, 1)
-        load_wa(1, 0, 0)
-        load_wa(0, 1, 0)
-        load_wbs(0)
-        load_wbs(1)
-        load_wbs(2)
-        load_wbs(3)
-        load_wa(0, 1, 1)
-        load_wa(1, 0, 1)
-        load_wa(1, 1, 0)
         load_ws(0)
         load_ws(1)
         load_ws(2)
         load_ws(3)
+        load_x(0)
+        load_xs(0)
+        load_xs(1)
+        load_xs(2)
+        load_xs(3)
+        load_wa(0, 0)
+        load_x(1)
+        load_wbs(0)
+        load_wbs(1)
+        load_wbs(2)
+        load_wbs(3)
+        load_wa(0, 1)
+        load_wa(1, 0)
         load_w(0)
-        load_wa(1, 1, 1)
+        load_wa(1, 1)
         load_wb(0)
-        load_w(1)
         load_wb(1)
+        load_w(1)
 
         xg = [sb(f"xg{s}", [P, E * C], U32) for s in range(PASSES)]
         xgs = [sb(f"xgs{s}", [P, E * C], U8) for s in range(PASSES)]
@@ -137,9 +129,9 @@ def tile_moe_elr_s_gelu_kernel(tc, x_words, x_scales, w_words, w_scales, wa, wb_
         def groups(e, u):
             return ((0, 2), (2, 4)) if (e, u) == (1, 1) else ((0, 4),)
 
-        def cast(engine, e, s, c, m0=0, m1=M_CHUNK):
-            src = raw[e, s, c][:].rearrange("p j (m t) -> p m j t", t=TILES)[:, m0:m1]
-            dst = grouped[e, s][:].rearrange("p t m j -> p m j t")[:, c * M_CHUNK + m0 : c * M_CHUNK + m1]
+        def cast(engine, e, s, m0, m1):
+            src = raw[e, s][:].rearrange("p j (m t) -> p m j t", t=TILES)[:, m0:m1]
+            dst = grouped[e, s][:].rearrange("p t m j -> p m j t")[:, m0:m1]
             if engine == "scalar":
                 nc.scalar.copy(dst, src)
             else:
@@ -152,12 +144,11 @@ def tile_moe_elr_s_gelu_kernel(tc, x_words, x_scales, w_words, w_scales, wa, wb_
                 in_=grouped[e, s][:].rearrange("p t m j -> p (t m j)"),
             )
 
-        def quantize_chunk(e, s, c, t):
-            ms = slice(c * M_CHUNK, (c + 1) * M_CHUNK)
+        def quantize_tile(e, s, t):
             nc.vector.quantize_mx(
-                out=wa_codes[e, s][:, t, ms].bitcast(FP8X4),
-                scales=wa_scale[e, s][:, t, ms],
-                in_=grouped[e, s][:, t, ms, :].rearrange("p m j -> p (m j)"),
+                out=wa_codes[e, s][:, t, :].bitcast(FP8X4),
+                scales=wa_scale[e, s][:, t, :],
+                in_=grouped[e, s][:, t, :, :].rearrange("p m j -> p (m j)"),
             )
 
         def slots(e, u):
@@ -232,35 +223,24 @@ def tile_moe_elr_s_gelu_kernel(tc, x_words, x_scales, w_words, w_scales, wa, wb_
         gather_scales(0)
         gather_words(1)
         gather_scales(1)
-        cast("vector", 0, 0, 0, 0, 16)
-        cast("scalar", 0, 0, 0, 16, 64)
-        cast("vector", 0, 0, 1, 0, 16)
-        cast("scalar", 0, 0, 1, 16, 64)
+        cast("scalar", 0, 0, 0, P)
         quantize_pass(0, 0)
         h_pass(0, 0, 0)
         h_pass(0, 0, 1)
-        cast("vector", 1, 0, 0, 0, 32)
-        cast("scalar", 1, 0, 0, 32, 64)
-        cast("vector", 1, 0, 1, 0, 32)
-        cast("scalar", 1, 0, 1, 32, 64)
-        quantize_pass(1, 0)
-        h_pass(1, 0, 0)
-        h_pass(1, 0, 1)
-        cast("vector", 0, 1, 0, 0, 32)
-        cast("scalar", 0, 1, 0, 32, 64)
-        cast("vector", 0, 1, 1, 0, 32)
-        cast("scalar", 0, 1, 1, 32, 64)
+        cast("vector", 0, 1, 0, 40)
+        cast("scalar", 0, 1, 40, P)
         quantize_pass(0, 1)
         h_pass(0, 1, 0)
         h_pass(0, 1, 1)
-        cast("vector", 1, 1, 0, 0, 40)
-        cast("scalar", 1, 1, 0, 40, 64)
+        cast("vector", 1, 0, 0, 64)
+        cast("scalar", 1, 0, 64, P)
+        quantize_pass(1, 0)
+        h_pass(1, 0, 0)
+        h_pass(1, 0, 1)
+        cast("vector", 1, 1, 0, 80)
+        cast("scalar", 1, 1, 80, P)
         for t in range(TILES):
-            quantize_chunk(1, 1, 0, t)
-        cast("vector", 1, 1, 1, 0, 40)
-        cast("scalar", 1, 1, 1, 40, 64)
-        for t in range(TILES):
-            quantize_chunk(1, 1, 1, t)
+            quantize_tile(1, 1, t)
         h_pass(1, 1, 0)
         h_pass(1, 1, 1)
         gelu(0, 0)
@@ -284,7 +264,7 @@ def tile_moe_elr_s_gelu_kernel(tc, x_words, x_scales, w_words, w_scales, wa, wb_
         wb_pass(1, 0)
         wb_pass(1, 1)
         evacuate("scalar", 0, 0, 0, 4)
-        evacuate("vector", 0, 1, 0, 4)
+        evacuate("scalar", 0, 1, 0, 4)
         store(0, 0, 2, 0, 4)
         evacuate("vector", 1, 0, 0, 4)
         store(1, 0, 1, 0, 4)

@@ -17,14 +17,25 @@ GELU = mybir.ActivationFunctionType.Gelu_apprx_tanh
 
 P = 128
 PACK = 4
-PASSES = K // (P * PACK)
+K_PASS = P * PACK
+PASSES = K // K_PASS
+QUADRANT = 32
+SCALE_ROWS = 4
+LIST_GROUP = 16
+TILES = N // P
 HALF = 128
 HALVES = C // HALF
-TILES = 4
+
+VECTOR_SHARE = {(0, 0): 0, (0, 1): 40, (1, 0): 64, (1, 1): 88}
+
+BANK_TILES = {0: ((0, 4),), 1: ((0, 2), (2, 4))}
 
 
-def tile_moe_elr_s_gelu_kernel(tc, x_words, x_scales, w_words, w_scales, wa, wb_words, wb_scales, offs, out):
+def tile_moe_elr_s_gelu_kernel(
+    tc, x_words, x_scales, w_words, w_scales, wa, wb_words, wb_scales, offs, out
+):
     nc = tc.nc
+    last = E - 1
     with ExitStack() as ctx:
         keep = ctx.enter_context(tc.tile_pool(name="keep", bufs=1))
         psum = ctx.enter_context(tc.psum_pool(name="psum", bufs=1))
@@ -32,69 +43,60 @@ def tile_moe_elr_s_gelu_kernel(tc, x_words, x_scales, w_words, w_scales, wa, wb_
         def sb(name, shape, dtype):
             return keep.tile(shape, dtype, name=name, align_bytes=64)
 
-        offsets = keep.tile([P, E * C // 16], U16, name="offsets")
+        offsets = keep.tile([P, E * C // LIST_GROUP], U16, name="offsets")
         nc.sync.dma_start(offsets[:], offs)
 
         warm = sb("warm", [P, 8], F32)
         warm_out = sb("warm_out", [P, 8], F32)
-        xs = sb("xs", [P, PASSES, T], U8)
-        ws = sb("ws", [P, E * PASSES, N], U8)
-        wbs = sb("wbs", [P, N], U8)
         nc.vector.memset(warm[:], 0.0)
         nc.scalar.activation(warm_out[:], warm[:], GELU)
-        nc.vector.memset(ws[:].bitcast(I32), 0)
-        nc.vector.memset(xs[:].bitcast(I32), 0)
-        nc.vector.memset(wbs[:].bitcast(I32), 0)
 
-        xw = [sb(f"xw{s}", [P, T], I32) for s in range(PASSES)]
-        raw = {}
-        for e in range(E):
-            for s in range(PASSES):
-                raw[e, s] = sb(f"raw{e}{s}", [P, PACK, H], F32)
-        ww = [sb(f"ww{e}", [P, PASSES, 2 * N], U8) for e in range(E)]
-        wbw = [sb(f"wbw{e}", [P, N], I32) for e in range(E)]
+        x_sc = sb("x_sc", [P, PASSES, T], U8)
+        w_sc = sb("w_sc", [P, E * PASSES, N], U8)
+        wb_sc = sb("wb_sc", [P, N], U8)
+        for plane in (wb_sc, x_sc, w_sc):
+            nc.vector.memset(plane[:].bitcast(I32), 0)
+
+        x_wd = [sb(f"x_wd{s}", [P, T], I32) for s in range(PASSES)]
+        w_wd = [sb(f"w_wd{e}", [P, PASSES, 2 * N], U8) for e in range(E)]
+        wb_wd = [sb(f"wb_wd{e}", [P, N], I32) for e in range(E)]
+        wa_raw = {(e, s): sb(f"wa_raw{e}{s}", [P, PACK, H], F32) for e in range(E) for s in range(PASSES)}
 
         def load_x(s):
-            nc.sync.dma_start(xw[s][:], x_words[s].rearrange("p t d -> p (t d)").bitcast(I32))
-
-        def load_xs(r):
-            rows = x_scales.rearrange("s (q r) t -> r q s t", r=4)
-            nc.sync.dma_start(xs[r:P:32].bitcast(I32), rows[r].bitcast(I32))
+            nc.sync.dma_start(x_wd[s][:], x_words[s].rearrange("p t d -> p (t d)").bitcast(I32))
 
         def load_wa(e, s):
-            rows = wa[e, 512 * s : 512 * (s + 1), :].rearrange("(p j) i -> p j i", j=PACK)
-            nc.sync.dma_start(raw[e, s][:], rows)
-
-        def load_ws(r):
-            rows = w_scales.rearrange("e s (q r) n -> r q (e s) n", r=4)
-            nc.gpsimd.dma_start(ws[r:P:32].bitcast(I32), rows[r].bitcast(I32))
-
-        def load_wbs(q):
-            nc.sync.dma_start(
-                wbs[32 * q + 4 : 32 * q + 4 + 4 * E].bitcast(I32), wb_scales[:, 0, 4 * q : 4 * q + 4, :].bitcast(I32)
-            )
+            rows = wa[e, K_PASS * s : K_PASS * (s + 1), :].rearrange("(p j) i -> p j i", j=PACK)
+            nc.sync.dma_start(wa_raw[e, s][:], rows)
 
         def load_w(e):
-            nc.sync.dma_start(ww[e][:].bitcast(I32), w_words[e].rearrange("s p b -> p s b").bitcast(I32))
+            nc.sync.dma_start(w_wd[e][:].bitcast(I32), w_words[e].rearrange("s p b -> p s b").bitcast(I32))
 
         def load_wb(e):
-            nc.sync.dma_start(wbw[e][:], wb_words[e, 0].rearrange("p n d -> p (n d)").bitcast(I32))
+            nc.sync.dma_start(wb_wd[e][:], wb_words[e, 0].rearrange("p n d -> p (n d)").bitcast(I32))
 
-        load_ws(0)
-        load_ws(1)
-        load_ws(2)
-        load_ws(3)
-        load_x(0)
-        load_xs(0)
-        load_xs(1)
-        load_xs(2)
-        load_xs(3)
+        def load_x_scales():
+            rows = x_scales.rearrange("s (q r) t -> r q s t", r=SCALE_ROWS)
+            for r in range(SCALE_ROWS):
+                nc.gpsimd.dma_start(x_sc[r:P:QUADRANT].bitcast(I32), rows[r].bitcast(I32))
+
+        def load_w_scales():
+            rows = w_scales.rearrange("e s (q r) n -> r q (e s) n", r=SCALE_ROWS)
+            for r in range(SCALE_ROWS):
+                nc.gpsimd.dma_start(w_sc[r:P:QUADRANT].bitcast(I32), rows[r].bitcast(I32))
+
+        def load_wb_scales():
+            for q in range(P // QUADRANT):
+                first = QUADRANT * q + SCALE_ROWS
+                rows = wb_scales[:, 0, SCALE_ROWS * q : SCALE_ROWS * (q + 1), :]
+                nc.sync.dma_start(wb_sc[first : first + SCALE_ROWS * E].bitcast(I32), rows.bitcast(I32))
+
+        load_x_scales()
+        load_w_scales()
+        for s in range(PASSES):
+            load_x(s)
+        load_wb_scales()
         load_wa(0, 0)
-        load_x(1)
-        load_wbs(0)
-        load_wbs(1)
-        load_wbs(2)
-        load_wbs(3)
         load_wa(0, 1)
         load_wa(1, 0)
         load_w(0)
@@ -103,81 +105,66 @@ def tile_moe_elr_s_gelu_kernel(tc, x_words, x_scales, w_words, w_scales, wa, wb_
         load_wb(1)
         load_w(1)
 
-        xg = [sb(f"xg{s}", [P, E * C], U32) for s in range(PASSES)]
-        xgs = [sb(f"xgs{s}", [P, E * C], U8) for s in range(PASSES)]
-        grouped, wa_codes, wa_scale = {}, {}, {}
+        slot_wd = [sb(f"slot_wd{s}", [P, E * C], U32) for s in range(PASSES)]
+        slot_sc = [sb(f"slot_sc{s}", [P, E * C], U8) for s in range(PASSES)]
+        wa_bf, wa_wd, wa_sc = {}, {}, {}
         for e in range(E):
             for s in range(PASSES):
-                grouped[e, s] = sb(f"grouped{e}{s}", [P, TILES, P, PACK], BF16)
-                wa_codes[e, s] = sb(f"wa_codes{e}{s}", [P, TILES, P], U32)
-                wa_scale[e, s] = sb(f"wa_scale{e}{s}", [P, TILES, P], U8)
-        h_bank, y_bank, h_bf, h_codes, h_scale = {}, {}, {}, {}, {}
+                wa_bf[e, s] = sb(f"wa_bf{e}{s}", [P, TILES, P, PACK], BF16)
+                wa_wd[e, s] = sb(f"wa_wd{e}{s}", [P, TILES, P], U32)
+                wa_sc[e, s] = sb(f"wa_sc{e}{s}", [P, TILES, P], U8)
+        h_bank, y_bank, h_bf, h_wd, h_sc = {}, {}, {}, {}, {}
         for e in range(E):
             for u in range(HALVES):
                 h_bank[e, u] = psum.tile([P, TILES, HALF], F32, name=f"h_bank{e}{u}", tag=f"h{e}{u}")
                 h_bf[e, u] = sb(f"h_bf{e}{u}", [P, HALF, PACK], BF16)
-                h_codes[e, u] = sb(f"h_codes{e}{u}", [P, HALF], U32)
-                h_scale[e, u] = sb(f"h_scale{e}{u}", [P, HALF], U8)
+                h_wd[e, u] = sb(f"h_wd{e}{u}", [P, HALF], U32)
+                h_sc[e, u] = sb(f"h_sc{e}{u}", [P, HALF], U8)
         y_sb = [sb(f"y_sb{e}", [P, TILES, C], F32) for e in range(E)]
-
-        def gather_words(s):
-            nc.vector.tensor_copy(xg[s][:], xw[s][:].bitcast(U32).indirect(offsets[:]))
-
-        def gather_scales(s):
-            nc.vector.tensor_copy(xgs[s][:], xs[:, s, :].indirect(offsets[:]))
-
-        def groups(e, u):
-            return ((0, 2), (2, 4)) if (e, u) == (1, 1) else ((0, 4),)
-
-        def cast(engine, e, s, m0, m1):
-            src = raw[e, s][:].rearrange("p j (m t) -> p m j t", t=TILES)[:, m0:m1]
-            dst = grouped[e, s][:].rearrange("p t m j -> p m j t")[:, m0:m1]
-            if engine == "scalar":
-                nc.scalar.copy(dst, src)
-            else:
-                nc.vector.tensor_copy(dst, src)
-
-        def quantize_pass(e, s):
-            nc.vector.quantize_mx(
-                out=wa_codes[e, s][:].rearrange("p t m -> p (t m)").bitcast(FP8X4),
-                scales=wa_scale[e, s][:].rearrange("p t m -> p (t m)"),
-                in_=grouped[e, s][:].rearrange("p t m j -> p (t m j)"),
-            )
-
-        def quantize_tile(e, s, t):
-            nc.vector.quantize_mx(
-                out=wa_codes[e, s][:, t, :].bitcast(FP8X4),
-                scales=wa_scale[e, s][:, t, :],
-                in_=grouped[e, s][:, t, :, :].rearrange("p m j -> p (m j)"),
-            )
+        out_rows = out.rearrange("(q p) j -> p q j", p=P)
 
         def slots(e, u):
             return slice(e * C + u * HALF, e * C + (u + 1) * HALF)
+
+        def cast_wa(e, s):
+            src = wa_raw[e, s][:].rearrange("p j (m t) -> p m j t", t=TILES)
+            dst = wa_bf[e, s][:].rearrange("p t m j -> p m j t")
+            share = VECTOR_SHARE[e, s]
+            if share:
+                nc.vector.tensor_copy(dst[:, :share], src[:, :share])
+            nc.scalar.copy(dst[:, share:], src[:, share:])
+
+        def quantize_wa(e, s, t0, t1):
+            nc.vector.quantize_mx(
+                out=wa_wd[e, s][:, t0:t1, :].rearrange("p t m -> p (t m)").bitcast(FP8X4),
+                scales=wa_sc[e, s][:, t0:t1, :].rearrange("p t m -> p (t m)"),
+                in_=wa_bf[e, s][:, t0:t1, :, :].rearrange("p t m j -> p (t m j)"),
+            )
 
         def h_pass(e, s, u):
             for t in range(TILES):
                 nc.tensor.matmul_mx(
                     out=h_bank[e, u][:, t, :],
-                    lhsT=wa_codes[e, s][:, t, :].bitcast(FP8X4),
-                    lhsT_scale=wa_scale[e, s][:, t, :],
-                    rhs=xg[s][:, slots(e, u)].bitcast(FP8X4),
-                    rhs_scale=xgs[s][:, slots(e, u)],
+                    lhsT=wa_wd[e, s][:, t, :].bitcast(FP8X4),
+                    lhsT_scale=wa_sc[e, s][:, t, :],
+                    rhs=slot_wd[s][:, slots(e, u)].bitcast(FP8X4),
+                    rhs_scale=slot_sc[s][:, slots(e, u)],
                     start=(s == 0 and t == 0),
                     stop=(s == PASSES - 1 and t == TILES - 1),
                 )
 
-        def w_pass(e, u, s):
-            for q0, q1 in groups(e, u):
+        def w_pass(e, s, u):
+            for q0, q1 in BANK_TILES[e]:
                 if s == 0:
-                    tag = "h00" if q0 else f"y{e}{u}"
+                    tag = f"h0{u}" if q0 else f"y{e}{u}"
                     y_bank[e, u, q0] = psum.tile([P, q1 - q0, HALF], F32, name=f"y_bank{e}{u}{q0}", tag=tag)
                 for q in range(q0, q1):
                     nc.tensor.matmul_mx(
                         out=y_bank[e, u, q0][:, q - q0, :],
-                        lhsT=ww[e][:, s, 2 * P * q : 2 * P * (q + 1)].bitcast(FP4X4),
-                        lhsT_scale=ws[:, e * PASSES + s, P * q : P * (q + 1)],
-                        rhs=xg[s][:, slots(e, u)].bitcast(FP8X4),
-                        rhs_scale=xgs[s][:, slots(e, u)],
+                        lhsT=w_wd[e][:, s, 2 * P * q : 2 * P * (q + 1)].bitcast(FP4X4),
+                        lhsT_scale=w_sc[:, e * PASSES + s, P * q : P * (q + 1)],
+                        rhs=slot_wd[s][:, slots(e, u)].bitcast(FP8X4),
+                        rhs_scale=slot_sc[s][:, slots(e, u)],
                         start=(s == 0 and q == q0),
                         stop=False,
                     )
@@ -187,88 +174,68 @@ def tile_moe_elr_s_gelu_kernel(tc, x_words, x_scales, w_words, w_scales, wa, wb_
 
         def quantize_h(e, u):
             nc.vector.quantize_mx(
-                out=h_codes[e, u][:].bitcast(FP8X4),
-                scales=h_scale[e, u][:],
+                out=h_wd[e, u][:].bitcast(FP8X4),
+                scales=h_sc[e, u][:],
                 in_=h_bf[e, u][:].rearrange("p n t -> p (n t)"),
             )
 
         def wb_pass(e, u):
-            for q0, q1 in groups(e, u):
+            for q0, q1 in BANK_TILES[e]:
                 for q in range(q0, q1):
                     nc.tensor.matmul_mx(
                         out=y_bank[e, u, q0][:, q - q0, :],
-                        lhsT=wbw[e][:, P * q : P * (q + 1)].bitcast(FP8X4),
-                        lhsT_scale=wbs[4 * (e + 1) : P, P * q : P * (q + 1)],
-                        rhs=h_codes[e, u][:].bitcast(FP8X4),
-                        rhs_scale=h_scale[e, u][:],
+                        lhsT=wb_wd[e][:, P * q : P * (q + 1)].bitcast(FP8X4),
+                        lhsT_scale=wb_sc[SCALE_ROWS * (e + 1) : P, P * q : P * (q + 1)],
+                        rhs=h_wd[e, u][:].bitcast(FP8X4),
+                        rhs_scale=h_sc[e, u][:],
                         start=False,
                         stop=(q == q1 - 1),
                     )
 
-        def evacuate(engine, e, u, q0, q1):
-            dst = y_sb[e][:, q0:q1, u * HALF : (u + 1) * HALF]
-            if engine == "scalar":
-                nc.scalar.copy(dst, y_bank[e, u, q0][:])
-            else:
-                nc.vector.tensor_copy(dst, y_bank[e, u, q0][:])
+        def evacuate(e, u):
+            for q0, q1 in BANK_TILES[e]:
+                copy = nc.scalar.copy if q1 == TILES else nc.vector.tensor_copy
+                copy(y_sb[e][:, q0:q1, u * HALF : (u + 1) * HALF], y_bank[e, u, q0][:])
 
-        out_rows = out.rearrange("(q p) j -> p q j", p=P)
+        def store(e, u0, u1):
+            columns = slice(e * C + u0 * HALF, e * C + u1 * HALF)
+            nc.sync.dma_start(out_rows[:, :, columns], y_sb[e][:, :, u0 * HALF : u1 * HALF])
 
-        def store(e, u0, u1, q0, q1):
-            nc.sync.dma_start(
-                out_rows[:, q0:q1, e * C + u0 * HALF : e * C + u1 * HALF], y_sb[e][:, q0:q1, u0 * HALF : u1 * HALF]
-            )
+        for s in range(PASSES):
+            nc.vector.tensor_copy(slot_wd[s][:], x_wd[s][:].bitcast(U32).indirect(offsets[:]))
+        for s in range(PASSES):
+            nc.vector.tensor_copy(slot_sc[s][:], x_sc[:, s, :].indirect(offsets[:]))
 
-        gather_words(0)
-        gather_scales(0)
-        gather_words(1)
-        gather_scales(1)
-        cast("scalar", 0, 0, 0, P)
-        quantize_pass(0, 0)
-        h_pass(0, 0, 0)
-        h_pass(0, 0, 1)
-        cast("vector", 0, 1, 0, 40)
-        cast("scalar", 0, 1, 40, P)
-        quantize_pass(0, 1)
-        h_pass(0, 1, 0)
-        h_pass(0, 1, 1)
-        cast("vector", 1, 0, 0, 64)
-        cast("scalar", 1, 0, 64, P)
-        quantize_pass(1, 0)
-        h_pass(1, 0, 0)
-        h_pass(1, 0, 1)
-        cast("vector", 1, 1, 0, 80)
-        cast("scalar", 1, 1, 80, P)
-        for t in range(TILES):
-            quantize_tile(1, 1, t)
-        h_pass(1, 1, 0)
-        h_pass(1, 1, 1)
-        gelu(0, 0)
-        gelu(0, 1)
-        quantize_h(0, 0)
-        quantize_h(0, 1)
-        w_pass(0, 0, 0)
-        w_pass(0, 0, 1)
-        w_pass(0, 1, 0)
-        w_pass(0, 1, 1)
-        gelu(1, 0)
-        quantize_h(1, 0)
-        gelu(1, 1)
-        quantize_h(1, 1)
-        wb_pass(0, 0)
-        wb_pass(0, 1)
-        w_pass(1, 0, 0)
-        w_pass(1, 0, 1)
-        w_pass(1, 1, 0)
-        w_pass(1, 1, 1)
-        wb_pass(1, 0)
-        wb_pass(1, 1)
-        evacuate("scalar", 0, 0, 0, 4)
-        evacuate("scalar", 0, 1, 0, 4)
-        store(0, 0, 2, 0, 4)
-        evacuate("vector", 1, 0, 0, 4)
-        store(1, 0, 1, 0, 4)
-        evacuate("vector", 1, 1, 0, 2)
-        store(1, 1, 2, 0, 2)
-        evacuate("scalar", 1, 1, 2, 4)
-        store(1, 1, 2, 2, 4)
+        for e in range(E):
+            for s in range(PASSES):
+                cast_wa(e, s)
+                step = 1 if (e, s) == (last, PASSES - 1) else TILES
+                for t in range(0, TILES, step):
+                    quantize_wa(e, s, t, t + step)
+                for u in range(HALVES):
+                    h_pass(e, s, u)
+
+        for u in range(HALVES):
+            gelu(0, u)
+        for u in range(HALVES):
+            quantize_h(0, u)
+        for u in range(HALVES):
+            for s in range(PASSES):
+                w_pass(0, s, u)
+        for u in range(HALVES):
+            gelu(last, u)
+            quantize_h(last, u)
+        for u in range(HALVES):
+            wb_pass(0, u)
+        for u in range(HALVES):
+            for s in range(PASSES):
+                w_pass(last, s, u)
+        for u in range(HALVES):
+            wb_pass(last, u)
+
+        for u in range(HALVES):
+            evacuate(0, u)
+        store(0, 0, HALVES)
+        for u in range(HALVES):
+            evacuate(last, u)
+            store(last, u, u + 1)

@@ -26,7 +26,7 @@ TILES = N // P
 HALF = 128
 HALVES = C // HALF
 
-VECTOR_SHARE = {(0, 0): 0, (0, 1): 40, (1, 0): 64, (1, 1): 88}
+VECTOR_SHARE = {(0, 0): 48, (0, 1): 72, (1, 0): 88, (1, 1): 88}
 
 BANK_TILES = {0: ((0, 4),), 1: ((0, 2), (2, 4))}
 
@@ -54,7 +54,7 @@ def tile_moe_elr_s_gelu_kernel(
         x_sc = sb("x_sc", [P, PASSES, T], U8)
         w_sc = sb("w_sc", [P, E * PASSES, N], U8)
         wb_sc = sb("wb_sc", [P, N], U8)
-        for plane in (wb_sc, x_sc, w_sc):
+        for plane in (w_sc, x_sc, wb_sc):
             nc.vector.memset(plane[:].bitcast(I32), 0)
 
         x_wd = [sb(f"x_wd{s}", [P, T], I32) for s in range(PASSES)]
@@ -78,7 +78,7 @@ def tile_moe_elr_s_gelu_kernel(
         def load_x_scales():
             rows = x_scales.rearrange("s (q r) t -> r q s t", r=SCALE_ROWS)
             for r in range(SCALE_ROWS):
-                nc.gpsimd.dma_start(x_sc[r:P:QUADRANT].bitcast(I32), rows[r].bitcast(I32))
+                nc.sync.dma_start(x_sc[r:P:QUADRANT].bitcast(I32), rows[r].bitcast(I32))
 
         def load_w_scales():
             rows = w_scales.rearrange("e s (q r) n -> r q (e s) n", r=SCALE_ROWS)
@@ -91,19 +91,19 @@ def tile_moe_elr_s_gelu_kernel(
                 rows = wb_scales[:, 0, SCALE_ROWS * q : SCALE_ROWS * (q + 1), :]
                 nc.sync.dma_start(wb_sc[first : first + SCALE_ROWS * E].bitcast(I32), rows.bitcast(I32))
 
-        load_x_scales()
         load_w_scales()
-        for s in range(PASSES):
-            load_x(s)
-        load_wb_scales()
+        load_x(0)
+        load_x_scales()
+        load_x(1)
         load_wa(0, 0)
         load_wa(0, 1)
-        load_wa(1, 0)
+        load_wa(last, 0)
         load_w(0)
-        load_wa(1, 1)
+        load_wb_scales()
+        load_wa(last, 1)
         load_wb(0)
-        load_wb(1)
-        load_w(1)
+        load_wb(last)
+        load_w(last)
 
         slot_wd = [sb(f"slot_wd{s}", [P, E * C], U32) for s in range(PASSES)]
         slot_sc = [sb(f"slot_sc{s}", [P, E * C], U8) for s in range(PASSES)]
@@ -130,8 +130,7 @@ def tile_moe_elr_s_gelu_kernel(
             src = wa_raw[e, s][:].rearrange("p j (m t) -> p m j t", t=TILES)
             dst = wa_bf[e, s][:].rearrange("p t m j -> p m j t")
             share = VECTOR_SHARE[e, s]
-            if share:
-                nc.vector.tensor_copy(dst[:, :share], src[:, :share])
+            nc.vector.tensor_copy(dst[:, :share], src[:, :share])
             nc.scalar.copy(dst[:, share:], src[:, share:])
 
         def quantize_wa(e, s, t0, t1):
@@ -203,7 +202,6 @@ def tile_moe_elr_s_gelu_kernel(
 
         for s in range(PASSES):
             nc.vector.tensor_copy(slot_wd[s][:], x_wd[s][:].bitcast(U32).indirect(offsets[:]))
-        for s in range(PASSES):
             nc.vector.tensor_copy(slot_sc[s][:], x_sc[:, s, :].indirect(offsets[:]))
 
         for e in range(E):

@@ -26,9 +26,10 @@ TILES = N // P
 HALF = 128
 HALVES = C // HALF
 
-VECTOR_SHARE = {(0, 0): 48, (0, 1): 72, (1, 0): 88, (1, 1): 88}
+VECTOR_SHARE = {(0, 0, 0): 32, (0, 1, 0): 64, (1, 0, 0): 76, (1, 1, 0): 80}
+ROW_PIECES = {(0, 0): ((0, 4),), (0, 1): ((0, 4),), (1, 0): ((0, 4),), (1, 1): ((0, 4),)}
 
-BANK_TILES = {0: ((0, 4),), 1: ((0, 2), (2, 4))}
+BANK_TILES = ((0, 2), (2, 4))
 
 
 def tile_moe_elr_s_gelu_kernel(
@@ -44,7 +45,6 @@ def tile_moe_elr_s_gelu_kernel(
             return keep.tile(shape, dtype, name=name, align_bytes=64)
 
         offsets = keep.tile([P, E * C // LIST_GROUP], U16, name="offsets")
-        nc.sync.dma_start(offsets[:], offs)
 
         warm = sb("warm", [P, 8], F32)
         warm_out = sb("warm_out", [P, 8], F32)
@@ -52,22 +52,28 @@ def tile_moe_elr_s_gelu_kernel(
         nc.scalar.activation(warm_out[:], warm[:], GELU)
 
         x_sc = sb("x_sc", [P, PASSES, T], U8)
-        w_sc = sb("w_sc", [P, E * PASSES, N], U8)
-        wb_sc = sb("wb_sc", [P, N], U8)
-        for plane in (w_sc, x_sc, wb_sc):
+        w_sc = [sb(f"w_sc{e}", [P, PASSES, N], U8) for e in range(E)]
+        wb_sc = sb("wb_sc", [P, E, N], U8)
+        for plane in (x_sc, w_sc[0], wb_sc, w_sc[last]):
             nc.vector.memset(plane[:].bitcast(I32), 0)
 
         x_wd = [sb(f"x_wd{s}", [P, T], I32) for s in range(PASSES)]
         w_wd = [sb(f"w_wd{e}", [P, PASSES, 2 * N], U8) for e in range(E)]
         wb_wd = [sb(f"wb_wd{e}", [P, N], I32) for e in range(E)]
-        wa_raw = {(e, s): sb(f"wa_raw{e}{s}", [P, PACK, H], F32) for e in range(E) for s in range(PASSES)}
+        wa_raw = {
+            (e, s, j0): sb(f"wa_raw{e}{s}{j0}", [P, j1 - j0, H], F32)
+            for e in range(E)
+            for s in range(PASSES)
+            for j0, j1 in ROW_PIECES[e, s]
+        }
 
         def load_x(s):
             nc.sync.dma_start(x_wd[s][:], x_words[s].rearrange("p t d -> p (t d)").bitcast(I32))
 
         def load_wa(e, s):
             rows = wa[e, K_PASS * s : K_PASS * (s + 1), :].rearrange("(p j) i -> p j i", j=PACK)
-            nc.sync.dma_start(wa_raw[e, s][:], rows)
+            for j0, j1 in ROW_PIECES[e, s]:
+                nc.sync.dma_start(wa_raw[e, s, j0][:], rows[:, j0:j1, :])
 
         def load_w(e):
             nc.sync.dma_start(w_wd[e][:].bitcast(I32), w_words[e].rearrange("s p b -> p s b").bitcast(I32))
@@ -80,30 +86,31 @@ def tile_moe_elr_s_gelu_kernel(
             for r in range(SCALE_ROWS):
                 nc.sync.dma_start(x_sc[r:P:QUADRANT].bitcast(I32), rows[r].bitcast(I32))
 
-        def load_w_scales():
-            rows = w_scales.rearrange("e s (q r) n -> r q (e s) n", r=SCALE_ROWS)
+        def load_w_scales(e, queue):
+            rows = w_scales[e].rearrange("s (q r) n -> r q s n", r=SCALE_ROWS)
             for r in range(SCALE_ROWS):
-                nc.gpsimd.dma_start(w_sc[r:P:QUADRANT].bitcast(I32), rows[r].bitcast(I32))
+                queue.dma_start(w_sc[e][r:P:QUADRANT].bitcast(I32), rows[r].bitcast(I32))
 
         def load_wb_scales():
-            for q in range(P // QUADRANT):
-                first = QUADRANT * q + SCALE_ROWS
-                rows = wb_scales[:, 0, SCALE_ROWS * q : SCALE_ROWS * (q + 1), :]
-                nc.sync.dma_start(wb_sc[first : first + SCALE_ROWS * E].bitcast(I32), rows.bitcast(I32))
+            rows = wb_scales.rearrange("e s (q r) n -> r q (e s) n", r=SCALE_ROWS)
+            for r in range(SCALE_ROWS):
+                nc.gpsimd.dma_start(wb_sc[SCALE_ROWS + r : P : QUADRANT].bitcast(I32), rows[r].bitcast(I32))
 
-        load_w_scales()
+        load_w_scales(0, nc.gpsimd)
+        load_wb_scales()
         load_x(0)
-        load_x_scales()
+        nc.sync.dma_start(offsets[:], offs)
         load_x(1)
+        load_x_scales()
         load_wa(0, 0)
         load_wa(0, 1)
         load_wa(last, 0)
         load_w(0)
-        load_wb_scales()
         load_wa(last, 1)
         load_wb(0)
-        load_wb(last)
+        load_w_scales(last, nc.sync)
         load_w(last)
+        load_wb(last)
 
         slot_wd = [sb(f"slot_wd{s}", [P, E * C], U32) for s in range(PASSES)]
         slot_sc = [sb(f"slot_sc{s}", [P, E * C], U8) for s in range(PASSES)]
@@ -118,20 +125,21 @@ def tile_moe_elr_s_gelu_kernel(
             for u in range(HALVES):
                 h_bank[e, u] = psum.tile([P, TILES, HALF], F32, name=f"h_bank{e}{u}", tag=f"h{e}{u}")
                 h_bf[e, u] = sb(f"h_bf{e}{u}", [P, HALF, PACK], BF16)
-                h_wd[e, u] = sb(f"h_wd{e}{u}", [P, HALF], U32)
-                h_sc[e, u] = sb(f"h_sc{e}{u}", [P, HALF], U8)
-        y_sb = [sb(f"y_sb{e}", [P, TILES, C], F32) for e in range(E)]
+            h_wd[e] = sb(f"h_wd{e}", [P, C], U32)
+            h_sc[e] = sb(f"h_sc{e}", [P, C], U8)
+        y_last = [sb(f"y_last{u}", [P, TILES, HALF], F32) for u in range(HALVES)]
         out_rows = out.rearrange("(q p) j -> p q j", p=P)
 
         def slots(e, u):
             return slice(e * C + u * HALF, e * C + (u + 1) * HALF)
 
         def cast_wa(e, s):
-            src = wa_raw[e, s][:].rearrange("p j (m t) -> p m j t", t=TILES)
-            dst = wa_bf[e, s][:].rearrange("p t m j -> p m j t")
-            share = VECTOR_SHARE[e, s]
-            nc.vector.tensor_copy(dst[:, :share], src[:, :share])
-            nc.scalar.copy(dst[:, share:], src[:, share:])
+            for j0, j1 in ROW_PIECES[e, s]:
+                src = wa_raw[e, s, j0][:].rearrange("p j (m t) -> p m j t", t=TILES)
+                dst = wa_bf[e, s][:].rearrange("p t m j -> p m j t")[:, :, j0:j1, :]
+                share = VECTOR_SHARE[e, s, j0]
+                nc.vector.tensor_copy(dst[:, :share], src[:, :share])
+                nc.scalar.copy(dst[:, share:], src[:, share:])
 
         def quantize_wa(e, s, t0, t1):
             nc.vector.quantize_mx(
@@ -152,56 +160,49 @@ def tile_moe_elr_s_gelu_kernel(
                     stop=(s == PASSES - 1 and t == TILES - 1),
                 )
 
+        def y_out(e, u, q, width):
+            q0 = q - q % 2
+            if e == 0:
+                return y_bank[0, q0][:, q - q0, u * HALF : u * HALF + width]
+            return y_bank[e, u, q0][:, q - q0, :]
+
         def w_pass(e, s, u):
-            for q0, q1 in BANK_TILES[e]:
-                if s == 0:
-                    tag = f"h0{u}" if q0 else f"y{e}{u}"
-                    y_bank[e, u, q0] = psum.tile([P, q1 - q0, HALF], F32, name=f"y_bank{e}{u}{q0}", tag=tag)
-                for q in range(q0, q1):
-                    nc.tensor.matmul_mx(
-                        out=y_bank[e, u, q0][:, q - q0, :],
-                        lhsT=w_wd[e][:, s, 2 * P * q : 2 * P * (q + 1)].bitcast(FP4X4),
-                        lhsT_scale=w_sc[:, e * PASSES + s, P * q : P * (q + 1)],
-                        rhs=slot_wd[s][:, slots(e, u)].bitcast(FP8X4),
-                        rhs_scale=slot_sc[s][:, slots(e, u)],
-                        start=(s == 0 and q == q0),
-                        stop=False,
-                    )
+            for q in range(TILES):
+                nc.tensor.matmul_mx(
+                    out=y_out(e, u, q, HALF),
+                    lhsT=w_wd[e][:, s, 2 * P * q : 2 * P * (q + 1)].bitcast(FP4X4),
+                    lhsT_scale=w_sc[e][:, s, P * q : P * (q + 1)],
+                    rhs=slot_wd[s][:, slots(e, u)].bitcast(FP8X4),
+                    rhs_scale=slot_sc[s][:, slots(e, u)],
+                    start=(s == 0 and q % 2 == 0 and (e == last or u == 0)),
+                    stop=False,
+                )
 
         def gelu(e, u):
             nc.scalar.activation(h_bf[e, u][:], h_bank[e, u][:].rearrange("p t n -> p n t"), GELU)
 
         def quantize_h(e, u):
             nc.vector.quantize_mx(
-                out=h_wd[e, u][:].bitcast(FP8X4),
-                scales=h_sc[e, u][:],
+                out=h_wd[e][:, u * HALF : (u + 1) * HALF].bitcast(FP8X4),
+                scales=h_sc[e][:, u * HALF : (u + 1) * HALF],
                 in_=h_bf[e, u][:].rearrange("p n t -> p (n t)"),
             )
 
-        def wb_pass(e, u):
-            for q0, q1 in BANK_TILES[e]:
-                for q in range(q0, q1):
-                    nc.tensor.matmul_mx(
-                        out=y_bank[e, u, q0][:, q - q0, :],
-                        lhsT=wb_wd[e][:, P * q : P * (q + 1)].bitcast(FP8X4),
-                        lhsT_scale=wb_sc[SCALE_ROWS * (e + 1) : P, P * q : P * (q + 1)],
-                        rhs=h_wd[e, u][:].bitcast(FP8X4),
-                        rhs_scale=h_sc[e, u][:],
-                        start=False,
-                        stop=(q == q1 - 1),
-                    )
-
-        def evacuate(e, u):
-            for q0, q1 in BANK_TILES[e]:
-                copy = nc.scalar.copy if q1 == TILES else nc.vector.tensor_copy
-                copy(y_sb[e][:, q0:q1, u * HALF : (u + 1) * HALF], y_bank[e, u, q0][:])
-
-        def store(e, u0, u1):
-            columns = slice(e * C + u0 * HALF, e * C + u1 * HALF)
-            nc.sync.dma_start(out_rows[:, :, columns], y_sb[e][:, :, u0 * HALF : u1 * HALF])
+        def wb_pass(e, u, width):
+            for q in range(TILES):
+                nc.tensor.matmul_mx(
+                    out=y_out(e, u, q, width),
+                    lhsT=wb_wd[e][:, P * q : P * (q + 1)].bitcast(FP8X4),
+                    lhsT_scale=wb_sc[SCALE_ROWS:P, e, P * q : P * (q + 1)],
+                    rhs=h_wd[e][:, u * HALF : u * HALF + width].bitcast(FP8X4),
+                    rhs_scale=h_sc[e][:, u * HALF : u * HALF + width],
+                    start=False,
+                    stop=(q % 2 == 1),
+                )
 
         for s in range(PASSES):
             nc.vector.tensor_copy(slot_wd[s][:], x_wd[s][:].bitcast(U32).indirect(offsets[:]))
+        for s in range(PASSES):
             nc.vector.tensor_copy(slot_sc[s][:], x_sc[:, s, :].indirect(offsets[:]))
 
         for e in range(E):
@@ -213,6 +214,8 @@ def tile_moe_elr_s_gelu_kernel(
                 for u in range(HALVES):
                     h_pass(e, s, u)
 
+        for q0, q1 in BANK_TILES:
+            y_bank[0, q0] = psum.tile([P, q1 - q0, C], F32, name=f"y_bank0{q0}", tag=f"y0{q0}")
         for u in range(HALVES):
             gelu(0, u)
         for u in range(HALVES):
@@ -220,20 +223,29 @@ def tile_moe_elr_s_gelu_kernel(
         for u in range(HALVES):
             for s in range(PASSES):
                 w_pass(0, s, u)
+        wb_pass(0, 0, C)
+        spent = wa_bf[last, PASSES - 1]
+        for q0, q1 in BANK_TILES:
+            y_first = spent[:, q0:q1].rearrange("p t m j -> p t (m j)").bitcast(F32)
+            nc.vector.tensor_copy(y_first, y_bank[0, q0][:])
+            nc.sync.dma_start(out_rows[:, q0:q1, 0:C], y_first)
+
         for u in range(HALVES):
             gelu(last, u)
             quantize_h(last, u)
         for u in range(HALVES):
-            wb_pass(0, u)
-        for u in range(HALVES):
+            for q0, q1 in BANK_TILES:
+                tag = f"h0{u}" if q0 else f"y{last}{u}"
+                y_bank[last, u, q0] = psum.tile([P, q1 - q0, HALF], F32, name=f"y_bank1{u}{q0}", tag=tag)
             for s in range(PASSES):
                 w_pass(last, s, u)
         for u in range(HALVES):
-            wb_pass(last, u)
-
+            wb_pass(last, u, HALF)
         for u in range(HALVES):
-            evacuate(0, u)
-        store(0, 0, HALVES)
-        for u in range(HALVES):
-            evacuate(last, u)
-            store(last, u, u + 1)
+            for q0, q1 in BANK_TILES:
+                copy = nc.scalar.copy if q0 else nc.vector.tensor_copy
+                copy(y_last[u][:, q0:q1, :], y_bank[last, u, q0][:])
+                if u == HALVES - 1:
+                    nc.sync.dma_start(out_rows[:, q0:q1, slots(last, u)], y_last[u][:, q0:q1, :])
+            if u < HALVES - 1:
+                nc.sync.dma_start(out_rows[:, :, slots(last, u)], y_last[u][:])

@@ -26,7 +26,7 @@ TILES = N // P
 HALF = 128
 HALVES = C // HALF
 
-VECTOR_SHARE = {(0, 0, 0): 32, (0, 1, 0): 64, (1, 0, 0): 76, (1, 1, 0): 80}
+VECTOR_SHARE = {(0, 0, 0): 0, (0, 1, 0): 76, (1, 0, 0): 88, (1, 1, 0): 76}
 ROW_PIECES = {(0, 0): ((0, 4),), (0, 1): ((0, 4),), (1, 0): ((0, 4),), (1, 1): ((0, 4),)}
 
 BANK_TILES = ((0, 2), (2, 4))
@@ -52,9 +52,9 @@ def tile_moe_elr_s_gelu_kernel(
         nc.scalar.activation(warm_out[:], warm[:], GELU)
 
         x_sc = sb("x_sc", [P, PASSES, T], U8)
-        w_sc = [sb(f"w_sc{e}", [P, PASSES, N], U8) for e in range(E)]
+        w_sc = sb("w_sc", [P, E * PASSES, N], U8)
         wb_sc = sb("wb_sc", [P, E, N], U8)
-        for plane in (x_sc, w_sc[0], wb_sc, w_sc[last]):
+        for plane in (x_sc, w_sc, wb_sc):
             nc.vector.memset(plane[:].bitcast(I32), 0)
 
         x_wd = [sb(f"x_wd{s}", [P, T], I32) for s in range(PASSES)]
@@ -86,29 +86,28 @@ def tile_moe_elr_s_gelu_kernel(
             for r in range(SCALE_ROWS):
                 nc.sync.dma_start(x_sc[r:P:QUADRANT].bitcast(I32), rows[r].bitcast(I32))
 
-        def load_w_scales(e, queue):
-            rows = w_scales[e].rearrange("s (q r) n -> r q s n", r=SCALE_ROWS)
+        def load_w_scales():
+            rows = w_scales.rearrange("e s (q r) n -> r q (e s) n", r=SCALE_ROWS)
             for r in range(SCALE_ROWS):
-                queue.dma_start(w_sc[e][r:P:QUADRANT].bitcast(I32), rows[r].bitcast(I32))
+                nc.sync.dma_start(w_sc[r:P:QUADRANT].bitcast(I32), rows[r].bitcast(I32))
 
         def load_wb_scales():
             rows = wb_scales.rearrange("e s (q r) n -> r q (e s) n", r=SCALE_ROWS)
             for r in range(SCALE_ROWS):
-                nc.gpsimd.dma_start(wb_sc[SCALE_ROWS + r : P : QUADRANT].bitcast(I32), rows[r].bitcast(I32))
+                nc.sync.dma_start(wb_sc[SCALE_ROWS + r : P : QUADRANT].bitcast(I32), rows[r].bitcast(I32))
 
-        load_w_scales(0, nc.gpsimd)
-        load_wb_scales()
         load_x(0)
         nc.sync.dma_start(offsets[:], offs)
-        load_x(1)
         load_x_scales()
         load_wa(0, 0)
+        load_x(1)
+        load_w_scales()
         load_wa(0, 1)
         load_wa(last, 0)
         load_w(0)
+        load_wb_scales()
         load_wa(last, 1)
         load_wb(0)
-        load_w_scales(last, nc.sync)
         load_w(last)
         load_wb(last)
 
@@ -138,7 +137,8 @@ def tile_moe_elr_s_gelu_kernel(
                 src = wa_raw[e, s, j0][:].rearrange("p j (m t) -> p m j t", t=TILES)
                 dst = wa_bf[e, s][:].rearrange("p t m j -> p m j t")[:, :, j0:j1, :]
                 share = VECTOR_SHARE[e, s, j0]
-                nc.vector.tensor_copy(dst[:, :share], src[:, :share])
+                if share:
+                    nc.vector.tensor_copy(dst[:, :share], src[:, :share])
                 nc.scalar.copy(dst[:, share:], src[:, share:])
 
         def quantize_wa(e, s, t0, t1):
@@ -171,7 +171,7 @@ def tile_moe_elr_s_gelu_kernel(
                 nc.tensor.matmul_mx(
                     out=y_out(e, u, q, HALF),
                     lhsT=w_wd[e][:, s, 2 * P * q : 2 * P * (q + 1)].bitcast(FP4X4),
-                    lhsT_scale=w_sc[e][:, s, P * q : P * (q + 1)],
+                    lhsT_scale=w_sc[:, e * PASSES + s, P * q : P * (q + 1)],
                     rhs=slot_wd[s][:, slots(e, u)].bitcast(FP8X4),
                     rhs_scale=slot_sc[s][:, slots(e, u)],
                     start=(s == 0 and q % 2 == 0 and (e == last or u == 0)),
@@ -200,10 +200,10 @@ def tile_moe_elr_s_gelu_kernel(
                     stop=(q % 2 == 1),
                 )
 
-        for s in range(PASSES):
-            nc.vector.tensor_copy(slot_wd[s][:], x_wd[s][:].bitcast(U32).indirect(offsets[:]))
+        nc.vector.tensor_copy(slot_wd[0][:], x_wd[0][:].bitcast(U32).indirect(offsets[:]))
         for s in range(PASSES):
             nc.vector.tensor_copy(slot_sc[s][:], x_sc[:, s, :].indirect(offsets[:]))
+        nc.vector.tensor_copy(slot_wd[1][:], x_wd[1][:].bitcast(U32).indirect(offsets[:]))
 
         for e in range(E):
             for s in range(PASSES):

@@ -26,10 +26,16 @@ TILES = N // P
 HALF = 128
 HALVES = C // HALF
 
-VECTOR_SHARE = {(0, 0, 0): 0, (0, 1, 0): 76, (1, 0, 0): 88, (1, 1, 0): 76}
-ROW_PIECES = {(0, 0): ((0, 4),), (0, 1): ((0, 4),), (1, 0): ((0, 4),), (1, 1): ((0, 4),)}
+VECTOR_SHARE = {(0, 0): 0, (0, 1): 76, (1, 0): 80, (1, 1): 68}
+CAST_TILES = {(0, 0): ((0, 4),), (0, 1): ((0, 4),), (1, 0): ((0, 4),), (1, 1): ((0, 2), (2, 4))}
 
 BANK_TILES = ((0, 2), (2, 4))
+
+W_SCALE_LOADS = ((0, 1), (1, 2))
+QUANT_STEP = {(0, 0): 4, (0, 1): 4, (1, 0): 4, (1, 1): 1}
+LAST_STORES = {(0, 0): ((0, 2, 0, 128),), (1, 0): ((0, 2, 128, 256),), (1, 2): ((2, 4, 0, 256),)}
+H_TAG = {0: "wa_raw10"}
+W_LOADS = {0: ((0, 1), (1, 2)), 1: ((0, 2),)}
 
 
 def tile_moe_elr_s_gelu_kernel(
@@ -41,8 +47,8 @@ def tile_moe_elr_s_gelu_kernel(
         keep = ctx.enter_context(tc.tile_pool(name="keep", bufs=1))
         psum = ctx.enter_context(tc.psum_pool(name="psum", bufs=1))
 
-        def sb(name, shape, dtype):
-            return keep.tile(shape, dtype, name=name, align_bytes=64)
+        def sb(name, shape, dtype, tag=None):
+            return keep.tile(shape, dtype, name=name, tag=tag or name, align_bytes=64)
 
         offsets = keep.tile([P, E * C // LIST_GROUP], U16, name="offsets")
 
@@ -52,31 +58,27 @@ def tile_moe_elr_s_gelu_kernel(
         nc.scalar.activation(warm_out[:], warm[:], GELU)
 
         x_sc = sb("x_sc", [P, PASSES, T], U8)
-        w_sc = sb("w_sc", [P, E * PASSES, N], U8)
+        w_sc = {e0: sb(f"w_sc{e0}", [P, (e1 - e0) * PASSES, N], U8) for e0, e1 in W_SCALE_LOADS}
         wb_sc = sb("wb_sc", [P, E, N], U8)
-        for plane in (x_sc, w_sc, wb_sc):
+        for plane in [x_sc, w_sc[0], wb_sc] + [w_sc[e0] for e0, e1 in W_SCALE_LOADS[1:]]:
             nc.vector.memset(plane[:].bitcast(I32), 0)
 
         x_wd = [sb(f"x_wd{s}", [P, T], I32) for s in range(PASSES)]
-        w_wd = [sb(f"w_wd{e}", [P, PASSES, 2 * N], U8) for e in range(E)]
+        w_wd = {(e, s0): sb(f"w_wd{e}{s0}", [P, s1 - s0, 2 * N], U8) for e in range(E) for s0, s1 in W_LOADS[e]}
         wb_wd = [sb(f"wb_wd{e}", [P, N], I32) for e in range(E)]
-        wa_raw = {
-            (e, s, j0): sb(f"wa_raw{e}{s}{j0}", [P, j1 - j0, H], F32)
-            for e in range(E)
-            for s in range(PASSES)
-            for j0, j1 in ROW_PIECES[e, s]
-        }
+        wa_raw = {(e, s): sb(f"wa_raw{e}{s}", [P, PACK, H], F32) for e in range(E) for s in range(PASSES)}
 
         def load_x(s):
             nc.sync.dma_start(x_wd[s][:], x_words[s].rearrange("p t d -> p (t d)").bitcast(I32))
 
         def load_wa(e, s):
             rows = wa[e, K_PASS * s : K_PASS * (s + 1), :].rearrange("(p j) i -> p j i", j=PACK)
-            for j0, j1 in ROW_PIECES[e, s]:
-                nc.sync.dma_start(wa_raw[e, s, j0][:], rows[:, j0:j1, :])
+            nc.sync.dma_start(wa_raw[e, s][:], rows)
 
-        def load_w(e):
-            nc.sync.dma_start(w_wd[e][:].bitcast(I32), w_words[e].rearrange("s p b -> p s b").bitcast(I32))
+        def load_w(e, piece):
+            s0, s1 = W_LOADS[e][piece]
+            rows = w_words[e, s0:s1].rearrange("s p b -> p s b")
+            nc.sync.dma_start(w_wd[e, s0][:].bitcast(I32), rows.bitcast(I32))
 
         def load_wb(e):
             nc.sync.dma_start(wb_wd[e][:], wb_words[e, 0].rearrange("p n d -> p (n d)").bitcast(I32))
@@ -86,29 +88,32 @@ def tile_moe_elr_s_gelu_kernel(
             for r in range(SCALE_ROWS):
                 nc.sync.dma_start(x_sc[r:P:QUADRANT].bitcast(I32), rows[r].bitcast(I32))
 
-        def load_w_scales():
-            rows = w_scales.rearrange("e s (q r) n -> r q (e s) n", r=SCALE_ROWS)
+        def load_w_scales(piece, queue):
+            e0, e1 = W_SCALE_LOADS[piece]
+            rows = w_scales[e0:e1].rearrange("e s (q r) n -> r q (e s) n", r=SCALE_ROWS)
             for r in range(SCALE_ROWS):
-                nc.sync.dma_start(w_sc[r:P:QUADRANT].bitcast(I32), rows[r].bitcast(I32))
+                queue.dma_start(w_sc[e0][r:P:QUADRANT].bitcast(I32), rows[r].bitcast(I32))
 
-        def load_wb_scales():
+        def load_wb_scales(queue):
             rows = wb_scales.rearrange("e s (q r) n -> r q (e s) n", r=SCALE_ROWS)
             for r in range(SCALE_ROWS):
-                nc.sync.dma_start(wb_sc[SCALE_ROWS + r : P : QUADRANT].bitcast(I32), rows[r].bitcast(I32))
+                queue.dma_start(wb_sc[SCALE_ROWS + r : P : QUADRANT].bitcast(I32), rows[r].bitcast(I32))
 
         load_x(0)
         nc.sync.dma_start(offsets[:], offs)
         load_x_scales()
         load_wa(0, 0)
         load_x(1)
-        load_w_scales()
+        load_w_scales(0, nc.sync)
         load_wa(0, 1)
         load_wa(last, 0)
-        load_w(0)
-        load_wb_scales()
+        load_w(0, 0)
+        load_wb_scales(nc.sync)
         load_wa(last, 1)
+        load_w(0, 1)
         load_wb(0)
-        load_w(last)
+        load_w_scales(1, nc.sync)
+        load_w(last, 0)
         load_wb(last)
 
         slot_wd = [sb(f"slot_wd{s}", [P, E * C], U32) for s in range(PASSES)]
@@ -123,20 +128,19 @@ def tile_moe_elr_s_gelu_kernel(
         for e in range(E):
             for u in range(HALVES):
                 h_bank[e, u] = psum.tile([P, TILES, HALF], F32, name=f"h_bank{e}{u}", tag=f"h{e}{u}")
-                h_bf[e, u] = sb(f"h_bf{e}{u}", [P, HALF, PACK], BF16)
             h_wd[e] = sb(f"h_wd{e}", [P, C], U32)
             h_sc[e] = sb(f"h_sc{e}", [P, C], U8)
-        y_last = [sb(f"y_last{u}", [P, TILES, HALF], F32) for u in range(HALVES)]
+        y_last = sb("y_last", [P, TILES, C], F32)
         out_rows = out.rearrange("(q p) j -> p q j", p=P)
 
         def slots(e, u):
             return slice(e * C + u * HALF, e * C + (u + 1) * HALF)
 
         def cast_wa(e, s):
-            for j0, j1 in ROW_PIECES[e, s]:
-                src = wa_raw[e, s, j0][:].rearrange("p j (m t) -> p m j t", t=TILES)
-                dst = wa_bf[e, s][:].rearrange("p t m j -> p m j t")[:, :, j0:j1, :]
-                share = VECTOR_SHARE[e, s, j0]
+            for t0, t1 in CAST_TILES[e, s]:
+                src = wa_raw[e, s][:].rearrange("p j (m t) -> p m j t", t=TILES)[:, :, :, t0:t1]
+                dst = wa_bf[e, s][:].rearrange("p t m j -> p m j t")[:, :, :, t0:t1]
+                share = VECTOR_SHARE[e, s]
                 if share:
                     nc.vector.tensor_copy(dst[:, :share], src[:, :share])
                 nc.scalar.copy(dst[:, share:], src[:, share:])
@@ -166,12 +170,14 @@ def tile_moe_elr_s_gelu_kernel(
                 return y_bank[0, q0][:, q - q0, u * HALF : u * HALF + width]
             return y_bank[e, u, q0][:, q - q0, :]
 
-        def w_pass(e, s, u):
-            for q in range(TILES):
+        def w_pass(e, s, u, tiles=range(TILES)):
+            s0 = max(first for first, end in W_LOADS[e] if first <= s)
+            e0 = max(first for first, end in W_SCALE_LOADS if first <= e)
+            for q in tiles:
                 nc.tensor.matmul_mx(
                     out=y_out(e, u, q, HALF),
-                    lhsT=w_wd[e][:, s, 2 * P * q : 2 * P * (q + 1)].bitcast(FP4X4),
-                    lhsT_scale=w_sc[:, e * PASSES + s, P * q : P * (q + 1)],
+                    lhsT=w_wd[e, s0][:, s - s0, 2 * P * q : 2 * P * (q + 1)].bitcast(FP4X4),
+                    lhsT_scale=w_sc[e0][:, (e - e0) * PASSES + s, P * q : P * (q + 1)],
                     rhs=slot_wd[s][:, slots(e, u)].bitcast(FP8X4),
                     rhs_scale=slot_sc[s][:, slots(e, u)],
                     start=(s == 0 and q % 2 == 0 and (e == last or u == 0)),
@@ -179,17 +185,19 @@ def tile_moe_elr_s_gelu_kernel(
                 )
 
         def gelu(e, u):
-            nc.scalar.activation(h_bf[e, u][:], h_bank[e, u][:].rearrange("p t n -> p n t"), GELU)
+            if u == 0:
+                h_bf[e] = sb(f"h_bf{e}", [P, C, PACK], BF16, tag=H_TAG.get(e))
+            nc.scalar.activation(h_bf[e][:, u * HALF : (u + 1) * HALF, :], h_bank[e, u][:].rearrange("p t n -> p n t"), GELU)
 
         def quantize_h(e, u):
             nc.vector.quantize_mx(
                 out=h_wd[e][:, u * HALF : (u + 1) * HALF].bitcast(FP8X4),
                 scales=h_sc[e][:, u * HALF : (u + 1) * HALF],
-                in_=h_bf[e, u][:].rearrange("p n t -> p (n t)"),
+                in_=h_bf[e][:, u * HALF : (u + 1) * HALF, :].rearrange("p n t -> p (n t)"),
             )
 
-        def wb_pass(e, u, width):
-            for q in range(TILES):
+        def wb_pass(e, u, width, tiles=range(TILES)):
+            for q in tiles:
                 nc.tensor.matmul_mx(
                     out=y_out(e, u, q, width),
                     lhsT=wb_wd[e][:, P * q : P * (q + 1)].bitcast(FP8X4),
@@ -208,7 +216,7 @@ def tile_moe_elr_s_gelu_kernel(
         for e in range(E):
             for s in range(PASSES):
                 cast_wa(e, s)
-                step = 1 if (e, s) == (last, PASSES - 1) else TILES
+                step = QUANT_STEP[e, s]
                 for t in range(0, TILES, step):
                     quantize_wa(e, s, t, t + step)
                 for u in range(HALVES):
@@ -221,12 +229,14 @@ def tile_moe_elr_s_gelu_kernel(
         for u in range(HALVES):
             quantize_h(0, u)
         for u in range(HALVES):
-            for s in range(PASSES):
-                w_pass(0, s, u)
-        wb_pass(0, 0, C)
-        spent = wa_bf[last, PASSES - 1]
+            w_pass(0, 0, u)
         for q0, q1 in BANK_TILES:
-            y_first = spent[:, q0:q1].rearrange("p t m j -> p t (m j)").bitcast(F32)
+            for u in range(HALVES):
+                w_pass(0, 1, u, range(q0, q1))
+            wb_pass(0, 0, C, range(q0, q1))
+        spent = sb("y_first", [P, TILES, C], F32, tag=f"wa_bf{last}{PASSES - 1}")
+        for q0, q1 in BANK_TILES:
+            y_first = spent[:, q0:q1, :]
             nc.vector.tensor_copy(y_first, y_bank[0, q0][:])
             nc.sync.dma_start(out_rows[:, q0:q1, 0:C], y_first)
 
@@ -244,8 +254,6 @@ def tile_moe_elr_s_gelu_kernel(
         for u in range(HALVES):
             for q0, q1 in BANK_TILES:
                 copy = nc.scalar.copy if q0 else nc.vector.tensor_copy
-                copy(y_last[u][:, q0:q1, :], y_bank[last, u, q0][:])
-                if u == HALVES - 1:
-                    nc.sync.dma_start(out_rows[:, q0:q1, slots(last, u)], y_last[u][:, q0:q1, :])
-            if u < HALVES - 1:
-                nc.sync.dma_start(out_rows[:, :, slots(last, u)], y_last[u][:])
+                copy(y_last[:, q0:q1, u * HALF : (u + 1) * HALF], y_bank[last, u, q0][:])
+                for a, b, c, d in LAST_STORES.get((u, q0), ()):
+                    nc.sync.dma_start(out_rows[:, a:b, last * C + c : last * C + d], y_last[:, a:b, c:d])

@@ -26,14 +26,19 @@ TILES = N // P
 HALF = 128
 HALVES = C // HALF
 
-VECTOR_SHARE = {(0, 0): 0, (0, 1): 76, (1, 0): 80, (1, 1): 68}
+VECTOR_SHARE = {(0, 0): 0, (0, 1): 76, (1, 0): 80, (1, 1): 84}
 CAST_TILES = {(0, 0): ((0, 4),), (0, 1): ((0, 4),), (1, 0): ((0, 4),), (1, 1): ((0, 2), (2, 4))}
 
 BANK_TILES = ((0, 2), (2, 4))
 
 W_SCALE_LOADS = ((0, 1), (1, 2))
-QUANT_STEP = {(0, 0): 4, (0, 1): 4, (1, 0): 4, (1, 1): 1}
-LAST_STORES = {(0, 0): ((0, 2, 0, 128),), (1, 0): ((0, 2, 128, 256),), (1, 2): ((2, 4, 0, 256),)}
+LAST_QUANT = ((0, 2), (2, 3), (3, 4))
+QUANT_TILES = {(0, 0): ((0, 4),), (0, 1): ((0, 4),), (1, 0): ((0, 4),), (1, 1): LAST_QUANT}
+LAST_STORES = {(0, 0): ((0, 2, 0, 128),), (0, 2): ((2, 4, 0, 128),), (1, 0): ((0, 2, 128, 256),), (1, 2): ((2, 4, 128, 256),)}
+FIRST_TAG = {0: None, 2: "wa_bf11"}
+FIRST_ON_SCALAR = (0,)
+LAST_ORDER = (("w", 0, 0, 4), ("w", 1, 0, 2), ("b", 0, 0, 4), ("w", 1, 2, 4), ("b", 1, 0, 4))
+WB_FIRST = 4
 H_TAG = {0: "wa_raw10"}
 W_LOADS = {0: ((0, 1), (1, 2)), 1: ((0, 2),)}
 
@@ -213,15 +218,15 @@ def tile_moe_elr_s_gelu_kernel(
             nc.vector.tensor_copy(slot_sc[s][:], x_sc[:, s, :].indirect(offsets[:]))
         nc.vector.tensor_copy(slot_wd[1][:], x_wd[1][:].bitcast(U32).indirect(offsets[:]))
 
-        for e in range(E):
-            for s in range(PASSES):
-                cast_wa(e, s)
-                step = QUANT_STEP[e, s]
-                for t in range(0, TILES, step):
-                    quantize_wa(e, s, t, t + step)
-                for u in range(HALVES):
-                    h_pass(e, s, u)
+        def prepare_wa(e, s):
+            cast_wa(e, s)
+            for t0, t1 in QUANT_TILES[e, s]:
+                quantize_wa(e, s, t0, t1)
 
+        for e, s in ((0, 0), (0, 1), (last, 0)):
+            prepare_wa(e, s)
+            for u in range(HALVES):
+                h_pass(e, s, u)
         for q0, q1 in BANK_TILES:
             y_bank[0, q0] = psum.tile([P, q1 - q0, C], F32, name=f"y_bank0{q0}", tag=f"y0{q0}")
         for u in range(HALVES):
@@ -230,15 +235,19 @@ def tile_moe_elr_s_gelu_kernel(
             quantize_h(0, u)
         for u in range(HALVES):
             w_pass(0, 0, u)
+        prepare_wa(last, 1)
         for q0, q1 in BANK_TILES:
             for u in range(HALVES):
                 w_pass(0, 1, u, range(q0, q1))
-            wb_pass(0, 0, C, range(q0, q1))
-        spent = sb("y_first", [P, TILES, C], F32, tag=f"wa_bf{last}{PASSES - 1}")
+        wb_pass(0, 0, C, range(0, WB_FIRST))
+        for u in range(HALVES):
+            h_pass(last, 1, u)
+        wb_pass(0, 0, C, range(WB_FIRST, 4))
         for q0, q1 in BANK_TILES:
-            y_first = spent[:, q0:q1, :]
-            nc.vector.tensor_copy(y_first, y_bank[0, q0][:])
-            nc.sync.dma_start(out_rows[:, q0:q1, 0:C], y_first)
+            y_first = sb(f"y_first{q0}", [P, q1 - q0, C], F32, tag=FIRST_TAG[q0])
+            copy = nc.scalar.copy if q0 in FIRST_ON_SCALAR else nc.vector.tensor_copy
+            copy(y_first[:], y_bank[0, q0][:])
+            nc.sync.dma_start(out_rows[:, q0:q1, 0:C], y_first[:])
 
         for u in range(HALVES):
             gelu(last, u)
@@ -247,10 +256,12 @@ def tile_moe_elr_s_gelu_kernel(
             for q0, q1 in BANK_TILES:
                 tag = f"h0{u}" if q0 else f"y{last}{u}"
                 y_bank[last, u, q0] = psum.tile([P, q1 - q0, HALF], F32, name=f"y_bank1{u}{q0}", tag=tag)
-            for s in range(PASSES):
-                w_pass(last, s, u)
-        for u in range(HALVES):
-            wb_pass(last, u, HALF)
+        for kind, u, q0, q1 in LAST_ORDER:
+            if kind == "w":
+                for s in range(PASSES):
+                    w_pass(last, s, u, range(q0, q1))
+            else:
+                wb_pass(last, u, HALF, range(q0, q1))
         for u in range(HALVES):
             for q0, q1 in BANK_TILES:
                 copy = nc.scalar.copy if q0 else nc.vector.tensor_copy

@@ -26,7 +26,7 @@ TILES = N // P
 HALF = 128
 HALVES = C // HALF
 
-VECTOR_SHARE = {(0, 0): 0, (0, 1): 76, (1, 0): 80, (1, 1): 84}
+VECTOR_SHARE = {(0, 0): 0, (0, 1): 68, (1, 0): 72, (1, 1): 68}
 CAST_TILES = {(0, 0): ((0, 4),), (0, 1): ((0, 4),), (1, 0): ((0, 4),), (1, 1): ((0, 2), (2, 4))}
 
 BANK_TILES = ((0, 2), (2, 4))
@@ -39,6 +39,10 @@ FIRST_TAG = {0: None, 2: "wa_bf11"}
 FIRST_ON_SCALAR = (0,)
 LAST_ORDER = (("w", 0, 0, 4), ("w", 1, 0, 2), ("b", 0, 0, 4), ("w", 1, 2, 4), ("b", 1, 0, 4))
 WB_FIRST = 4
+LAST_TILE_ORDER = (2, 0, 1, 3)
+LAST_BANKS = ((0, 1), (1, 2), (2, 4))
+LAST_BANK_TAGS = (("y10", "h00", "y11"), ("h01", "y00", "y02"))
+LAST_ON_SCALAR = (0, 2)
 H_TAG = {0: "wa_raw10"}
 W_LOADS = {0: ((0, 1), (1, 2)), 1: ((0, 2),)}
 
@@ -157,8 +161,8 @@ def tile_moe_elr_s_gelu_kernel(
                 in_=wa_bf[e, s][:, t0:t1, :, :].rearrange("p t m j -> p (t m j)"),
             )
 
-        def h_pass(e, s, u):
-            for t in range(TILES):
+        def h_pass(e, s, u, order=range(TILES)):
+            for t in order:
                 nc.tensor.matmul_mx(
                     out=h_bank[e, u][:, t, :],
                     lhsT=wa_wd[e, s][:, t, :].bitcast(FP8X4),
@@ -169,8 +173,11 @@ def tile_moe_elr_s_gelu_kernel(
                     stop=(s == PASSES - 1 and t == TILES - 1),
                 )
 
+        def banks(e):
+            return LAST_BANKS if e == last else BANK_TILES
+
         def y_out(e, u, q, width):
-            q0 = q - q % 2
+            q0 = max(a for a, b in banks(e) if a <= q)
             if e == 0:
                 return y_bank[0, q0][:, q - q0, u * HALF : u * HALF + width]
             return y_bank[e, u, q0][:, q - q0, :]
@@ -185,7 +192,7 @@ def tile_moe_elr_s_gelu_kernel(
                     lhsT_scale=w_sc[e0][:, (e - e0) * PASSES + s, P * q : P * (q + 1)],
                     rhs=slot_wd[s][:, slots(e, u)].bitcast(FP8X4),
                     rhs_scale=slot_sc[s][:, slots(e, u)],
-                    start=(s == 0 and q % 2 == 0 and (e == last or u == 0)),
+                    start=(s == 0 and q in [a for a, b in banks(e)] and (e == last or u == 0)),
                     stop=False,
                 )
 
@@ -210,7 +217,7 @@ def tile_moe_elr_s_gelu_kernel(
                     rhs=h_wd[e][:, u * HALF : u * HALF + width].bitcast(FP8X4),
                     rhs_scale=h_sc[e][:, u * HALF : u * HALF + width],
                     start=False,
-                    stop=(q % 2 == 1),
+                    stop=(q + 1 in [b for a, b in banks(e)]),
                 )
 
         nc.vector.tensor_copy(slot_wd[0][:], x_wd[0][:].bitcast(U32).indirect(offsets[:]))
@@ -241,7 +248,7 @@ def tile_moe_elr_s_gelu_kernel(
                 w_pass(0, 1, u, range(q0, q1))
         wb_pass(0, 0, C, range(0, WB_FIRST))
         for u in range(HALVES):
-            h_pass(last, 1, u)
+            h_pass(last, 1, u, LAST_TILE_ORDER)
         wb_pass(0, 0, C, range(WB_FIRST, 4))
         for q0, q1 in BANK_TILES:
             y_first = sb(f"y_first{q0}", [P, q1 - q0, C], F32, tag=FIRST_TAG[q0])
@@ -253,8 +260,8 @@ def tile_moe_elr_s_gelu_kernel(
             gelu(last, u)
             quantize_h(last, u)
         for u in range(HALVES):
-            for q0, q1 in BANK_TILES:
-                tag = f"h0{u}" if q0 else f"y{last}{u}"
+            for k, (q0, q1) in enumerate(LAST_BANKS):
+                tag = LAST_BANK_TAGS[u][k]
                 y_bank[last, u, q0] = psum.tile([P, q1 - q0, HALF], F32, name=f"y_bank1{u}{q0}", tag=tag)
         for kind, u, q0, q1 in LAST_ORDER:
             if kind == "w":
@@ -263,8 +270,7 @@ def tile_moe_elr_s_gelu_kernel(
             else:
                 wb_pass(last, u, HALF, range(q0, q1))
         for u in range(HALVES):
-            for q0, q1 in BANK_TILES:
-                copy = nc.scalar.copy if q0 else nc.vector.tensor_copy
+            for k, (q0, q1) in enumerate(LAST_BANKS):
+                copy = nc.scalar.copy if k in LAST_ON_SCALAR else nc.vector.tensor_copy
                 copy(y_last[:, q0:q1, u * HALF : (u + 1) * HALF], y_bank[last, u, q0][:])
-                for a, b, c, d in LAST_STORES.get((u, q0), ()):
-                    nc.sync.dma_start(out_rows[:, a:b, last * C + c : last * C + d], y_last[:, a:b, c:d])
+                nc.sync.dma_start(out_rows[:, q0:q1, slots(last, u)], y_last[:, q0:q1, u * HALF : (u + 1) * HALF])

@@ -26,7 +26,7 @@ TILES = N // P
 HALF = 128
 HALVES = C // HALF
 
-VECTOR_SHARE = {(0, 0): 0, (0, 1): 68, (1, 0): 72, (1, 1): 68}
+VECTOR_SHARE = {(0, 0): 0, (0, 1): 76, (1, 0): 80, (1, 1): 84}
 CAST_TILES = {(0, 0): ((0, 4),), (0, 1): ((0, 4),), (1, 0): ((0, 4),), (1, 1): ((0, 2), (2, 4))}
 
 BANK_TILES = ((0, 2), (2, 4))
@@ -39,7 +39,7 @@ FIRST_TAG = {0: None, 2: "wa_bf11"}
 FIRST_ON_SCALAR = (0,)
 LAST_ORDER = (("w", 0, 0, 4), ("w", 1, 0, 2), ("b", 0, 0, 4), ("w", 1, 2, 4), ("b", 1, 0, 4))
 WB_FIRST = 4
-LAST_TILE_ORDER = (2, 0, 1, 3)
+LAST_TILE_ORDER = (0, 1, 2, 3)
 LAST_BANKS = ((0, 1), (1, 2), (2, 4))
 LAST_BANK_TAGS = (("y10", "h00", "y11"), ("h01", "y00", "y02"))
 LAST_ON_SCALAR = (0, 2)

@@ -25,33 +25,23 @@ LIST_GROUP = 16
 TILES = N // P
 HALF = 128
 HALVES = C // HALF
+FIRST, LAST = 0, 1
 
-VECTOR_SHARE = {(0, 0): 0, (0, 1): 76, (1, 0): 80, (1, 1): 84}
-CAST_TILES = {(0, 0): ((0, 4),), (0, 1): ((0, 4),), (1, 0): ((0, 4),), (1, 1): ((0, 2), (2, 4))}
+VECTOR_SHARE = {(FIRST, 0): 0, (FIRST, 1): 76, (LAST, 0): 80, (LAST, 1): 84}
 
-BANK_TILES = ((0, 2), (2, 4))
+WHOLE_PASS = ((0, TILES),)
+FINAL_CASTS = ((0, 2), (2, TILES))
+FINAL_QUANTIZES = ((0, 2), (2, 3), (3, TILES))
 
-W_SCALE_LOADS = ((0, 1), (1, 2))
-LAST_QUANT = ((0, 2), (2, 3), (3, 4))
-QUANT_TILES = {(0, 0): ((0, 4),), (0, 1): ((0, 4),), (1, 0): ((0, 4),), (1, 1): LAST_QUANT}
-LAST_STORES = {(0, 0): ((0, 2, 0, 128),), (0, 2): ((2, 4, 0, 128),), (1, 0): ((0, 2, 128, 256),), (1, 2): ((2, 4, 128, 256),)}
-FIRST_TAG = {0: None, 2: "wa_bf11"}
-FIRST_ON_SCALAR = (0,)
-LAST_ORDER = (("w", 0, 0, 4), ("w", 1, 0, 2), ("b", 0, 0, 4), ("w", 1, 2, 4), ("b", 1, 0, 4))
-WB_FIRST = 4
-LAST_TILE_ORDER = (0, 1, 2, 3)
-LAST_BANKS = ((0, 1), (1, 2), (2, 4))
+BANKS = {FIRST: ((0, 2), (2, TILES)), LAST: ((0, 1), (1, 2), (2, TILES))}
 LAST_BANK_TAGS = (("y10", "h00", "y11"), ("h01", "y00", "y02"))
-LAST_ON_SCALAR = (0, 2)
-H_TAG = {0: "wa_raw10"}
-W_LOADS = {0: ((0, 1), (1, 2)), 1: ((0, 2),)}
+W_LOADS = {FIRST: ((0, 1), (1, PASSES)), LAST: ((0, PASSES),)}
 
 
 def tile_moe_elr_s_gelu_kernel(
     tc, x_words, x_scales, w_words, w_scales, wa, wb_words, wb_scales, offs, out
 ):
     nc = tc.nc
-    last = E - 1
     with ExitStack() as ctx:
         keep = ctx.enter_context(tc.tile_pool(name="keep", bufs=1))
         psum = ctx.enter_context(tc.psum_pool(name="psum", bufs=1))
@@ -67,10 +57,10 @@ def tile_moe_elr_s_gelu_kernel(
         nc.scalar.activation(warm_out[:], warm[:], GELU)
 
         x_sc = sb("x_sc", [P, PASSES, T], U8)
-        w_sc = {e0: sb(f"w_sc{e0}", [P, (e1 - e0) * PASSES, N], U8) for e0, e1 in W_SCALE_LOADS}
+        w_sc = [sb(f"w_sc{e}", [P, PASSES, N], U8) for e in range(E)]
         wb_sc = sb("wb_sc", [P, E, N], U8)
-        for plane in [x_sc, w_sc[0], wb_sc] + [w_sc[e0] for e0, e1 in W_SCALE_LOADS[1:]]:
-            nc.vector.memset(plane[:].bitcast(I32), 0)
+        for scale_tile in (x_sc, w_sc[FIRST], wb_sc, w_sc[LAST]):
+            nc.vector.memset(scale_tile[:].bitcast(I32), 0)
 
         x_wd = [sb(f"x_wd{s}", [P, T], I32) for s in range(PASSES)]
         w_wd = {(e, s0): sb(f"w_wd{e}{s0}", [P, s1 - s0, 2 * N], U8) for e in range(E) for s0, s1 in W_LOADS[e]}
@@ -84,46 +74,36 @@ def tile_moe_elr_s_gelu_kernel(
             rows = wa[e, K_PASS * s : K_PASS * (s + 1), :].rearrange("(p j) i -> p j i", j=PACK)
             nc.sync.dma_start(wa_raw[e, s][:], rows)
 
-        def load_w(e, piece):
-            s0, s1 = W_LOADS[e][piece]
+        def load_w(e, s0, s1):
             rows = w_words[e, s0:s1].rearrange("s p b -> p s b")
             nc.sync.dma_start(w_wd[e, s0][:].bitcast(I32), rows.bitcast(I32))
 
         def load_wb(e):
             nc.sync.dma_start(wb_wd[e][:], wb_words[e, 0].rearrange("p n d -> p (n d)").bitcast(I32))
 
-        def load_x_scales():
-            rows = x_scales.rearrange("s (q r) t -> r q s t", r=SCALE_ROWS)
+        def load_scales(scale_tile, first, rows):
             for r in range(SCALE_ROWS):
-                nc.sync.dma_start(x_sc[r:P:QUADRANT].bitcast(I32), rows[r].bitcast(I32))
+                nc.sync.dma_start(scale_tile[first + r : P : QUADRANT].bitcast(I32), rows[r].bitcast(I32))
 
-        def load_w_scales(piece, queue):
-            e0, e1 = W_SCALE_LOADS[piece]
-            rows = w_scales[e0:e1].rearrange("e s (q r) n -> r q (e s) n", r=SCALE_ROWS)
-            for r in range(SCALE_ROWS):
-                queue.dma_start(w_sc[e0][r:P:QUADRANT].bitcast(I32), rows[r].bitcast(I32))
-
-        def load_wb_scales(queue):
-            rows = wb_scales.rearrange("e s (q r) n -> r q (e s) n", r=SCALE_ROWS)
-            for r in range(SCALE_ROWS):
-                queue.dma_start(wb_sc[SCALE_ROWS + r : P : QUADRANT].bitcast(I32), rows[r].bitcast(I32))
+        def load_w_scales(e):
+            load_scales(w_sc[e], 0, w_scales[e : e + 1].rearrange("e s (q r) n -> r q (e s) n", r=SCALE_ROWS))
 
         load_x(0)
         nc.sync.dma_start(offsets[:], offs)
-        load_x_scales()
-        load_wa(0, 0)
+        load_scales(x_sc, 0, x_scales.rearrange("s (q r) t -> r q s t", r=SCALE_ROWS))
+        load_wa(FIRST, 0)
         load_x(1)
-        load_w_scales(0, nc.sync)
-        load_wa(0, 1)
-        load_wa(last, 0)
-        load_w(0, 0)
-        load_wb_scales(nc.sync)
-        load_wa(last, 1)
-        load_w(0, 1)
-        load_wb(0)
-        load_w_scales(1, nc.sync)
-        load_w(last, 0)
-        load_wb(last)
+        load_w_scales(FIRST)
+        load_wa(FIRST, 1)
+        load_wa(LAST, 0)
+        load_w(FIRST, 0, 1)
+        load_scales(wb_sc, SCALE_ROWS, wb_scales.rearrange("e s (q r) n -> r q (e s) n", r=SCALE_ROWS))
+        load_wa(LAST, 1)
+        load_w(FIRST, 1, PASSES)
+        load_wb(FIRST)
+        load_w_scales(LAST)
+        load_w(LAST, 0, PASSES)
+        load_wb(LAST)
 
         slot_wd = [sb(f"slot_wd{s}", [P, E * C], U32) for s in range(PASSES)]
         slot_sc = [sb(f"slot_sc{s}", [P, E * C], U8) for s in range(PASSES)]
@@ -142,74 +122,72 @@ def tile_moe_elr_s_gelu_kernel(
         y_last = sb("y_last", [P, TILES, C], F32)
         out_rows = out.rearrange("(q p) j -> p q j", p=P)
 
+        def half(u):
+            return slice(u * HALF, (u + 1) * HALF)
+
         def slots(e, u):
             return slice(e * C + u * HALF, e * C + (u + 1) * HALF)
 
-        def cast_wa(e, s):
-            for t0, t1 in CAST_TILES[e, s]:
+        def prepare_wa(e, s, casts, quantizes):
+            share = VECTOR_SHARE[e, s]
+            for t0, t1 in casts:
                 src = wa_raw[e, s][:].rearrange("p j (m t) -> p m j t", t=TILES)[:, :, :, t0:t1]
                 dst = wa_bf[e, s][:].rearrange("p t m j -> p m j t")[:, :, :, t0:t1]
-                share = VECTOR_SHARE[e, s]
                 if share:
                     nc.vector.tensor_copy(dst[:, :share], src[:, :share])
                 nc.scalar.copy(dst[:, share:], src[:, share:])
-
-        def quantize_wa(e, s, t0, t1):
-            nc.vector.quantize_mx(
-                out=wa_wd[e, s][:, t0:t1, :].rearrange("p t m -> p (t m)").bitcast(FP8X4),
-                scales=wa_sc[e, s][:, t0:t1, :].rearrange("p t m -> p (t m)"),
-                in_=wa_bf[e, s][:, t0:t1, :, :].rearrange("p t m j -> p (t m j)"),
-            )
-
-        def h_pass(e, s, u, order=range(TILES)):
-            for t in order:
-                nc.tensor.matmul_mx(
-                    out=h_bank[e, u][:, t, :],
-                    lhsT=wa_wd[e, s][:, t, :].bitcast(FP8X4),
-                    lhsT_scale=wa_sc[e, s][:, t, :],
-                    rhs=slot_wd[s][:, slots(e, u)].bitcast(FP8X4),
-                    rhs_scale=slot_sc[s][:, slots(e, u)],
-                    start=(s == 0 and t == 0),
-                    stop=(s == PASSES - 1 and t == TILES - 1),
+            for t0, t1 in quantizes:
+                nc.vector.quantize_mx(
+                    out=wa_wd[e, s][:, t0:t1, :].rearrange("p t m -> p (t m)").bitcast(FP8X4),
+                    scales=wa_sc[e, s][:, t0:t1, :].rearrange("p t m -> p (t m)"),
+                    in_=wa_bf[e, s][:, t0:t1, :, :].rearrange("p t m j -> p (t m j)"),
                 )
 
-        def banks(e):
-            return LAST_BANKS if e == last else BANK_TILES
+        def h_pass(e, s):
+            for u in range(HALVES):
+                for t in range(TILES):
+                    nc.tensor.matmul_mx(
+                        out=h_bank[e, u][:, t, :],
+                        lhsT=wa_wd[e, s][:, t, :].bitcast(FP8X4),
+                        lhsT_scale=wa_sc[e, s][:, t, :],
+                        rhs=slot_wd[s][:, slots(e, u)].bitcast(FP8X4),
+                        rhs_scale=slot_sc[s][:, slots(e, u)],
+                        start=(s == 0 and t == 0),
+                        stop=(s == PASSES - 1 and t == TILES - 1),
+                    )
 
         def y_out(e, u, q, width):
-            q0 = max(a for a, b in banks(e) if a <= q)
-            if e == 0:
-                return y_bank[0, q0][:, q - q0, u * HALF : u * HALF + width]
-            return y_bank[e, u, q0][:, q - q0, :]
+            q0 = max(first for first, end in BANKS[e] if first <= q)
+            if e == FIRST:
+                return y_bank[FIRST, q0][:, q - q0, u * HALF : u * HALF + width]
+            return y_bank[LAST, u, q0][:, q - q0, :]
 
-        def w_pass(e, s, u, tiles=range(TILES)):
+        def w_pass(e, s, u, q0, q1):
             s0 = max(first for first, end in W_LOADS[e] if first <= s)
-            e0 = max(first for first, end in W_SCALE_LOADS if first <= e)
-            for q in tiles:
+            for q in range(q0, q1):
+                opens_bank = q in [first for first, end in BANKS[e]] and (e == LAST or u == 0)
                 nc.tensor.matmul_mx(
                     out=y_out(e, u, q, HALF),
                     lhsT=w_wd[e, s0][:, s - s0, 2 * P * q : 2 * P * (q + 1)].bitcast(FP4X4),
-                    lhsT_scale=w_sc[e0][:, (e - e0) * PASSES + s, P * q : P * (q + 1)],
+                    lhsT_scale=w_sc[e][:, s, P * q : P * (q + 1)],
                     rhs=slot_wd[s][:, slots(e, u)].bitcast(FP8X4),
                     rhs_scale=slot_sc[s][:, slots(e, u)],
-                    start=(s == 0 and q in [a for a, b in banks(e)] and (e == last or u == 0)),
+                    start=(s == 0 and opens_bank),
                     stop=False,
                 )
 
         def gelu(e, u):
-            if u == 0:
-                h_bf[e] = sb(f"h_bf{e}", [P, C, PACK], BF16, tag=H_TAG.get(e))
-            nc.scalar.activation(h_bf[e][:, u * HALF : (u + 1) * HALF, :], h_bank[e, u][:].rearrange("p t n -> p n t"), GELU)
+            nc.scalar.activation(h_bf[e][:, half(u), :], h_bank[e, u][:].rearrange("p t n -> p n t"), GELU)
 
         def quantize_h(e, u):
             nc.vector.quantize_mx(
-                out=h_wd[e][:, u * HALF : (u + 1) * HALF].bitcast(FP8X4),
-                scales=h_sc[e][:, u * HALF : (u + 1) * HALF],
-                in_=h_bf[e][:, u * HALF : (u + 1) * HALF, :].rearrange("p n t -> p (n t)"),
+                out=h_wd[e][:, half(u)].bitcast(FP8X4),
+                scales=h_sc[e][:, half(u)],
+                in_=h_bf[e][:, half(u), :].rearrange("p n t -> p (n t)"),
             )
 
-        def wb_pass(e, u, width, tiles=range(TILES)):
-            for q in tiles:
+        def wb_pass(e, u, width):
+            for q in range(TILES):
                 nc.tensor.matmul_mx(
                     out=y_out(e, u, q, width),
                     lhsT=wb_wd[e][:, P * q : P * (q + 1)].bitcast(FP8X4),
@@ -217,7 +195,7 @@ def tile_moe_elr_s_gelu_kernel(
                     rhs=h_wd[e][:, u * HALF : u * HALF + width].bitcast(FP8X4),
                     rhs_scale=h_sc[e][:, u * HALF : u * HALF + width],
                     start=False,
-                    stop=(q + 1 in [b for a, b in banks(e)]),
+                    stop=(q + 1 in [end for first, end in BANKS[e]]),
                 )
 
         nc.vector.tensor_copy(slot_wd[0][:], x_wd[0][:].bitcast(U32).indirect(offsets[:]))
@@ -225,52 +203,48 @@ def tile_moe_elr_s_gelu_kernel(
             nc.vector.tensor_copy(slot_sc[s][:], x_sc[:, s, :].indirect(offsets[:]))
         nc.vector.tensor_copy(slot_wd[1][:], x_wd[1][:].bitcast(U32).indirect(offsets[:]))
 
-        def prepare_wa(e, s):
-            cast_wa(e, s)
-            for t0, t1 in QUANT_TILES[e, s]:
-                quantize_wa(e, s, t0, t1)
+        for e, s in ((FIRST, 0), (FIRST, 1), (LAST, 0)):
+            prepare_wa(e, s, WHOLE_PASS, WHOLE_PASS)
+            h_pass(e, s)
+        for q0, q1 in BANKS[FIRST]:
+            y_bank[FIRST, q0] = psum.tile([P, q1 - q0, C], F32, name=f"y_bank0{q0}", tag=f"y0{q0}")
+        h_bf[FIRST] = sb("h_bf0", [P, C, PACK], BF16, tag="wa_raw10")
+        for u in range(HALVES):
+            gelu(FIRST, u)
+        for u in range(HALVES):
+            quantize_h(FIRST, u)
+        for u in range(HALVES):
+            w_pass(FIRST, 0, u, 0, TILES)
 
-        for e, s in ((0, 0), (0, 1), (last, 0)):
-            prepare_wa(e, s)
+        prepare_wa(LAST, 1, FINAL_CASTS, FINAL_QUANTIZES)
+        for q0, q1 in BANKS[FIRST]:
             for u in range(HALVES):
-                h_pass(e, s, u)
-        for q0, q1 in BANK_TILES:
-            y_bank[0, q0] = psum.tile([P, q1 - q0, C], F32, name=f"y_bank0{q0}", tag=f"y0{q0}")
-        for u in range(HALVES):
-            gelu(0, u)
-        for u in range(HALVES):
-            quantize_h(0, u)
-        for u in range(HALVES):
-            w_pass(0, 0, u)
-        prepare_wa(last, 1)
-        for q0, q1 in BANK_TILES:
-            for u in range(HALVES):
-                w_pass(0, 1, u, range(q0, q1))
-        wb_pass(0, 0, C, range(0, WB_FIRST))
-        for u in range(HALVES):
-            h_pass(last, 1, u, LAST_TILE_ORDER)
-        wb_pass(0, 0, C, range(WB_FIRST, 4))
-        for q0, q1 in BANK_TILES:
-            y_first = sb(f"y_first{q0}", [P, q1 - q0, C], F32, tag=FIRST_TAG[q0])
-            copy = nc.scalar.copy if q0 in FIRST_ON_SCALAR else nc.vector.tensor_copy
-            copy(y_first[:], y_bank[0, q0][:])
+                w_pass(FIRST, 1, u, q0, q1)
+        wb_pass(FIRST, 0, C)
+        h_pass(LAST, 1)
+
+        for (q0, q1), copy, tag in zip(BANKS[FIRST], (nc.scalar.copy, nc.vector.tensor_copy), (None, "wa_bf11")):
+            y_first = sb(f"y_first{q0}", [P, q1 - q0, C], F32, tag=tag)
+            copy(y_first[:], y_bank[FIRST, q0][:])
             nc.sync.dma_start(out_rows[:, q0:q1, 0:C], y_first[:])
 
+        h_bf[LAST] = sb("h_bf1", [P, C, PACK], BF16)
         for u in range(HALVES):
-            gelu(last, u)
-            quantize_h(last, u)
+            gelu(LAST, u)
+            quantize_h(LAST, u)
         for u in range(HALVES):
-            for k, (q0, q1) in enumerate(LAST_BANKS):
-                tag = LAST_BANK_TAGS[u][k]
-                y_bank[last, u, q0] = psum.tile([P, q1 - q0, HALF], F32, name=f"y_bank1{u}{q0}", tag=tag)
-        for kind, u, q0, q1 in LAST_ORDER:
-            if kind == "w":
-                for s in range(PASSES):
-                    w_pass(last, s, u, range(q0, q1))
-            else:
-                wb_pass(last, u, HALF, range(q0, q1))
+            for (q0, q1), tag in zip(BANKS[LAST], LAST_BANK_TAGS[u]):
+                y_bank[LAST, u, q0] = psum.tile([P, q1 - q0, HALF], F32, name=f"y_bank1{u}{q0}", tag=tag)
+        for s in range(PASSES):
+            w_pass(LAST, s, 0, 0, TILES)
+        for s in range(PASSES):
+            w_pass(LAST, s, 1, 0, TILES // 2)
+        wb_pass(LAST, 0, HALF)
+        for s in range(PASSES):
+            w_pass(LAST, s, 1, TILES // 2, TILES)
+        wb_pass(LAST, 1, HALF)
+
         for u in range(HALVES):
-            for k, (q0, q1) in enumerate(LAST_BANKS):
-                copy = nc.scalar.copy if k in LAST_ON_SCALAR else nc.vector.tensor_copy
-                copy(y_last[:, q0:q1, u * HALF : (u + 1) * HALF], y_bank[last, u, q0][:])
-                nc.sync.dma_start(out_rows[:, q0:q1, slots(last, u)], y_last[:, q0:q1, u * HALF : (u + 1) * HALF])
+            for (q0, q1), copy in zip(BANKS[LAST], (nc.vector.tensor_copy, nc.scalar.copy, nc.vector.tensor_copy)):
+                copy(y_last[:, q0:q1, half(u)], y_bank[LAST, u, q0][:])
+                nc.sync.dma_start(out_rows[:, q0:q1, slots(LAST, u)], y_last[:, q0:q1, half(u)])

@@ -21,6 +21,7 @@ K_PASS = P * PACK
 PASSES = K // K_PASS
 QUADRANT = 32
 SCALE_ROWS = 4
+SPREAD = 8
 LIST_GROUP = 16
 TILES = N // P
 HALF = 128
@@ -89,12 +90,26 @@ def tile_moe_elr_s_gelu_kernel(
             load_scales(w_sc[e], 0, w_scales[e : e + 1].rearrange("e s (q r) n -> r q (e s) n", r=SCALE_ROWS))
 
         load_x(0)
+        nc.sync.dma_start(x_sc[0:P:SPREAD].bitcast(I32), x_scales.rearrange("s b t -> b s t").bitcast(I32))
         nc.sync.dma_start(offsets[:], offs)
-        load_scales(x_sc, 0, x_scales.rearrange("s (q r) t -> r q s t", r=SCALE_ROWS))
         load_wa(FIRST, 0)
         load_x(1)
         load_w_scales(FIRST)
         load_wa(FIRST, 1)
+
+        slot_wd = [sb(f"slot_wd{s}", [P, E * C], U32, tag=tag) for s, tag in enumerate(("x_sc", None))]
+        spread_sc = sb("spread_sc", [P, PASSES, E * C], U8)
+        slot_sc = sb("slot_sc", [P, PASSES, E * C], U8)
+        for s in range(PASSES):
+            nc.vector.tensor_copy(spread_sc[:, s, :], x_sc[:, s, :].indirect(offsets[:]))
+        spread_rows = spread_sc[:].rearrange("p s c -> p (s c)").bitcast(I32)
+        slot_rows = slot_sc[:].rearrange("p s c -> p (s c)").bitcast(I32)
+        nc.vector.tensor_copy(slot_rows, spread_rows)
+        for r in range(1, SCALE_ROWS):
+            nc.sync.dma_start(slot_rows[r:P:QUADRANT], spread_rows[SPREAD * r : P : QUADRANT])
+        nc.vector.tensor_copy(slot_wd[0][:], x_wd[0][:].bitcast(U32).indirect(offsets[:]))
+        nc.vector.tensor_copy(slot_wd[1][:], x_wd[1][:].bitcast(U32).indirect(offsets[:]))
+
         load_wa(LAST, 0)
         load_w(FIRST, 0, 1)
         load_scales(wb_sc, SCALE_ROWS, wb_scales.rearrange("e s (q r) n -> r q (e s) n", r=SCALE_ROWS))
@@ -105,8 +120,6 @@ def tile_moe_elr_s_gelu_kernel(
         load_w(LAST, 0, PASSES)
         load_wb(LAST)
 
-        slot_wd = [sb(f"slot_wd{s}", [P, E * C], U32) for s in range(PASSES)]
-        slot_sc = [sb(f"slot_sc{s}", [P, E * C], U8) for s in range(PASSES)]
         wa_bf, wa_wd, wa_sc = {}, {}, {}
         for e in range(E):
             for s in range(PASSES):
@@ -151,7 +164,7 @@ def tile_moe_elr_s_gelu_kernel(
                         lhsT=wa_wd[e, s][:, t, :].bitcast(FP8X4),
                         lhsT_scale=wa_sc[e, s][:, t, :],
                         rhs=slot_wd[s][:, slots(e, u)].bitcast(FP8X4),
-                        rhs_scale=slot_sc[s][:, slots(e, u)],
+                        rhs_scale=slot_sc[:, s, slots(e, u)],
                         start=(s == 0 and t == 0),
                         stop=(s == PASSES - 1 and t == TILES - 1),
                     )
@@ -171,7 +184,7 @@ def tile_moe_elr_s_gelu_kernel(
                     lhsT=w_wd[e, s0][:, s - s0, 2 * P * q : 2 * P * (q + 1)].bitcast(FP4X4),
                     lhsT_scale=w_sc[e][:, s, P * q : P * (q + 1)],
                     rhs=slot_wd[s][:, slots(e, u)].bitcast(FP8X4),
-                    rhs_scale=slot_sc[s][:, slots(e, u)],
+                    rhs_scale=slot_sc[:, s, slots(e, u)],
                     start=(s == 0 and opens_bank),
                     stop=False,
                 )
@@ -197,11 +210,6 @@ def tile_moe_elr_s_gelu_kernel(
                     start=False,
                     stop=(q + 1 in [end for first, end in BANKS[e]]),
                 )
-
-        nc.vector.tensor_copy(slot_wd[0][:], x_wd[0][:].bitcast(U32).indirect(offsets[:]))
-        for s in range(PASSES):
-            nc.vector.tensor_copy(slot_sc[s][:], x_sc[:, s, :].indirect(offsets[:]))
-        nc.vector.tensor_copy(slot_wd[1][:], x_wd[1][:].bitcast(U32).indirect(offsets[:]))
 
         for e, s in ((FIRST, 0), (FIRST, 1), (LAST, 0)):
             prepare_wa(e, s, WHOLE_PASS, WHOLE_PASS)

@@ -22,6 +22,9 @@ PASSES = K // K_PASS
 QUADRANT = 32
 SCALE_ROWS = 4
 SPREAD = 8
+BS_SPLIT = 0
+SQ = False
+HELD = 1
 LIST_GROUP = 16
 TILES = N // P
 HALF = 128
@@ -86,6 +89,10 @@ def tile_moe_elr_s_gelu_kernel(
             for r in range(SCALE_ROWS):
                 nc.sync.dma_start(scale_tile[first + r : P : QUADRANT].bitcast(I32), rows[r].bitcast(I32))
 
+        def load_wb_scales(e0, e1):
+            rows = wb_scales[e0:e1].rearrange("e s (q r) n -> r q (e s) n", r=SCALE_ROWS)
+            load_scales(wb_sc[:, e0:e1, :], SCALE_ROWS, rows)
+
         def load_w_scales(e):
             load_scales(w_sc[e], 0, w_scales[e : e + 1].rearrange("e s (q r) n -> r q (e s) n", r=SCALE_ROWS))
 
@@ -112,13 +119,17 @@ def tile_moe_elr_s_gelu_kernel(
 
         load_wa(LAST, 0)
         load_w(FIRST, 0, 1)
-        load_scales(wb_sc, SCALE_ROWS, wb_scales.rearrange("e s (q r) n -> r q (e s) n", r=SCALE_ROWS))
+        load_wb_scales(0, 1 if BS_SPLIT else 2)
         load_wa(LAST, 1)
         load_w(FIRST, 1, PASSES)
         load_wb(FIRST)
         load_w_scales(LAST)
         load_w(LAST, 0, PASSES)
+        if BS_SPLIT == 1:
+            load_wb_scales(1, 2)
         load_wb(LAST)
+        if BS_SPLIT == 2:
+            load_wb_scales(1, 2)
 
         wa_bf, wa_wd, wa_sc = {}, {}, {}
         for e in range(E):
@@ -253,6 +264,13 @@ def tile_moe_elr_s_gelu_kernel(
         wb_pass(LAST, 1, HALF)
 
         for u in range(HALVES):
-            for (q0, q1), copy in zip(BANKS[LAST], (nc.vector.tensor_copy, nc.scalar.copy, nc.vector.tensor_copy)):
+            copies = (nc.vector.tensor_copy, nc.scalar.copy, nc.vector.tensor_copy)
+            for (q0, q1), copy, queue in zip(BANKS[LAST], copies, (nc.sync, nc.scalar if SQ else nc.sync, nc.sync)):
                 copy(y_last[:, q0:q1, half(u)], y_bank[LAST, u, q0][:])
-                nc.sync.dma_start(out_rows[:, q0:q1, slots(LAST, u)], y_last[:, q0:q1, half(u)])
+                q1 = min(q1, TILES - HELD)
+                if q0 < q1:
+                    queue.dma_start(out_rows[:, q0:q1, slots(LAST, u)], y_last[:, q0:q1, half(u)])
+        if HELD:
+            (nc.scalar if SQ else nc.sync).dma_start(
+                out_rows[:, TILES - HELD :, LAST * C : (LAST + 1) * C], y_last[:, TILES - HELD :, :]
+            )

@@ -22,8 +22,6 @@ PASSES = K // K_PASS
 QUADRANT = 32
 SCALE_ROWS = 4
 SPREAD = 8
-BS_SPLIT = 0
-SQ = False
 HELD = 1
 LIST_GROUP = 16
 TILES = N // P
@@ -51,7 +49,7 @@ def tile_moe_elr_s_gelu_kernel(
         psum = ctx.enter_context(tc.psum_pool(name="psum", bufs=1))
 
         def sb(name, shape, dtype, tag=None):
-            return keep.tile(shape, dtype, name=name, tag=tag or name, align_bytes=64)
+            return keep.tile(shape, dtype, name=name, tag=tag or name, align_bytes=256)
 
         offsets = keep.tile([P, E * C // LIST_GROUP], U16, name="offsets")
 
@@ -119,17 +117,13 @@ def tile_moe_elr_s_gelu_kernel(
 
         load_wa(LAST, 0)
         load_w(FIRST, 0, 1)
-        load_wb_scales(0, 1 if BS_SPLIT else 2)
+        load_wb_scales(0, E)
         load_wa(LAST, 1)
         load_w(FIRST, 1, PASSES)
         load_wb(FIRST)
         load_w_scales(LAST)
         load_w(LAST, 0, PASSES)
-        if BS_SPLIT == 1:
-            load_wb_scales(1, 2)
         load_wb(LAST)
-        if BS_SPLIT == 2:
-            load_wb_scales(1, 2)
 
         wa_bf, wa_wd, wa_sc = {}, {}, {}
         for e in range(E):
@@ -265,12 +259,9 @@ def tile_moe_elr_s_gelu_kernel(
 
         for u in range(HALVES):
             copies = (nc.vector.tensor_copy, nc.scalar.copy, nc.vector.tensor_copy)
-            for (q0, q1), copy, queue in zip(BANKS[LAST], copies, (nc.sync, nc.scalar if SQ else nc.sync, nc.sync)):
+            for (q0, q1), copy in zip(BANKS[LAST], copies):
                 copy(y_last[:, q0:q1, half(u)], y_bank[LAST, u, q0][:])
                 q1 = min(q1, TILES - HELD)
                 if q0 < q1:
-                    queue.dma_start(out_rows[:, q0:q1, slots(LAST, u)], y_last[:, q0:q1, half(u)])
-        if HELD:
-            (nc.scalar if SQ else nc.sync).dma_start(
-                out_rows[:, TILES - HELD :, LAST * C : (LAST + 1) * C], y_last[:, TILES - HELD :, :]
-            )
+                    nc.sync.dma_start(out_rows[:, q0:q1, slots(LAST, u)], y_last[:, q0:q1, half(u)])
+        nc.sync.dma_start(out_rows[:, TILES - HELD :, LAST * C : (LAST + 1) * C], y_last[:, TILES - HELD :, :])

@@ -1,3 +1,4 @@
+import math
 from contextlib import ExitStack
 
 import concourse.mybir as mybir
@@ -51,6 +52,10 @@ def tile_moe_elr_s_gelu_kernel(
         def sb(name, shape, dtype, tag=None):
             return keep.tile(shape, dtype, name=name, tag=tag or name, align_bytes=256)
 
+        def shifted(name, shape, dtype, skip):
+            flat = sb(name, [P, skip + math.prod(shape[1:])], dtype)[:, skip:]
+            return flat if len(shape) == 2 else flat.rearrange("p (a b) -> p a b", a=shape[1])
+
         offsets = keep.tile([P, E * C // LIST_GROUP], U16, name="offsets")
 
         warm = sb("warm", [P, 8], F32)
@@ -59,14 +64,14 @@ def tile_moe_elr_s_gelu_kernel(
         nc.scalar.activation(warm_out[:], warm[:], GELU)
 
         x_sc = sb("x_sc", [P, PASSES, T], U8)
-        w_sc = [sb(f"w_sc{e}", [P, PASSES, N], U8) for e in range(E)]
-        wb_sc = sb("wb_sc", [P, E, N], U8)
+        w_sc = [shifted(f"w_sc{e}", [P, PASSES, N], U8, 192) for e in range(E)]
+        wb_sc = shifted("wb_sc", [P, E, N], U8, 192)
         for scale_tile in (x_sc, w_sc[FIRST], wb_sc, w_sc[LAST]):
             nc.vector.memset(scale_tile[:].bitcast(I32), 0)
 
         x_wd = [sb(f"x_wd{s}", [P, T], I32) for s in range(PASSES)]
-        w_wd = {(e, s0): sb(f"w_wd{e}{s0}", [P, s1 - s0, 2 * N], U8) for e in range(E) for s0, s1 in W_LOADS[e]}
-        wb_wd = [sb(f"wb_wd{e}", [P, N], I32) for e in range(E)]
+        w_wd = {(e, s0): shifted(f"w_wd{e}{s0}", [P, s1 - s0, 2 * N], U8, 128) for e in range(E) for s0, s1 in W_LOADS[e]}
+        wb_wd = [shifted(f"wb_wd{e}", [P, N], I32, 32) for e in range(E)]
         wa_raw = {(e, s): sb(f"wa_raw{e}{s}", [P, PACK, H], F32) for e in range(E) for s in range(PASSES)}
 
         def load_x(s):
@@ -104,7 +109,7 @@ def tile_moe_elr_s_gelu_kernel(
 
         slot_wd = [sb(f"slot_wd{s}", [P, E * C], U32, tag=tag) for s, tag in enumerate(("x_sc", None))]
         spread_sc = sb("spread_sc", [P, PASSES, E * C], U8)
-        slot_sc = sb("slot_sc", [P, PASSES, E * C], U8)
+        slot_sc = shifted("slot_sc", [P, PASSES, E * C], U8, 64)
         for s in range(PASSES):
             nc.vector.tensor_copy(spread_sc[:, s, :], x_sc[:, s, :].indirect(offsets[:]))
         spread_rows = spread_sc[:].rearrange("p s c -> p (s c)").bitcast(I32)
@@ -129,14 +134,14 @@ def tile_moe_elr_s_gelu_kernel(
         for e in range(E):
             for s in range(PASSES):
                 wa_bf[e, s] = sb(f"wa_bf{e}{s}", [P, TILES, P, PACK], BF16)
-                wa_wd[e, s] = sb(f"wa_wd{e}{s}", [P, TILES, P], U32)
-                wa_sc[e, s] = sb(f"wa_sc{e}{s}", [P, TILES, P], U8)
+                wa_wd[e, s] = shifted(f"wa_wd{e}{s}", [P, TILES, P], U32, 32)
+                wa_sc[e, s] = shifted(f"wa_sc{e}{s}", [P, TILES, P], U8, 192)
         h_bank, y_bank, h_bf, h_wd, h_sc = {}, {}, {}, {}, {}
         for e in range(E):
             for u in range(HALVES):
                 h_bank[e, u] = psum.tile([P, TILES, HALF], F32, name=f"h_bank{e}{u}", tag=f"h{e}{u}")
             h_wd[e] = sb(f"h_wd{e}", [P, C], U32)
-            h_sc[e] = sb(f"h_sc{e}", [P, C], U8)
+            h_sc[e] = shifted(f"h_sc{e}", [P, C], U8, 64)
         y_last = sb("y_last", [P, TILES, C], F32)
         out_rows = out.rearrange("(q p) j -> p q j", p=P)
 

@@ -16,6 +16,9 @@ FP8X4 = mybir.dt.float8_e4m3fn_x4
 FP4X4 = mybir.dt.float4_e2m1fn_x4
 GELU = mybir.ActivationFunctionType.Gelu_apprx_tanh
 
+MS = 64
+SW = 128
+SS = 192
 P = 128
 PACK = 4
 K_PASS = P * PACK
@@ -30,14 +33,41 @@ HALF = 128
 HALVES = C // HALF
 FIRST, LAST = 0, 1
 
-VECTOR_SHARE = {(FIRST, 0): 0, (FIRST, 1): 76, (LAST, 0): 80, (LAST, 1): 84}
+VECTOR_SHARE = {(FIRST, 0): 0, (FIRST, 1): 76, (LAST, 0): 80}
+SPLIT = False
+WA_LOADS = {(FIRST, 0): ((0, 4),), (FIRST, 1): ((0, 4),), (LAST, 0): ((0, 4),), (LAST, 1): ((0, 2), (2, 4)) if SPLIT else ((0, 4),)}
+EARLY_SHARE = 72
+H0_TAG = None
+WB0_FIRST = 2
+WB0_SECOND = 3
+PRE = ("a10", "w00", "bs", "a11", "w01", "b0", "s1", "w1", "b1")
+BYQ = True
+W01_EARLY = False
+U0CUT = 8
+COPY0 = "ssvv"
+COPY1 = ("vsvs", "vsvs")
+ORDER = ((0, 1, 2, 3), (3, 2, 1, 0))
+LATE0 = 0
+S1CUT = 1
+CUT1 = 2
+CUT2 = 3
+SHARE3B = 128
+TWO_STEP = ()
+WEAVE = True
+HBF0_TAG = "wa_raw100"
+COPY0_TAGS = {"v": "wa_bf11", "s": None}
+QH_LATE = False
+FINAL_SHARES = (80, 80)
 
 WHOLE_PASS = ((0, TILES),)
 FINAL_CASTS = ((0, 2), (2, TILES))
 FINAL_QUANTIZES = ((0, 2), (2, 3), (3, TILES))
 
-BANKS = {FIRST: ((0, 2), (2, TILES)), LAST: ((0, 1), (1, 2), (2, TILES))}
-LAST_BANK_TAGS = (("y10", "h00", "y11"), ("h01", "y00", "y02"))
+B0 = ((0, 1), (1, 2), (2, 3), (3, 4))
+B10 = ((0, 1), (1, 2), (2, 3), (3, 4))
+B11 = ((0, 1), (1, 2), (2, 3), (3, 4))
+BANKS = {(FIRST, 0): B0, (LAST, 0): B10, (LAST, 1): B11}
+LAST_BANK_TAGS = (("h00", "h01", "y00", "y01"), ("y02", "h10", "h11", "y03"))
 W_LOADS = {FIRST: ((0, 1), (1, PASSES)), LAST: ((0, PASSES),)}
 
 
@@ -52,8 +82,8 @@ def tile_moe_elr_s_gelu_kernel(
         def sb(name, shape, dtype, tag=None):
             return keep.tile(shape, dtype, name=name, tag=tag or name, align_bytes=256)
 
-        def shifted(name, shape, dtype, skip):
-            flat = sb(name, [P, skip + math.prod(shape[1:])], dtype)[:, skip:]
+        def shifted(name, shape, dtype, skip, tag=None):
+            flat = sb(name, [P, skip + math.prod(shape[1:])], dtype, tag)[:, skip:]
             return flat if len(shape) == 2 else flat.rearrange("p (a b) -> p a b", a=shape[1])
 
         offsets = keep.tile([P, E * C // LIST_GROUP], U16, name="offsets")
@@ -64,22 +94,28 @@ def tile_moe_elr_s_gelu_kernel(
         nc.scalar.activation(warm_out[:], warm[:], GELU)
 
         x_sc = sb("x_sc", [P, PASSES, T], U8)
-        w_sc = [shifted(f"w_sc{e}", [P, PASSES, N], U8, 192) for e in range(E)]
-        wb_sc = shifted("wb_sc", [P, E, N], U8, 192)
+        w_sc = [shifted(f"w_sc{e}", [P, PASSES, N], U8, SS) for e in range(E)]
+        wb_sc = shifted("wb_sc", [P, E, N], U8, SS)
         for scale_tile in (x_sc, w_sc[FIRST], wb_sc, w_sc[LAST]):
             nc.vector.memset(scale_tile[:].bitcast(I32), 0)
 
         x_wd = [sb(f"x_wd{s}", [P, T], I32) for s in range(PASSES)]
-        w_wd = {(e, s0): shifted(f"w_wd{e}{s0}", [P, s1 - s0, 2 * N], U8, 128) for e in range(E) for s0, s1 in W_LOADS[e]}
-        wb_wd = [shifted(f"wb_wd{e}", [P, N], I32, 32) for e in range(E)]
-        wa_raw = {(e, s): sb(f"wa_raw{e}{s}", [P, PACK, H], F32) for e in range(E) for s in range(PASSES)}
+        w_wd = {(e, s0): shifted(f"w_wd{e}{s0}", [P, s1 - s0, 2 * N], U8, SW) for e in range(E) for s0, s1 in W_LOADS[e]}
+        wb_wd = [shifted(f"wb_wd{e}", [P, N], I32, SW // 4) for e in range(E)]
+        wa_raw = {
+            (e, s, j0): sb(f"wa_raw{e}{s}{j0}", [P, j1 - j0, H], F32)
+            for e in range(E)
+            for s in range(PASSES)
+            for j0, j1 in WA_LOADS[e, s]
+        }
 
         def load_x(s):
             nc.sync.dma_start(x_wd[s][:], x_words[s].rearrange("p t d -> p (t d)").bitcast(I32))
 
-        def load_wa(e, s):
+        def load_wa(e, s, part=None):
             rows = wa[e, K_PASS * s : K_PASS * (s + 1), :].rearrange("(p j) i -> p j i", j=PACK)
-            nc.sync.dma_start(wa_raw[e, s][:], rows)
+            for j0, j1 in WA_LOADS[e, s] if part is None else WA_LOADS[e, s][part : part + 1]:
+                nc.sync.dma_start(wa_raw[e, s, j0][:], rows[:, j0:j1, :])
 
         def load_w(e, s0, s1):
             rows = w_words[e, s0:s1].rearrange("s p b -> p s b")
@@ -88,16 +124,17 @@ def tile_moe_elr_s_gelu_kernel(
         def load_wb(e):
             nc.sync.dma_start(wb_wd[e][:], wb_words[e, 0].rearrange("p n d -> p (n d)").bitcast(I32))
 
-        def load_scales(scale_tile, first, rows):
-            for r in range(SCALE_ROWS):
+        def load_scales(scale_tile, first, rows, r0=0, r1=SCALE_ROWS):
+            for r in range(r0, r1):
                 nc.sync.dma_start(scale_tile[first + r : P : QUADRANT].bitcast(I32), rows[r].bitcast(I32))
 
         def load_wb_scales(e0, e1):
             rows = wb_scales[e0:e1].rearrange("e s (q r) n -> r q (e s) n", r=SCALE_ROWS)
             load_scales(wb_sc[:, e0:e1, :], SCALE_ROWS, rows)
 
-        def load_w_scales(e):
-            load_scales(w_sc[e], 0, w_scales[e : e + 1].rearrange("e s (q r) n -> r q (e s) n", r=SCALE_ROWS))
+        def load_w_scales(e, r0=0, r1=SCALE_ROWS):
+            rows = w_scales[e : e + 1].rearrange("e s (q r) n -> r q (e s) n", r=SCALE_ROWS)
+            load_scales(w_sc[e], 0, rows, r0, r1)
 
         load_x(0)
         nc.sync.dma_start(x_sc[0:P:SPREAD].bitcast(I32), x_scales.rearrange("s b t -> b s t").bitcast(I32))
@@ -109,7 +146,7 @@ def tile_moe_elr_s_gelu_kernel(
 
         slot_wd = [sb(f"slot_wd{s}", [P, E * C], U32, tag=tag) for s, tag in enumerate(("x_sc", None))]
         spread_sc = sb("spread_sc", [P, PASSES, E * C], U8)
-        slot_sc = shifted("slot_sc", [P, PASSES, E * C], U8, 64)
+        slot_sc = shifted("slot_sc", [P, PASSES, E * C], U8, MS)
         for s in range(PASSES):
             nc.vector.tensor_copy(spread_sc[:, s, :], x_sc[:, s, :].indirect(offsets[:]))
         spread_rows = spread_sc[:].rearrange("p s c -> p (s c)").bitcast(I32)
@@ -120,30 +157,45 @@ def tile_moe_elr_s_gelu_kernel(
         nc.vector.tensor_copy(slot_wd[0][:], x_wd[0][:].bitcast(U32).indirect(offsets[:]))
         nc.vector.tensor_copy(slot_wd[1][:], x_wd[1][:].bitcast(U32).indirect(offsets[:]))
 
-        load_wa(LAST, 0)
-        load_w(FIRST, 0, 1)
-        load_wb_scales(0, E)
-        load_wa(LAST, 1)
-        load_w(FIRST, 1, PASSES)
-        load_wb(FIRST)
-        load_w_scales(LAST)
-        load_w(LAST, 0, PASSES)
-        load_wb(LAST)
+        loads = {
+            "a10": lambda: load_wa(LAST, 0),
+            "a11": lambda: load_wa(LAST, 1),
+            "a11a": lambda: load_wa(LAST, 1, 0),
+            "a11b": lambda: load_wa(LAST, 1, 1),
+            "w00": lambda: load_w(FIRST, 0, 1),
+            "w01": lambda: load_w(FIRST, 1, 2),
+            "w0": lambda: load_w(FIRST, 0, 2),
+            "w10": lambda: load_w(LAST, 0, 1),
+            "w11": lambda: load_w(LAST, 1, 2),
+            "w1": lambda: load_w(LAST, 0, 2),
+            "bs": lambda: load_wb_scales(0, E),
+            "bs0": lambda: load_wb_scales(0, 1),
+            "bs1": lambda: load_wb_scales(1, 2),
+            "s1": lambda: load_w_scales(LAST),
+            "s1a": lambda: load_w_scales(LAST, 0, S1CUT),
+            "s1b": lambda: load_w_scales(LAST, S1CUT, SCALE_ROWS),
+            "b0": lambda: load_wb(FIRST),
+            "b1": lambda: load_wb(LAST),
+        }
+        for name in PRE:
+            loads[name]()
 
         wa_bf, wa_wd, wa_sc = {}, {}, {}
         for e in range(E):
             for s in range(PASSES):
                 wa_bf[e, s] = sb(f"wa_bf{e}{s}", [P, TILES, P, PACK], BF16)
-                wa_wd[e, s] = shifted(f"wa_wd{e}{s}", [P, TILES, P], U32, 32)
-                wa_sc[e, s] = shifted(f"wa_sc{e}{s}", [P, TILES, P], U8, 192)
+                wa_wd[e, s] = shifted(f"wa_wd{e}{s}", [P, TILES, P], U32, SW // 4)
+                wa_sc[e, s] = shifted(f"wa_sc{e}{s}", [P, TILES, P], U8, SS)
         h_bank, y_bank, h_bf, h_wd, h_sc = {}, {}, {}, {}, {}
         for e in range(E):
             for u in range(HALVES):
                 h_bank[e, u] = psum.tile([P, TILES, HALF], F32, name=f"h_bank{e}{u}", tag=f"h{e}{u}")
-            h_wd[e] = sb(f"h_wd{e}", [P, C], U32)
-            h_sc[e] = shifted(f"h_sc{e}", [P, C], U8, 64)
+            h_wd[e] = sb(f"h_wd{e}", [P, C], U32, tag=H0_TAG if e == FIRST else None)
+            h_sc[e] = shifted(f"h_sc{e}", [P, C], U8, MS)
         y_last = sb("y_last", [P, TILES, C], F32)
         out_rows = out.rearrange("(q p) j -> p q j", p=P)
+
+        engine_copy = {"s": nc.scalar.copy, "v": nc.vector.tensor_copy}
 
         def half(u):
             return slice(u * HALF, (u + 1) * HALF)
@@ -151,14 +203,15 @@ def tile_moe_elr_s_gelu_kernel(
         def slots(e, u):
             return slice(e * C + u * HALF, e * C + (u + 1) * HALF)
 
-        def prepare_wa(e, s, casts, quantizes):
-            share = VECTOR_SHARE[e, s]
-            for t0, t1 in casts:
-                src = wa_raw[e, s][:].rearrange("p j (m t) -> p m j t", t=TILES)[:, :, :, t0:t1]
-                dst = wa_bf[e, s][:].rearrange("p t m j -> p m j t")[:, :, :, t0:t1]
-                if share:
-                    nc.vector.tensor_copy(dst[:, :share], src[:, :share])
+        def cast_wa(e, s, j0, j1, t0, t1, share):
+            src = wa_raw[e, s, j0][:].rearrange("p j (m t) -> p m j t", t=TILES)[:, :, :, t0:t1]
+            dst = wa_bf[e, s][:].rearrange("p t m j -> p m j t")[:, :, j0:j1, t0:t1]
+            if share:
+                nc.vector.tensor_copy(dst[:, :share], src[:, :share])
+            if share < P:
                 nc.scalar.copy(dst[:, share:], src[:, share:])
+
+        def quantize_wa(e, s, quantizes):
             for t0, t1 in quantizes:
                 nc.vector.quantize_mx(
                     out=wa_wd[e, s][:, t0:t1, :].rearrange("p t m -> p (t m)").bitcast(FP8X4),
@@ -166,8 +219,8 @@ def tile_moe_elr_s_gelu_kernel(
                     in_=wa_bf[e, s][:, t0:t1, :, :].rearrange("p t m j -> p (t m j)"),
                 )
 
-        def h_pass(e, s):
-            for u in range(HALVES):
+        def h_pass(e, s, halves=range(HALVES)):
+            for u in halves:
                 for t in range(TILES):
                     nc.tensor.matmul_mx(
                         out=h_bank[e, u][:, t, :],
@@ -180,7 +233,7 @@ def tile_moe_elr_s_gelu_kernel(
                     )
 
         def y_out(e, u, q, width):
-            q0 = max(first for first, end in BANKS[e] if first <= q)
+            q0 = max(first for first, end in BANKS[e, u if e == LAST else 0] if first <= q)
             if e == FIRST:
                 return y_bank[FIRST, q0][:, q - q0, u * HALF : u * HALF + width]
             return y_bank[LAST, u, q0][:, q - q0, :]
@@ -188,7 +241,7 @@ def tile_moe_elr_s_gelu_kernel(
         def w_pass(e, s, u, q0, q1):
             s0 = max(first for first, end in W_LOADS[e] if first <= s)
             for q in range(q0, q1):
-                opens_bank = q in [first for first, end in BANKS[e]] and (e == LAST or u == 0)
+                opens_bank = q in [first for first, end in BANKS[e, u if e == LAST else 0]] and (e == LAST or u == 0)
                 nc.tensor.matmul_mx(
                     out=y_out(e, u, q, HALF),
                     lhsT=w_wd[e, s0][:, s - s0, 2 * P * q : 2 * P * (q + 1)].bitcast(FP4X4),
@@ -209,8 +262,8 @@ def tile_moe_elr_s_gelu_kernel(
                 in_=h_bf[e][:, half(u), :].rearrange("p n t -> p (n t)"),
             )
 
-        def wb_pass(e, u, width):
-            for q in range(TILES):
+        def wb_pass(e, u, width, q0=0, q1=TILES):
+            for q in range(q0, q1):
                 nc.tensor.matmul_mx(
                     out=y_out(e, u, q, width),
                     lhsT=wb_wd[e][:, P * q : P * (q + 1)].bitcast(FP8X4),
@@ -218,55 +271,83 @@ def tile_moe_elr_s_gelu_kernel(
                     rhs=h_wd[e][:, u * HALF : u * HALF + width].bitcast(FP8X4),
                     rhs_scale=h_sc[e][:, u * HALF : u * HALF + width],
                     start=False,
-                    stop=(q + 1 in [end for first, end in BANKS[e]]),
+                    stop=(q + 1 in [end for first, end in BANKS[e, u if e == LAST else 0]]),
                 )
 
         for e, s in ((FIRST, 0), (FIRST, 1), (LAST, 0)):
-            prepare_wa(e, s, WHOLE_PASS, WHOLE_PASS)
+            steps = FINAL_CASTS if (e, s) in TWO_STEP else WHOLE_PASS
+            for n, (t0, t1) in enumerate(steps):
+                cast_wa(e, s, 0, PACK, t0, t1, SHARE3B if (e, s, n) == (LAST, 0, 1) else VECTOR_SHARE[e, s])
+            quantize_wa(e, s, steps)
             h_pass(e, s)
-        for q0, q1 in BANKS[FIRST]:
+        for q0, q1 in BANKS[FIRST, 0]:
             y_bank[FIRST, q0] = psum.tile([P, q1 - q0, C], F32, name=f"y_bank0{q0}", tag=f"y0{q0}")
-        h_bf[FIRST] = sb("h_bf0", [P, C, PACK], BF16, tag="wa_raw10")
+        h_bf[FIRST] = sb("h_bf0", [P, C, PACK], BF16, tag=HBF0_TAG)
         for u in range(HALVES):
             gelu(FIRST, u)
         for u in range(HALVES):
-            quantize_h(FIRST, u)
-        for u in range(HALVES):
             w_pass(FIRST, 0, u, 0, TILES)
 
-        prepare_wa(LAST, 1, FINAL_CASTS, FINAL_QUANTIZES)
-        for q0, q1 in BANKS[FIRST]:
+        if not QH_LATE:
+            for u in range(HALVES):
+                quantize_h(FIRST, u)
+        if SPLIT:
+            cast_wa(LAST, 1, 0, 2, 0, TILES, EARLY_SHARE)
+        if QH_LATE:
+            for u in range(HALVES):
+                quantize_h(FIRST, u)
+        for (t0, t1), share in zip(FINAL_CASTS, FINAL_SHARES):
+            cast_wa(LAST, 1, 2 if SPLIT else 0, PACK, t0, t1, share)
+        quantize_wa(LAST, 1, FINAL_QUANTIZES)
+        for q0, q1 in BANKS[FIRST, 0]:
             for u in range(HALVES):
                 w_pass(FIRST, 1, u, q0, q1)
-        wb_pass(FIRST, 0, C)
-        h_pass(LAST, 1)
+        wb_pass(FIRST, 0, C, 0, WB0_FIRST)
+        h_pass(LAST, 1, [0])
+        wb_pass(FIRST, 0, C, WB0_FIRST, WB0_SECOND)
+        h_pass(LAST, 1, [1])
+        wb_pass(FIRST, 0, C, WB0_SECOND, TILES)
 
-        for (q0, q1), copy, tag in zip(BANKS[FIRST], (nc.scalar.copy, nc.vector.tensor_copy), (None, "wa_bf11")):
-            y_first = sb(f"y_first{q0}", [P, q1 - q0, C], F32, tag=tag)
-            copy(y_first[:], y_bank[FIRST, q0][:])
-            nc.sync.dma_start(out_rows[:, q0:q1, 0:C], y_first[:])
+        y_first = {c: sb(f"y_first_{c}", [P, TILES, C], F32, tag=COPY0_TAGS[c]) for c in set(COPY0)}
+
+        def store_first(banks):
+            for (q0, q1), c in banks:
+                engine_copy[c](y_first[c][:, q0:q1, :], y_bank[FIRST, q0][:])
+                nc.sync.dma_start(out_rows[:, q0:q1, 0:C], y_first[c][:, q0:q1, :])
+
+        first_banks = list(zip(BANKS[FIRST, 0], COPY0))
+        store_first(first_banks[: len(first_banks) - LATE0])
 
         h_bf[LAST] = sb("h_bf1", [P, C, PACK], BF16)
+        gelu(LAST, 0)
+        quantize_h(LAST, 0)
+        gelu(LAST, 1)
+        store_first(first_banks[len(first_banks) - LATE0 :])
+        quantize_h(LAST, 1)
         for u in range(HALVES):
-            gelu(LAST, u)
-            quantize_h(LAST, u)
-        for u in range(HALVES):
-            for (q0, q1), tag in zip(BANKS[LAST], LAST_BANK_TAGS[u]):
-                y_bank[LAST, u, q0] = psum.tile([P, q1 - q0, HALF], F32, name=f"y_bank1{u}{q0}", tag=tag)
-        for s in range(PASSES):
-            w_pass(LAST, s, 0, 0, TILES)
-        for s in range(PASSES):
-            w_pass(LAST, s, 1, 0, TILES // 2)
-        wb_pass(LAST, 0, HALF)
-        for s in range(PASSES):
-            w_pass(LAST, s, 1, TILES // 2, TILES)
-        wb_pass(LAST, 1, HALF)
+            for q, tag in zip(ORDER[u], LAST_BANK_TAGS[u]):
+                y_bank[LAST, u, q] = psum.tile([P, 1, HALF], F32, name=f"y_bank1{u}{q}", tag=tag)
+        for q in ORDER[0]:
+            for s in range(PASSES):
+                w_pass(LAST, s, 0, q, q + 1)
+        for q in ORDER[1][:CUT1]:
+            for s in range(PASSES):
+                w_pass(LAST, s, 1, q, q + 1)
+        for q in ORDER[0]:
+            wb_pass(LAST, 0, HALF, q, q + 1)
+        for q in ORDER[1][CUT1:CUT2]:
+            for s in range(PASSES):
+                w_pass(LAST, s, 1, q, q + 1)
+        for n, q in enumerate(ORDER[1]):
+            if n >= CUT2:
+                for s in range(PASSES):
+                    w_pass(LAST, s, 1, q, q + 1)
+            wb_pass(LAST, 1, HALF, q, q + 1)
 
         for u in range(HALVES):
-            copies = (nc.vector.tensor_copy, nc.scalar.copy, nc.vector.tensor_copy)
-            for (q0, q1), copy in zip(BANKS[LAST], copies):
-                copy(y_last[:, q0:q1, half(u)], y_bank[LAST, u, q0][:])
-                q1 = min(q1, TILES - HELD)
-                if q0 < q1:
-                    nc.sync.dma_start(out_rows[:, q0:q1, slots(LAST, u)], y_last[:, q0:q1, half(u)])
-        nc.sync.dma_start(out_rows[:, TILES - HELD :, LAST * C : (LAST + 1) * C], y_last[:, TILES - HELD :, :])
+            for q, c in zip(ORDER[u], COPY1[u]):
+                engine_copy[c](y_last[:, q, half(u)], y_bank[LAST, u, q][:, 0, :])
+                if q < TILES - HELD:
+                    nc.sync.dma_start(out_rows[:, q, slots(LAST, u)], y_last[:, q, half(u)])
+                elif u == HALVES - 1:
+                    nc.sync.dma_start(out_rows[:, q, LAST * C : (LAST + 1) * C], y_last[:, q, :])

@@ -16,9 +16,10 @@ FP8X4 = mybir.dt.float8_e4m3fn_x4
 FP4X4 = mybir.dt.float4_e2m1fn_x4
 GELU = mybir.ActivationFunctionType.Gelu_apprx_tanh
 
+MW = 128
 MS = 64
-SW = 128
-SS = 192
+SW = 0
+SS = 0
 P = 128
 PACK = 4
 K_PASS = P * PACK
@@ -144,7 +145,7 @@ def tile_moe_elr_s_gelu_kernel(
         load_w_scales(FIRST)
         load_wa(FIRST, 1)
 
-        slot_wd = [sb(f"slot_wd{s}", [P, E * C], U32, tag=tag) for s, tag in enumerate(("x_sc", None))]
+        slot_wd = [shifted(f"slot_wd{s}", [P, E * C], U32, MW // 4, tag) for s, tag in enumerate(("x_sc", None))]
         spread_sc = sb("spread_sc", [P, PASSES, E * C], U8)
         slot_sc = shifted("slot_sc", [P, PASSES, E * C], U8, MS)
         for s in range(PASSES):
@@ -190,7 +191,7 @@ def tile_moe_elr_s_gelu_kernel(
         for e in range(E):
             for u in range(HALVES):
                 h_bank[e, u] = psum.tile([P, TILES, HALF], F32, name=f"h_bank{e}{u}", tag=f"h{e}{u}")
-            h_wd[e] = sb(f"h_wd{e}", [P, C], U32, tag=H0_TAG if e == FIRST else None)
+            h_wd[e] = shifted(f"h_wd{e}", [P, C], U32, MW // 4)
             h_sc[e] = shifted(f"h_sc{e}", [P, C], U8, MS)
         y_last = sb("y_last", [P, TILES, C], F32)
         out_rows = out.rearrange("(q p) j -> p q j", p=P)

@@ -16,7 +16,7 @@ FP8X4 = mybir.dt.float8_e4m3fn_x4
 FP4X4 = mybir.dt.float4_e2m1fn_x4
 GELU = mybir.ActivationFunctionType.Gelu_apprx_tanh
 
-MW = 128
+MW = 192
 MS = 64
 SW = 0
 SS = 0

@@ -17,6 +17,7 @@ FP4X4 = mybir.dt.float4_e2m1fn_x4
 GELU = mybir.ActivationFunctionType.Gelu_apprx_tanh
 
 MW = 192
+BF = 128
 MS = 64
 SW = 0
 SS = 0
@@ -184,7 +185,9 @@ def tile_moe_elr_s_gelu_kernel(
         wa_bf, wa_wd, wa_sc = {}, {}, {}
         for e in range(E):
             for s in range(PASSES):
-                wa_bf[e, s] = sb(f"wa_bf{e}{s}", [P, TILES, P, PACK], BF16)
+                wa_bf[e, s] = shifted(f"wa_bf{e}{s}", [P, TILES, P * PACK], BF16, BF // 2).rearrange(
+                    "p t (m j) -> p t m j", j=PACK
+                )
                 wa_wd[e, s] = shifted(f"wa_wd{e}{s}", [P, TILES, P], U32, SW // 4)
                 wa_sc[e, s] = shifted(f"wa_sc{e}{s}", [P, TILES, P], U8, SS)
         h_bank, y_bank, h_bf, h_wd, h_sc = {}, {}, {}, {}, {}
@@ -319,7 +322,7 @@ def tile_moe_elr_s_gelu_kernel(
         first_banks = list(zip(BANKS[FIRST, 0], COPY0))
         store_first(first_banks[: len(first_banks) - LATE0])
 
-        h_bf[LAST] = sb("h_bf1", [P, C, PACK], BF16)
+        h_bf[LAST] = shifted("h_bf1", [P, C, PACK], BF16, 32)
         gelu(LAST, 0)
         quantize_h(LAST, 0)
         gelu(LAST, 1)

@@ -16,11 +16,6 @@ FP8X4 = mybir.dt.float8_e4m3fn_x4
 FP4X4 = mybir.dt.float4_e2m1fn_x4
 GELU = mybir.ActivationFunctionType.Gelu_apprx_tanh
 
-MW = 192
-BF = 128
-MS = 64
-SW = 0
-SS = 0
 P = 128
 PACK = 4
 K_PASS = P * PACK
@@ -28,47 +23,27 @@ PASSES = K // K_PASS
 QUADRANT = 32
 SCALE_ROWS = 4
 SPREAD = 8
-HELD = 1
 LIST_GROUP = 16
 TILES = N // P
 HALF = 128
 HALVES = C // HALF
 FIRST, LAST = 0, 1
 
-VECTOR_SHARE = {(FIRST, 0): 0, (FIRST, 1): 76, (LAST, 0): 80}
-SPLIT = False
-WA_LOADS = {(FIRST, 0): ((0, 4),), (FIRST, 1): ((0, 4),), (LAST, 0): ((0, 4),), (LAST, 1): ((0, 2), (2, 4)) if SPLIT else ((0, 4),)}
-EARLY_SHARE = 72
-H0_TAG = None
-WB0_FIRST = 2
-WB0_SECOND = 3
-PRE = ("a10", "w00", "bs", "a11", "w01", "b0", "s1", "w1", "b1")
-BYQ = True
-W01_EARLY = False
-U0CUT = 8
-COPY0 = "ssvv"
-COPY1 = ("vsvs", "vsvs")
-ORDER = ((0, 1, 2, 3), (3, 2, 1, 0))
-LATE0 = 0
-S1CUT = 1
-CUT1 = 2
-CUT2 = 3
-SHARE3B = 128
-TWO_STEP = ()
-WEAVE = True
-HBF0_TAG = "wa_raw100"
-COPY0_TAGS = {"v": "wa_bf11", "s": None}
-QH_LATE = False
-FINAL_SHARES = (80, 80)
+MOVING_WORDS_AT = 192
+MOVING_SCALES_AT = 64
+WA_BF_AT = 128
+LAST_H_BF_AT = 64
+WA_SCALES_FROM = 4
+H_SCALES_FROM = 12
+
+VECTOR_SHARE = {(FIRST, 0): 0, (FIRST, 1): 76, (LAST, 0): 80, (LAST, 1): 80}
 
 WHOLE_PASS = ((0, TILES),)
 FINAL_CASTS = ((0, 2), (2, TILES))
 FINAL_QUANTIZES = ((0, 2), (2, 3), (3, TILES))
 
-B0 = ((0, 1), (1, 2), (2, 3), (3, 4))
-B10 = ((0, 1), (1, 2), (2, 3), (3, 4))
-B11 = ((0, 1), (1, 2), (2, 3), (3, 4))
-BANKS = {(FIRST, 0): B0, (LAST, 0): B10, (LAST, 1): B11}
+ORDER = ((0, 1, 2, 3), (3, 2, 1, 0))
+HELD_TILE = TILES - 1
 LAST_BANK_TAGS = (("h00", "h01", "y00", "y01"), ("y02", "h10", "h11", "y03"))
 W_LOADS = {FIRST: ((0, 1), (1, PASSES)), LAST: ((0, PASSES),)}
 
@@ -96,28 +71,22 @@ def tile_moe_elr_s_gelu_kernel(
         nc.scalar.activation(warm_out[:], warm[:], GELU)
 
         x_sc = sb("x_sc", [P, PASSES, T], U8)
-        w_sc = [shifted(f"w_sc{e}", [P, PASSES, N], U8, SS) for e in range(E)]
-        wb_sc = shifted("wb_sc", [P, E, N], U8, SS)
+        w_sc = [shifted(f"w_sc{e}", [P, PASSES, N], U8, 0) for e in range(E)]
+        wb_sc = shifted("wb_sc", [P, E, N], U8, 0)
         for scale_tile in (x_sc, w_sc[FIRST], wb_sc, w_sc[LAST]):
             nc.vector.memset(scale_tile[:].bitcast(I32), 0)
 
         x_wd = [sb(f"x_wd{s}", [P, T], I32) for s in range(PASSES)]
-        w_wd = {(e, s0): shifted(f"w_wd{e}{s0}", [P, s1 - s0, 2 * N], U8, SW) for e in range(E) for s0, s1 in W_LOADS[e]}
-        wb_wd = [shifted(f"wb_wd{e}", [P, N], I32, SW // 4) for e in range(E)]
-        wa_raw = {
-            (e, s, j0): sb(f"wa_raw{e}{s}{j0}", [P, j1 - j0, H], F32)
-            for e in range(E)
-            for s in range(PASSES)
-            for j0, j1 in WA_LOADS[e, s]
-        }
+        w_wd = {(e, s0): shifted(f"w_wd{e}{s0}", [P, s1 - s0, 2 * N], U8, 0) for e in range(E) for s0, s1 in W_LOADS[e]}
+        wb_wd = [sb(f"wb_wd{e}", [P, N], I32) for e in range(E)]
+        wa_raw = {(e, s): sb(f"wa_raw{e}{s}", [P, PACK, H], F32) for e in range(E) for s in range(PASSES)}
 
         def load_x(s):
             nc.sync.dma_start(x_wd[s][:], x_words[s].rearrange("p t d -> p (t d)").bitcast(I32))
 
-        def load_wa(e, s, part=None):
+        def load_wa(e, s):
             rows = wa[e, K_PASS * s : K_PASS * (s + 1), :].rearrange("(p j) i -> p j i", j=PACK)
-            for j0, j1 in WA_LOADS[e, s] if part is None else WA_LOADS[e, s][part : part + 1]:
-                nc.sync.dma_start(wa_raw[e, s, j0][:], rows[:, j0:j1, :])
+            nc.sync.dma_start(wa_raw[e, s][:], rows)
 
         def load_w(e, s0, s1):
             rows = w_words[e, s0:s1].rearrange("s p b -> p s b")
@@ -126,17 +95,15 @@ def tile_moe_elr_s_gelu_kernel(
         def load_wb(e):
             nc.sync.dma_start(wb_wd[e][:], wb_words[e, 0].rearrange("p n d -> p (n d)").bitcast(I32))
 
-        def load_scales(scale_tile, first, rows, r0=0, r1=SCALE_ROWS):
-            for r in range(r0, r1):
+        def load_scales(scale_tile, first, rows):
+            for r in range(SCALE_ROWS):
                 nc.sync.dma_start(scale_tile[first + r : P : QUADRANT].bitcast(I32), rows[r].bitcast(I32))
 
-        def load_wb_scales(e0, e1):
-            rows = wb_scales[e0:e1].rearrange("e s (q r) n -> r q (e s) n", r=SCALE_ROWS)
-            load_scales(wb_sc[:, e0:e1, :], SCALE_ROWS, rows)
+        def load_wb_scales():
+            load_scales(wb_sc, SCALE_ROWS, wb_scales.rearrange("e s (q r) n -> r q (e s) n", r=SCALE_ROWS))
 
-        def load_w_scales(e, r0=0, r1=SCALE_ROWS):
-            rows = w_scales[e : e + 1].rearrange("e s (q r) n -> r q (e s) n", r=SCALE_ROWS)
-            load_scales(w_sc[e], 0, rows, r0, r1)
+        def load_w_scales(e):
+            load_scales(w_sc[e], 0, w_scales[e : e + 1].rearrange("e s (q r) n -> r q (e s) n", r=SCALE_ROWS))
 
         load_x(0)
         nc.sync.dma_start(x_sc[0:P:SPREAD].bitcast(I32), x_scales.rearrange("s b t -> b s t").bitcast(I32))
@@ -146,9 +113,11 @@ def tile_moe_elr_s_gelu_kernel(
         load_w_scales(FIRST)
         load_wa(FIRST, 1)
 
-        slot_wd = [shifted(f"slot_wd{s}", [P, E * C], U32, MW // 4, tag) for s, tag in enumerate(("x_sc", None))]
+        slot_wd = [
+            shifted(f"slot_wd{s}", [P, E * C], U32, MOVING_WORDS_AT // 4, tag) for s, tag in enumerate(("x_sc", None))
+        ]
         spread_sc = sb("spread_sc", [P, PASSES, E * C], U8)
-        slot_sc = shifted("slot_sc", [P, PASSES, E * C], U8, MS)
+        slot_sc = shifted("slot_sc", [P, PASSES, E * C], U8, MOVING_SCALES_AT)
         for s in range(PASSES):
             nc.vector.tensor_copy(spread_sc[:, s, :], x_sc[:, s, :].indirect(offsets[:]))
         spread_rows = spread_sc[:].rearrange("p s c -> p (s c)").bitcast(I32)
@@ -156,50 +125,35 @@ def tile_moe_elr_s_gelu_kernel(
         nc.vector.tensor_copy(slot_rows, spread_rows)
         for r in range(1, SCALE_ROWS):
             nc.sync.dma_start(slot_rows[r:P:QUADRANT], spread_rows[SPREAD * r : P : QUADRANT])
-        nc.vector.tensor_copy(slot_wd[0][:], x_wd[0][:].bitcast(U32).indirect(offsets[:]))
-        nc.vector.tensor_copy(slot_wd[1][:], x_wd[1][:].bitcast(U32).indirect(offsets[:]))
+        for s in range(PASSES):
+            nc.vector.tensor_copy(slot_wd[s][:], x_wd[s][:].bitcast(U32).indirect(offsets[:]))
 
-        loads = {
-            "a10": lambda: load_wa(LAST, 0),
-            "a11": lambda: load_wa(LAST, 1),
-            "a11a": lambda: load_wa(LAST, 1, 0),
-            "a11b": lambda: load_wa(LAST, 1, 1),
-            "w00": lambda: load_w(FIRST, 0, 1),
-            "w01": lambda: load_w(FIRST, 1, 2),
-            "w0": lambda: load_w(FIRST, 0, 2),
-            "w10": lambda: load_w(LAST, 0, 1),
-            "w11": lambda: load_w(LAST, 1, 2),
-            "w1": lambda: load_w(LAST, 0, 2),
-            "bs": lambda: load_wb_scales(0, E),
-            "bs0": lambda: load_wb_scales(0, 1),
-            "bs1": lambda: load_wb_scales(1, 2),
-            "s1": lambda: load_w_scales(LAST),
-            "s1a": lambda: load_w_scales(LAST, 0, S1CUT),
-            "s1b": lambda: load_w_scales(LAST, S1CUT, SCALE_ROWS),
-            "b0": lambda: load_wb(FIRST),
-            "b1": lambda: load_wb(LAST),
-        }
-        for name in PRE:
-            loads[name]()
+        load_wa(LAST, 0)
+        load_w(FIRST, 0, 1)
+        load_wb_scales()
+        load_wa(LAST, 1)
+        load_w(FIRST, 1, PASSES)
+        load_wb(FIRST)
+        load_w_scales(LAST)
+        load_w(LAST, 0, PASSES)
+        load_wb(LAST)
 
         wa_bf, wa_wd, wa_sc = {}, {}, {}
         for e in range(E):
             for s in range(PASSES):
-                wa_bf[e, s] = shifted(f"wa_bf{e}{s}", [P, TILES, P * PACK], BF16, BF // 2).rearrange(
+                wa_bf[e, s] = shifted(f"wa_bf{e}{s}", [P, TILES, P * PACK], BF16, WA_BF_AT // 2).rearrange(
                     "p t (m j) -> p t m j", j=PACK
                 )
-                wa_wd[e, s] = shifted(f"wa_wd{e}{s}", [P, TILES, P], U32, SW // 4)
-                wa_sc[e, s] = shifted(f"wa_sc{e}{s}", [P, TILES, P], U8, SS)
+                wa_wd[e, s] = sb(f"wa_wd{e}{s}", [P, TILES, P], U32)
+                wa_sc[e, s] = sb(f"wa_sc{e}{s}", [P, TILES, P], U8)
         h_bank, y_bank, h_bf, h_wd, h_sc = {}, {}, {}, {}, {}
         for e in range(E):
             for u in range(HALVES):
                 h_bank[e, u] = psum.tile([P, TILES, HALF], F32, name=f"h_bank{e}{u}", tag=f"h{e}{u}")
-            h_wd[e] = shifted(f"h_wd{e}", [P, C], U32, MW // 4)
-            h_sc[e] = shifted(f"h_sc{e}", [P, C], U8, MS)
+            h_wd[e] = shifted(f"h_wd{e}", [P, C], U32, MOVING_WORDS_AT // 4)
+            h_sc[e] = shifted(f"h_sc{e}", [P, C], U8, MOVING_SCALES_AT)
         y_last = sb("y_last", [P, TILES, C], F32)
         out_rows = out.rearrange("(q p) j -> p q j", p=P)
-
-        engine_copy = {"s": nc.scalar.copy, "v": nc.vector.tensor_copy}
 
         def half(u):
             return slice(u * HALF, (u + 1) * HALF)
@@ -207,54 +161,44 @@ def tile_moe_elr_s_gelu_kernel(
         def slots(e, u):
             return slice(e * C + u * HALF, e * C + (u + 1) * HALF)
 
-        def cast_wa(e, s, j0, j1, t0, t1, share):
-            src = wa_raw[e, s, j0][:].rearrange("p j (m t) -> p m j t", t=TILES)[:, :, :, t0:t1]
-            dst = wa_bf[e, s][:].rearrange("p t m j -> p m j t")[:, :, j0:j1, t0:t1]
+        def cast_wa(e, s, t0, t1):
+            share = VECTOR_SHARE[e, s]
+            src = wa_raw[e, s][:].rearrange("p j (m t) -> p m j t", t=TILES)[:, :, :, t0:t1]
+            dst = wa_bf[e, s][:].rearrange("p t m j -> p m j t")[:, :, :, t0:t1]
             if share:
                 nc.vector.tensor_copy(dst[:, :share], src[:, :share])
-            if share < P:
-                nc.scalar.copy(dst[:, share:], src[:, share:])
+            nc.scalar.copy(dst[:, share:], src[:, share:])
 
-        def quantize_wa(e, s, quantizes):
-            for t0, t1 in quantizes:
-                nc.vector.quantize_mx(
-                    out=wa_wd[e, s][:, t0:t1, :].rearrange("p t m -> p (t m)").bitcast(FP8X4),
-                    scales=wa_sc[e, s][:, t0:t1, :].rearrange("p t m -> p (t m)"),
-                    in_=wa_bf[e, s][:, t0:t1, :, :].rearrange("p t m j -> p (t m j)"),
-                )
+        def quantize_wa(e, s, t0, t1):
+            nc.vector.quantize_mx(
+                out=wa_wd[e, s][:, t0:t1, :].rearrange("p t m -> p (t m)").bitcast(FP8X4),
+                scales=wa_sc[e, s][WA_SCALES_FROM:P, t0:t1, :].rearrange("p t m -> p (t m)"),
+                in_=wa_bf[e, s][:, t0:t1, :, :].rearrange("p t m j -> p (t m j)"),
+            )
 
-        def h_pass(e, s, halves=range(HALVES)):
-            for u in halves:
-                for t in range(TILES):
-                    nc.tensor.matmul_mx(
-                        out=h_bank[e, u][:, t, :],
-                        lhsT=wa_wd[e, s][:, t, :].bitcast(FP8X4),
-                        lhsT_scale=wa_sc[e, s][:, t, :],
-                        rhs=slot_wd[s][:, slots(e, u)].bitcast(FP8X4),
-                        rhs_scale=slot_sc[:, s, slots(e, u)],
-                        start=(s == 0 and t == 0),
-                        stop=(s == PASSES - 1 and t == TILES - 1),
-                    )
-
-        def y_out(e, u, q, width):
-            q0 = max(first for first, end in BANKS[e, u if e == LAST else 0] if first <= q)
-            if e == FIRST:
-                return y_bank[FIRST, q0][:, q - q0, u * HALF : u * HALF + width]
-            return y_bank[LAST, u, q0][:, q - q0, :]
-
-        def w_pass(e, s, u, q0, q1):
-            s0 = max(first for first, end in W_LOADS[e] if first <= s)
-            for q in range(q0, q1):
-                opens_bank = q in [first for first, end in BANKS[e, u if e == LAST else 0]] and (e == LAST or u == 0)
+        def h_pass(e, s, u, t0=0, t1=TILES):
+            for t in range(t0, t1):
                 nc.tensor.matmul_mx(
-                    out=y_out(e, u, q, HALF),
-                    lhsT=w_wd[e, s0][:, s - s0, 2 * P * q : 2 * P * (q + 1)].bitcast(FP4X4),
-                    lhsT_scale=w_sc[e][:, s, P * q : P * (q + 1)],
+                    out=h_bank[e, u][:, t, :],
+                    lhsT=wa_wd[e, s][:, t, :].bitcast(FP8X4),
+                    lhsT_scale=wa_sc[e, s][WA_SCALES_FROM:P, t, :],
                     rhs=slot_wd[s][:, slots(e, u)].bitcast(FP8X4),
                     rhs_scale=slot_sc[:, s, slots(e, u)],
-                    start=(s == 0 and opens_bank),
-                    stop=False,
+                    start=(s == 0 and t == 0),
+                    stop=(s == PASSES - 1 and t == TILES - 1),
                 )
+
+        def w_pass(e, s, u, q):
+            s0 = max(first for first, end in W_LOADS[e] if first <= s)
+            nc.tensor.matmul_mx(
+                out=y_bank[FIRST, q][:, half(u)] if e == FIRST else y_bank[LAST, u, q][:],
+                lhsT=w_wd[e, s0][:, s - s0, 2 * P * q : 2 * P * (q + 1)].bitcast(FP4X4),
+                lhsT_scale=w_sc[e][:, s, P * q : P * (q + 1)],
+                rhs=slot_wd[s][:, slots(e, u)].bitcast(FP8X4),
+                rhs_scale=slot_sc[:, s, slots(e, u)],
+                start=(s == 0 and (e == LAST or u == 0)),
+                stop=False,
+            )
 
         def gelu(e, u):
             nc.scalar.activation(h_bf[e][:, half(u), :], h_bank[e, u][:].rearrange("p t n -> p n t"), GELU)
@@ -262,96 +206,93 @@ def tile_moe_elr_s_gelu_kernel(
         def quantize_h(e, u):
             nc.vector.quantize_mx(
                 out=h_wd[e][:, half(u)].bitcast(FP8X4),
-                scales=h_sc[e][:, half(u)],
+                scales=h_sc[e][H_SCALES_FROM:P, half(u)],
                 in_=h_bf[e][:, half(u), :].rearrange("p n t -> p (n t)"),
             )
 
-        def wb_pass(e, u, width, q0=0, q1=TILES):
-            for q in range(q0, q1):
-                nc.tensor.matmul_mx(
-                    out=y_out(e, u, q, width),
-                    lhsT=wb_wd[e][:, P * q : P * (q + 1)].bitcast(FP8X4),
-                    lhsT_scale=wb_sc[SCALE_ROWS:P, e, P * q : P * (q + 1)],
-                    rhs=h_wd[e][:, u * HALF : u * HALF + width].bitcast(FP8X4),
-                    rhs_scale=h_sc[e][:, u * HALF : u * HALF + width],
-                    start=False,
-                    stop=(q + 1 in [end for first, end in BANKS[e, u if e == LAST else 0]]),
-                )
+        def wb_pass(e, bank, columns, q):
+            nc.tensor.matmul_mx(
+                out=bank[:],
+                lhsT=wb_wd[e][:, P * q : P * (q + 1)].bitcast(FP8X4),
+                lhsT_scale=wb_sc[SCALE_ROWS:P, e, P * q : P * (q + 1)],
+                rhs=h_wd[e][:, columns].bitcast(FP8X4),
+                rhs_scale=h_sc[e][H_SCALES_FROM:P, columns],
+                start=False,
+                stop=True,
+            )
+
+        def wb_first(q):
+            wb_pass(FIRST, y_bank[FIRST, q], slice(0, C), q)
+
+        def wb_last(u, q):
+            wb_pass(LAST, y_bank[LAST, u, q], half(u), q)
 
         for e, s in ((FIRST, 0), (FIRST, 1), (LAST, 0)):
-            steps = FINAL_CASTS if (e, s) in TWO_STEP else WHOLE_PASS
-            for n, (t0, t1) in enumerate(steps):
-                cast_wa(e, s, 0, PACK, t0, t1, SHARE3B if (e, s, n) == (LAST, 0, 1) else VECTOR_SHARE[e, s])
-            quantize_wa(e, s, steps)
-            h_pass(e, s)
-        for q0, q1 in BANKS[FIRST, 0]:
-            y_bank[FIRST, q0] = psum.tile([P, q1 - q0, C], F32, name=f"y_bank0{q0}", tag=f"y0{q0}")
-        h_bf[FIRST] = sb("h_bf0", [P, C, PACK], BF16, tag=HBF0_TAG)
+            cast_wa(e, s, 0, TILES)
+            quantize_wa(e, s, 0, TILES)
+            for u in range(HALVES):
+                h_pass(e, s, u)
+        for q in range(TILES):
+            y_bank[FIRST, q] = psum.tile([P, C], F32, name=f"y_bank0{q}", tag=f"y0{q}")
+        h_bf[FIRST] = sb("h_bf0", [P, C, PACK], BF16, tag="wa_raw10")
         for u in range(HALVES):
             gelu(FIRST, u)
         for u in range(HALVES):
-            w_pass(FIRST, 0, u, 0, TILES)
+            for q in range(TILES):
+                w_pass(FIRST, 0, u, q)
+        for u in range(HALVES):
+            quantize_h(FIRST, u)
 
-        if not QH_LATE:
+        for t0, t1 in FINAL_CASTS:
+            cast_wa(LAST, 1, t0, t1)
+        for t0, t1 in FINAL_QUANTIZES:
+            quantize_wa(LAST, 1, t0, t1)
+        for q in range(TILES):
             for u in range(HALVES):
-                quantize_h(FIRST, u)
-        if SPLIT:
-            cast_wa(LAST, 1, 0, 2, 0, TILES, EARLY_SHARE)
-        if QH_LATE:
-            for u in range(HALVES):
-                quantize_h(FIRST, u)
-        for (t0, t1), share in zip(FINAL_CASTS, FINAL_SHARES):
-            cast_wa(LAST, 1, 2 if SPLIT else 0, PACK, t0, t1, share)
-        quantize_wa(LAST, 1, FINAL_QUANTIZES)
-        for q0, q1 in BANKS[FIRST, 0]:
-            for u in range(HALVES):
-                w_pass(FIRST, 1, u, q0, q1)
-        wb_pass(FIRST, 0, C, 0, WB0_FIRST)
-        h_pass(LAST, 1, [0])
-        wb_pass(FIRST, 0, C, WB0_FIRST, WB0_SECOND)
-        h_pass(LAST, 1, [1])
-        wb_pass(FIRST, 0, C, WB0_SECOND, TILES)
+                w_pass(FIRST, 1, u, q)
+        wb_first(0)
+        wb_first(1)
+        h_pass(LAST, 1, 0)
+        wb_first(2)
+        h_pass(LAST, 1, 1)
+        wb_first(3)
 
-        y_first = {c: sb(f"y_first_{c}", [P, TILES, C], F32, tag=COPY0_TAGS[c]) for c in set(COPY0)}
+        y_first_v = sb("y_first_v", [P, TILES, C], F32, tag="wa_bf11")
+        y_first_s = sb("y_first_s", [P, TILES, C], F32)
+        for q in range(TILES):
+            staged = y_first_s if q < 2 else y_first_v
+            copy = nc.scalar.copy if q < 2 else nc.vector.tensor_copy
+            copy(staged[:, q, :], y_bank[FIRST, q][:])
+            nc.sync.dma_start(out_rows[:, q, 0:C], staged[:, q, :])
 
-        def store_first(banks):
-            for (q0, q1), c in banks:
-                engine_copy[c](y_first[c][:, q0:q1, :], y_bank[FIRST, q0][:])
-                nc.sync.dma_start(out_rows[:, q0:q1, 0:C], y_first[c][:, q0:q1, :])
-
-        first_banks = list(zip(BANKS[FIRST, 0], COPY0))
-        store_first(first_banks[: len(first_banks) - LATE0])
-
-        h_bf[LAST] = shifted("h_bf1", [P, C, PACK], BF16, 32)
-        gelu(LAST, 0)
-        quantize_h(LAST, 0)
-        gelu(LAST, 1)
-        store_first(first_banks[len(first_banks) - LATE0 :])
-        quantize_h(LAST, 1)
+        h_bf[LAST] = shifted("h_bf1", [P, C, PACK], BF16, LAST_H_BF_AT // 2)
+        for u in range(HALVES):
+            gelu(LAST, u)
+            quantize_h(LAST, u)
         for u in range(HALVES):
             for q, tag in zip(ORDER[u], LAST_BANK_TAGS[u]):
-                y_bank[LAST, u, q] = psum.tile([P, 1, HALF], F32, name=f"y_bank1{u}{q}", tag=tag)
+                y_bank[LAST, u, q] = psum.tile([P, HALF], F32, name=f"y_bank1{u}{q}", tag=tag)
+        for s in range(PASSES):
+            for q in ORDER[0]:
+                w_pass(LAST, s, 0, q)
+        for s in range(PASSES):
+            for q in ORDER[1][:2]:
+                w_pass(LAST, s, 1, q)
         for q in ORDER[0]:
-            for s in range(PASSES):
-                w_pass(LAST, s, 0, q, q + 1)
-        for q in ORDER[1][:CUT1]:
-            for s in range(PASSES):
-                w_pass(LAST, s, 1, q, q + 1)
-        for q in ORDER[0]:
-            wb_pass(LAST, 0, HALF, q, q + 1)
-        for q in ORDER[1][CUT1:CUT2]:
-            for s in range(PASSES):
-                w_pass(LAST, s, 1, q, q + 1)
-        for n, q in enumerate(ORDER[1]):
-            if n >= CUT2:
-                for s in range(PASSES):
-                    w_pass(LAST, s, 1, q, q + 1)
-            wb_pass(LAST, 1, HALF, q, q + 1)
+            wb_last(0, q)
+        for q in ORDER[1][2:]:
+            w_pass(LAST, 0, 1, q)
+        for early, late in zip(ORDER[1][:2], ORDER[1][2:]):
+            wb_last(1, early)
+            w_pass(LAST, 1, 1, late)
+        for q in ORDER[1][2:]:
+            wb_last(1, q)
 
         for u in range(HALVES):
-            for q, c in zip(ORDER[u], COPY1[u]):
-                engine_copy[c](y_last[:, q, half(u)], y_bank[LAST, u, q][:, 0, :])
-                if q < TILES - HELD:
+            for n, q in enumerate(ORDER[u]):
+                copy = nc.vector.tensor_copy if n % 2 == 0 else nc.scalar.copy
+                copy(y_last[:, q, half(u)], y_bank[LAST, u, q][:])
+                if q != HELD_TILE:
                     nc.sync.dma_start(out_rows[:, q, slots(LAST, u)], y_last[:, q, half(u)])
                 elif u == HALVES - 1:
                     nc.sync.dma_start(out_rows[:, q, LAST * C : (LAST + 1) * C], y_last[:, q, :])

@@ -36,9 +36,11 @@ LAST_H_BF_AT = 64
 WA_SCALES_FROM = 4
 H_SCALES_FROM = 12
 
-VECTOR_SHARE = {(FIRST, 0): 0, (FIRST, 1): 76, (LAST, 0): 80, (LAST, 1): 80}
+VECTOR_SHARE = {(FIRST, 0): 0, (FIRST, 1): 76, (LAST, 0): 96, (LAST, 1): 80}
 
-WHOLE_PASS = ((0, TILES),)
+H_HALF_WORDS = HALF * PACK // 2
+THIRD_MARGIN = H_HALF_WORDS - 64
+
 FINAL_CASTS = ((0, 2), (2, TILES))
 FINAL_QUANTIZES = ((0, 2), (2, 3), (3, TILES))
 
@@ -79,7 +81,9 @@ def tile_moe_elr_s_gelu_kernel(
         x_wd = [sb(f"x_wd{s}", [P, T], I32) for s in range(PASSES)]
         w_wd = {(e, s0): shifted(f"w_wd{e}{s0}", [P, s1 - s0, 2 * N], U8, 0) for e in range(E) for s0, s1 in W_LOADS[e]}
         wb_wd = [sb(f"wb_wd{e}", [P, N], I32) for e in range(E)]
-        wa_raw = {(e, s): sb(f"wa_raw{e}{s}", [P, PACK, H], F32) for e in range(E) for s in range(PASSES)}
+        wa_raw = {(e, s): sb(f"wa_raw{e}{s}", [P, PACK, H], F32) for e, s in ((FIRST, 0), (FIRST, 1), (LAST, 1))}
+        third = sb("third", [P, THIRD_MARGIN + PACK * H + THIRD_MARGIN], F32)
+        wa_raw[LAST, 0] = third[:, THIRD_MARGIN : THIRD_MARGIN + PACK * H].rearrange("p (j i) -> p j i", j=PACK)
 
         def load_x(s):
             nc.sync.dma_start(x_wd[s][:], x_words[s].rearrange("p t d -> p (t d)").bitcast(I32))
@@ -161,13 +165,16 @@ def tile_moe_elr_s_gelu_kernel(
         def slots(e, u):
             return slice(e * C + u * HALF, e * C + (u + 1) * HALF)
 
+        def cast(copy, e, s, groups, t0, t1):
+            src = wa_raw[e, s][:].rearrange("p j (m t) -> p m j t", t=TILES)[:, groups, :, t0:t1]
+            dst = wa_bf[e, s][:].rearrange("p t m j -> p m j t")[:, groups, :, t0:t1]
+            copy(dst, src)
+
         def cast_wa(e, s, t0, t1):
             share = VECTOR_SHARE[e, s]
-            src = wa_raw[e, s][:].rearrange("p j (m t) -> p m j t", t=TILES)[:, :, :, t0:t1]
-            dst = wa_bf[e, s][:].rearrange("p t m j -> p m j t")[:, :, :, t0:t1]
             if share:
-                nc.vector.tensor_copy(dst[:, :share], src[:, :share])
-            nc.scalar.copy(dst[:, share:], src[:, share:])
+                cast(nc.vector.tensor_copy, e, s, slice(0, share), t0, t1)
+            cast(nc.scalar.copy, e, s, slice(share, P), t0, t1)
 
         def quantize_wa(e, s, t0, t1):
             nc.vector.quantize_mx(
@@ -201,13 +208,13 @@ def tile_moe_elr_s_gelu_kernel(
             )
 
         def gelu(e, u):
-            nc.scalar.activation(h_bf[e][:, half(u), :], h_bank[e, u][:].rearrange("p t n -> p n t"), GELU)
+            nc.scalar.activation(h_bf[e, u], h_bank[e, u][:].rearrange("p t n -> p n t"), GELU)
 
         def quantize_h(e, u):
             nc.vector.quantize_mx(
                 out=h_wd[e][:, half(u)].bitcast(FP8X4),
                 scales=h_sc[e][H_SCALES_FROM:P, half(u)],
-                in_=h_bf[e][:, half(u), :].rearrange("p n t -> p (n t)"),
+                in_=h_bf[e, u].rearrange("p n t -> p (n t)"),
             )
 
         def wb_pass(e, bank, columns, q):
@@ -228,14 +235,25 @@ def tile_moe_elr_s_gelu_kernel(
             wb_pass(LAST, y_bank[LAST, u, q], half(u), q)
 
         for e, s in ((FIRST, 0), (FIRST, 1), (LAST, 0)):
-            cast_wa(e, s, 0, TILES)
-            quantize_wa(e, s, 0, TILES)
+            steps = FINAL_CASTS if e == LAST else ((0, TILES),)
+            if (e, s) == (LAST, 0):
+                below = (P - VECTOR_SHARE[e, s]) // 2
+                for groups in (slice(0, below), slice(P - below, P)):
+                    cast(nc.scalar.copy, e, s, groups, 0, TILES)
+                for t0, t1 in steps:
+                    cast(nc.vector.tensor_copy, e, s, slice(below, P - below), t0, t1)
+            else:
+                for t0, t1 in steps:
+                    cast_wa(e, s, t0, t1)
+            for t0, t1 in steps:
+                quantize_wa(e, s, t0, t1)
             for u in range(HALVES):
                 h_pass(e, s, u)
         for q in range(TILES):
             y_bank[FIRST, q] = psum.tile([P, C], F32, name=f"y_bank0{q}", tag=f"y0{q}")
-        h_bf[FIRST] = sb("h_bf0", [P, C, PACK], BF16, tag="wa_raw10")
-        for u in range(HALVES):
+        for u, first in enumerate((0, PACK * H + 2 * THIRD_MARGIN - H_HALF_WORDS)):
+            words = third[:, first : first + H_HALF_WORDS]
+            h_bf[FIRST, u] = words.bitcast(BF16).rearrange("p (n t) -> p n t", t=PACK)
             gelu(FIRST, u)
         for u in range(HALVES):
             for q in range(TILES):
@@ -265,8 +283,9 @@ def tile_moe_elr_s_gelu_kernel(
             copy(staged[:, q, :], y_bank[FIRST, q][:])
             nc.sync.dma_start(out_rows[:, q, 0:C], staged[:, q, :])
 
-        h_bf[LAST] = shifted("h_bf1", [P, C, PACK], BF16, LAST_H_BF_AT // 2)
+        h_bf_last = shifted("h_bf1", [P, C, PACK], BF16, LAST_H_BF_AT // 2)
         for u in range(HALVES):
+            h_bf[LAST, u] = h_bf_last[:, half(u), :]
             gelu(LAST, u)
             quantize_h(LAST, u)
         for u in range(HALVES):

import math
from contextlib import ExitStack

import concourse.mybir as mybir

K, T, E, C, H, N = 1024, 1024, 2, 256, 512, 512
FLOPS = 2 * E * C * (K * N + K * H + H * N)

F32 = mybir.dt.float32
BF16 = mybir.dt.bfloat16
I32 = mybir.dt.int32
U32 = mybir.dt.uint32
U16 = mybir.dt.uint16
U8 = mybir.dt.uint8
FP8X4 = mybir.dt.float8_e4m3fn_x4
FP4X4 = mybir.dt.float4_e2m1fn_x4
GELU = mybir.ActivationFunctionType.Gelu_apprx_tanh

P = 128
PACK = 4
K_PASS = P * PACK
PASSES = K // K_PASS
QUADRANT = 32
SCALE_ROWS = 4
SPREAD = 8
LIST_GROUP = 16
TILES = N // P
HALF = 128
HALVES = C // HALF
FIRST, LAST = 0, 1

MOVING_WORDS_AT = 192
MOVING_SCALES_AT = 64
WA_BF_AT = 128
LAST_H_BF_AT = 64
WA_SCALES_FROM = 4
H_SCALES_FROM = 12

VECTOR_SHARE = {(FIRST, 0): 0, (FIRST, 1): 76, (LAST, 0): 96, (LAST, 1): 80}

H_HALF_WORDS = HALF * PACK // 2
THIRD_MARGIN = H_HALF_WORDS - 64

FINAL_CASTS = ((0, 2), (2, TILES))
FINAL_QUANTIZES = ((0, 2), (2, 3), (3, TILES))

ORDER = ((0, 1, 2, 3), (3, 2, 1, 0))
HELD_TILE = TILES - 1
LAST_BANK_TAGS = (("h00", "h01", "y00", "y01"), ("y02", "h10", "h11", "y03"))
W_LOADS = {FIRST: ((0, 1), (1, PASSES)), LAST: ((0, PASSES),)}


def tile_moe_elr_s_gelu_kernel(
    tc, x_words, x_scales, w_words, w_scales, wa, wb_words, wb_scales, offs, out
):
    nc = tc.nc
    with ExitStack() as ctx:
        keep = ctx.enter_context(tc.tile_pool(name="keep", bufs=1))
        psum = ctx.enter_context(tc.psum_pool(name="psum", bufs=1))

        def sb(name, shape, dtype, tag=None):
            return keep.tile(shape, dtype, name=name, tag=tag or name, align_bytes=256)

        def shifted(name, shape, dtype, skip, tag=None):
            flat = sb(name, [P, skip + math.prod(shape[1:])], dtype, tag)[:, skip:]
            return flat if len(shape) == 2 else flat.rearrange("p (a b) -> p a b", a=shape[1])

        offsets = keep.tile([P, E * C // LIST_GROUP], U16, name="offsets")

        warm = sb("warm", [P, 8], F32)
        warm_out = sb("warm_out", [P, 8], F32)
        nc.vector.memset(warm[:], 0.0)
        nc.scalar.activation(warm_out[:], warm[:], GELU)

        x_sc = sb("x_sc", [P, PASSES, T], U8)
        w_sc = [shifted(f"w_sc{e}", [P, PASSES, N], U8, 0) for e in range(E)]
        wb_sc = shifted("wb_sc", [P, E, N], U8, 0)
        for scale_tile in (x_sc, w_sc[FIRST], wb_sc, w_sc[LAST]):
            nc.vector.memset(scale_tile[:].bitcast(I32), 0)

        x_wd = [sb(f"x_wd{s}", [P, T], I32) for s in range(PASSES)]
        w_wd = {(e, s0): shifted(f"w_wd{e}{s0}", [P, s1 - s0, 2 * N], U8, 0) for e in range(E) for s0, s1 in W_LOADS[e]}
        wb_wd = [sb(f"wb_wd{e}", [P, N], I32) for e in range(E)]
        wa_raw = {(e, s): sb(f"wa_raw{e}{s}", [P, PACK, H], F32) for e, s in ((FIRST, 0), (FIRST, 1), (LAST, 1))}
        third = sb("third", [P, THIRD_MARGIN + PACK * H + THIRD_MARGIN], F32)
        wa_raw[LAST, 0] = third[:, THIRD_MARGIN : THIRD_MARGIN + PACK * H].rearrange("p (j i) -> p j i", j=PACK)

        def load_x(s):
            nc.sync.dma_start(x_wd[s][:], x_words[s].rearrange("p t d -> p (t d)").bitcast(I32))

        def load_wa(e, s):
            rows = wa[e, K_PASS * s : K_PASS * (s + 1), :].rearrange("(p j) i -> p j i", j=PACK)
            nc.sync.dma_start(wa_raw[e, s][:], rows)

        def load_w(e, s0, s1):
            rows = w_words[e, s0:s1].rearrange("s p b -> p s b")
            nc.sync.dma_start(w_wd[e, s0][:].bitcast(I32), rows.bitcast(I32))

        def load_wb(e):
            nc.sync.dma_start(wb_wd[e][:], wb_words[e, 0].rearrange("p n d -> p (n d)").bitcast(I32))

        def load_scales(scale_tile, first, rows):
            for r in range(SCALE_ROWS):
                nc.sync.dma_start(scale_tile[first + r : P : QUADRANT].bitcast(I32), rows[r].bitcast(I32))

        def load_wb_scales():
            load_scales(wb_sc, SCALE_ROWS, wb_scales.rearrange("e s (q r) n -> r q (e s) n", r=SCALE_ROWS))

        def load_w_scales(e):
            load_scales(w_sc[e], 0, w_scales[e : e + 1].rearrange("e s (q r) n -> r q (e s) n", r=SCALE_ROWS))

        load_x(0)
        nc.sync.dma_start(x_sc[0:P:SPREAD].bitcast(I32), x_scales.rearrange("s b t -> b s t").bitcast(I32))
        nc.sync.dma_start(offsets[:], offs)
        load_wa(FIRST, 0)
        load_x(1)
        load_w_scales(FIRST)
        load_wa(FIRST, 1)

        slot_wd = [
            shifted(f"slot_wd{s}", [P, E * C], U32, MOVING_WORDS_AT // 4, tag) for s, tag in enumerate(("x_sc", None))
        ]
        spread_sc = sb("spread_sc", [P, PASSES, E * C], U8)
        slot_sc = shifted("slot_sc", [P, PASSES, E * C], U8, MOVING_SCALES_AT)
        for s in range(PASSES):
            nc.vector.tensor_copy(spread_sc[:, s, :], x_sc[:, s, :].indirect(offsets[:]))
        spread_rows = spread_sc[:].rearrange("p s c -> p (s c)").bitcast(I32)
        slot_rows = slot_sc[:].rearrange("p s c -> p (s c)").bitcast(I32)
        nc.vector.tensor_copy(slot_rows, spread_rows)
        for r in range(1, SCALE_ROWS):
            nc.sync.dma_start(slot_rows[r:P:QUADRANT], spread_rows[SPREAD * r : P : QUADRANT])
        for s in range(PASSES):
            nc.vector.tensor_copy(slot_wd[s][:], x_wd[s][:].bitcast(U32).indirect(offsets[:]))

        load_wa(LAST, 0)
        load_w(FIRST, 0, 1)
        load_wb_scales()
        load_wa(LAST, 1)
        load_w(FIRST, 1, PASSES)
        load_wb(FIRST)
        load_w_scales(LAST)
        load_w(LAST, 0, PASSES)
        load_wb(LAST)

        wa_bf, wa_wd, wa_sc = {}, {}, {}
        for e in range(E):
            for s in range(PASSES):
                wa_bf[e, s] = shifted(f"wa_bf{e}{s}", [P, TILES, P * PACK], BF16, WA_BF_AT // 2).rearrange(
                    "p t (m j) -> p t m j", j=PACK
                )
                wa_wd[e, s] = sb(f"wa_wd{e}{s}", [P, TILES, P], U32)
                wa_sc[e, s] = sb(f"wa_sc{e}{s}", [P, TILES, P], U8)
        h_bank, y_bank, h_bf, h_wd, h_sc = {}, {}, {}, {}, {}
        for e in range(E):
            for u in range(HALVES):
                h_bank[e, u] = psum.tile([P, TILES, HALF], F32, name=f"h_bank{e}{u}", tag=f"h{e}{u}")
            h_wd[e] = shifted(f"h_wd{e}", [P, C], U32, MOVING_WORDS_AT // 4)
            h_sc[e] = shifted(f"h_sc{e}", [P, C], U8, MOVING_SCALES_AT)
        y_last = sb("y_last", [P, TILES, C], F32)
        out_rows = out.rearrange("(q p) j -> p q j", p=P)

        def half(u):
            return slice(u * HALF, (u + 1) * HALF)

        def slots(e, u):
            return slice(e * C + u * HALF, e * C + (u + 1) * HALF)

        def cast(copy, e, s, groups, t0, t1):
            src = wa_raw[e, s][:].rearrange("p j (m t) -> p m j t", t=TILES)[:, groups, :, t0:t1]
            dst = wa_bf[e, s][:].rearrange("p t m j -> p m j t")[:, groups, :, t0:t1]
            copy(dst, src)

        def cast_wa(e, s, t0, t1):
            share = VECTOR_SHARE[e, s]
            if share:
                cast(nc.vector.tensor_copy, e, s, slice(0, share), t0, t1)
            cast(nc.scalar.copy, e, s, slice(share, P), t0, t1)

        def quantize_wa(e, s, t0, t1):
            nc.vector.quantize_mx(
                out=wa_wd[e, s][:, t0:t1, :].rearrange("p t m -> p (t m)").bitcast(FP8X4),
                scales=wa_sc[e, s][WA_SCALES_FROM:P, t0:t1, :].rearrange("p t m -> p (t m)"),
                in_=wa_bf[e, s][:, t0:t1, :, :].rearrange("p t m j -> p (t m j)"),
            )

        def h_pass(e, s, u, t0=0, t1=TILES):
            for t in range(t0, t1):
                nc.tensor.matmul_mx(
                    out=h_bank[e, u][:, t, :],
                    lhsT=wa_wd[e, s][:, t, :].bitcast(FP8X4),
                    lhsT_scale=wa_sc[e, s][WA_SCALES_FROM:P, t, :],
                    rhs=slot_wd[s][:, slots(e, u)].bitcast(FP8X4),
                    rhs_scale=slot_sc[:, s, slots(e, u)],
                    start=(s == 0 and t == 0),
                    stop=(s == PASSES - 1 and t == TILES - 1),
                )

        def w_pass(e, s, u, q):
            s0 = max(first for first, end in W_LOADS[e] if first <= s)
            nc.tensor.matmul_mx(
                out=y_bank[FIRST, q][:, half(u)] if e == FIRST else y_bank[LAST, u, q][:],
                lhsT=w_wd[e, s0][:, s - s0, 2 * P * q : 2 * P * (q + 1)].bitcast(FP4X4),
                lhsT_scale=w_sc[e][:, s, P * q : P * (q + 1)],
                rhs=slot_wd[s][:, slots(e, u)].bitcast(FP8X4),
                rhs_scale=slot_sc[:, s, slots(e, u)],
                start=(s == 0 and (e == LAST or u == 0)),
                stop=False,
            )

        def gelu(e, u):
            nc.scalar.activation(h_bf[e, u], h_bank[e, u][:].rearrange("p t n -> p n t"), GELU)

        def quantize_h(e, u):
            nc.vector.quantize_mx(
                out=h_wd[e][:, half(u)].bitcast(FP8X4),
                scales=h_sc[e][H_SCALES_FROM:P, half(u)],
                in_=h_bf[e, u].rearrange("p n t -> p (n t)"),
            )

        def wb_pass(e, bank, columns, q):
            nc.tensor.matmul_mx(
                out=bank[:],
                lhsT=wb_wd[e][:, P * q : P * (q + 1)].bitcast(FP8X4),
                lhsT_scale=wb_sc[SCALE_ROWS:P, e, P * q : P * (q + 1)],
                rhs=h_wd[e][:, columns].bitcast(FP8X4),
                rhs_scale=h_sc[e][H_SCALES_FROM:P, columns],
                start=False,
                stop=True,
            )

        def wb_first(q):
            wb_pass(FIRST, y_bank[FIRST, q], slice(0, C), q)

        def wb_last(u, q):
            wb_pass(LAST, y_bank[LAST, u, q], half(u), q)

        for e, s in ((FIRST, 0), (FIRST, 1), (LAST, 0)):
            steps = FINAL_CASTS if e == LAST else ((0, TILES),)
            if (e, s) == (LAST, 0):
                below = (P - VECTOR_SHARE[e, s]) // 2
                for groups in (slice(0, below), slice(P - below, P)):
                    cast(nc.scalar.copy, e, s, groups, 0, TILES)
                for t0, t1 in steps:
                    cast(nc.vector.tensor_copy, e, s, slice(below, P - below), t0, t1)
            else:
                for t0, t1 in steps:
                    cast_wa(e, s, t0, t1)
            for t0, t1 in steps:
                quantize_wa(e, s, t0, t1)
            for u in range(HALVES):
                h_pass(e, s, u)
        for q in range(TILES):
            y_bank[FIRST, q] = psum.tile([P, C], F32, name=f"y_bank0{q}", tag=f"y0{q}")
        for u, first in enumerate((0, PACK * H + 2 * THIRD_MARGIN - H_HALF_WORDS)):
            words = third[:, first : first + H_HALF_WORDS]
            h_bf[FIRST, u] = words.bitcast(BF16).rearrange("p (n t) -> p n t", t=PACK)
            gelu(FIRST, u)
        for u in range(HALVES):
            for q in range(TILES):
                w_pass(FIRST, 0, u, q)
        for u in range(HALVES):
            quantize_h(FIRST, u)

        for t0, t1 in FINAL_CASTS:
            cast_wa(LAST, 1, t0, t1)
        for t0, t1 in FINAL_QUANTIZES:
            quantize_wa(LAST, 1, t0, t1)
        for q in range(TILES):
            for u in range(HALVES):
                w_pass(FIRST, 1, u, q)
        wb_first(0)
        wb_first(1)
        h_pass(LAST, 1, 0)
        wb_first(2)
        h_pass(LAST, 1, 1)
        wb_first(3)

        y_first_v = sb("y_first_v", [P, TILES, C], F32, tag="wa_bf11")
        y_first_s = sb("y_first_s", [P, TILES, C], F32)
        for q in range(TILES):
            staged = y_first_s if q < 2 else y_first_v
            copy = nc.scalar.copy if q < 2 else nc.vector.tensor_copy
            copy(staged[:, q, :], y_bank[FIRST, q][:])
            nc.sync.dma_start(out_rows[:, q, 0:C], staged[:, q, :])

        h_bf_last = shifted("h_bf1", [P, C, PACK], BF16, LAST_H_BF_AT // 2)
        for u in range(HALVES):
            h_bf[LAST, u] = h_bf_last[:, half(u), :]
            gelu(LAST, u)
            quantize_h(LAST, u)
        for u in range(HALVES):
            for q, tag in zip(ORDER[u], LAST_BANK_TAGS[u]):
                y_bank[LAST, u, q] = psum.tile([P, HALF], F32, name=f"y_bank1{u}{q}", tag=tag)
        for s in range(PASSES):
            for q in ORDER[0]:
                w_pass(LAST, s, 0, q)
        for s in range(PASSES):
            for q in ORDER[1][:2]:
                w_pass(LAST, s, 1, q)
        for q in ORDER[0]:
            wb_last(0, q)
        for q in ORDER[1][2:]:
            w_pass(LAST, 0, 1, q)
        for early, late in zip(ORDER[1][:2], ORDER[1][2:]):
            wb_last(1, early)
            w_pass(LAST, 1, 1, late)
        for q in ORDER[1][2:]:
            wb_last(1, q)

        for u in range(HALVES):
            for n, q in enumerate(ORDER[u]):
                copy = nc.vector.tensor_copy if n % 2 == 0 else nc.scalar.copy
                copy(y_last[:, q, half(u)], y_bank[LAST, u, q][:])
                if q != HELD_TILE:
                    nc.sync.dma_start(out_rows[:, q, slots(LAST, u)], y_last[:, q, half(u)])
                elif u == HALVES - 1:
                    nc.sync.dma_start(out_rows[:, q, LAST * C : (LAST + 1) * C], y_last[:, q, :])
